import numpy as np
import ml_dtypes


def mxq(x, axis, fmt="e4m3"):
    dtype, down = {"e4m3": (ml_dtypes.float8_e4m3fn, 7), "e5m2": (ml_dtypes.float8_e5m2, 14)}[fmt]
    v = np.moveaxis(np.asarray(x, np.float32).astype(ml_dtypes.bfloat16).astype(np.float64), axis, -1)
    blocks = v.reshape(v.shape[:-1] + (-1, 32))
    amax = np.abs(blocks).max(-1, keepdims=True)
    byte = np.maximum(np.where(amax > 0, np.frexp(amax)[1] - 1 + 127, 0) - down, 1)
    scale = np.exp2(byte - 127.0)
    codes = (blocks / scale).astype(np.float32).astype(dtype).astype(np.float64)
    return np.moveaxis((codes * scale).reshape(v.shape), -1, axis)


WIDE = False


def mx_kscale(k):
    if not WIDE:
        return np.ones(k)
    levels = np.array([10, -10, 5, -5, 0])
    if k % 512:
        return np.exp2(np.random.permutation(np.resize(levels, k // 32))).repeat(32)
    a = np.empty((k // 512, 16))
    for p in range(k // 512):
        a[p, :8] = np.random.permutation(np.resize(levels, 8))
        for g in range(8):
            far = levels[np.abs(levels - a[p, g]) >= 10]
            a[p, g + 8] = far[np.random.randint(len(far))]
    return np.exp2(a.ravel()).repeat(32)


def f64(x):
    return np.asarray(x).astype(np.float64)


def striped(idx):
    return np.tile(idx.reshape(-1, 16).T, (8, 1)).astype(np.uint16)


def unstriped(offs):
    return offs[:16].T.reshape(-1).astype(np.int64)


def pack_weight(w):
    k, n = w.shape
    w = f64(np.asarray(w, np.float32).astype(ml_dtypes.bfloat16)).reshape(k // 32, 32, n)
    amax = np.abs(w).max(1)
    byte = np.clip(np.where(amax > 0, np.frexp(amax)[1] - 1 + 127 - 7, 1), 1, 254)
    scaled = (w * np.exp2(127.0 - byte)[:, None, :]).reshape(k, n).astype(np.float32)
    words = np.ascontiguousarray(scaled.reshape(k // 512, 128, 4, n).transpose(0, 1, 3, 2)).astype(ml_dtypes.float8_e4m3fn).view(np.uint8)
    return words, np.ascontiguousarray(byte.astype(np.uint8).reshape(k // 512, 16, n))


def unpack_weight(words, scales):
    g, p, n, _ = words.shape
    vals = np.ascontiguousarray(words).view(ml_dtypes.float8_e4m3fn).astype(np.float64) * np.repeat(np.exp2(scales.astype(np.float64) - 127.0), 8, axis=1)[..., None]
    return vals.transpose(0, 1, 3, 2).reshape(g * 512, n)


K, T, S, D, H, N = 512, 2048, 512, 8, 512, 128


def setup_inputs():
    n = np.random.standard_normal
    s = mx_kscale(K)[:, None]
    u = mx_kscale(H)
    packed_xT = pack_weight(n((K, T)) * s)
    packed_eT = pack_weight(n((K, T)) * s)
    return {
        "x_words": packed_xT[0],
        "x_scales": packed_xT[1],
        "e_words": packed_eT[0],
        "e_scales": packed_eT[1],
        "w1": (n((K, H)) / np.sqrt(K) / s).astype(np.float32),
        "unit": (np.random.uniform(0.7, 1.3, (H, 1)) * u[:, None]).astype(np.float32),
        "w2": (n((H, N)) / np.sqrt(H) / u[:, None]).astype(np.float32),
        "offs": striped(np.random.permutation(T)[:S]),
    }


def reference(x_words, x_scales, e_words, e_scales, w1, unit, w2, offs):
    e_offs = unpack_weight(e_words, e_scales)[:, unstriped(offs)]
    w1q = mxq(f64(w1), 0, "e4m3")
    h = w1q.T @ e_offs
    mb = h.reshape(len(h), -1, D).mean(axis=2)
    g0 = ((mb) ** 2) / ((mb) ** 2 + 0.2)
    xq = unpack_weight(x_words, x_scales)[:, unstriped(offs)]
    y = w1q.T @ xq
    mc = y.reshape(len(y), -1, D).mean(axis=2)
    gm = g0 * mc
    d2 = (h - np.repeat(mb, D, axis=1)) ** 2
    vb = d2.reshape(len(d2), -1, D).mean(axis=2)
    g1 = vb / (vb + 0.3)
    z = f64(unit) * (np.repeat(gm, D, axis=1) + np.repeat(g1, D, axis=1) * (y - np.repeat(mc, D, axis=1)))
    return mxq(f64(w2), 0, "e4m3").T @ mxq(z, 0, "e4m3")

@@ -1,0 +1,273 @@
+from contextlib import ExitStack
+
+import concourse.mybir as mybir
+from concourse.masks import make_identity
+
+K, T, S, D, H, N = 512, 2048, 512, 8, 512, 128
+FLOPS = 2 * K * H * S * 2 + 2 * H * N * S
+
+F32 = mybir.dt.float32
+BF16 = mybir.dt.bfloat16
+I32 = mybir.dt.int32
+U32 = mybir.dt.uint32
+U16 = mybir.dt.uint16
+U8 = mybir.dt.uint8
+FP8X4 = mybir.dt.float8_e4m3fn_x4
+ALU = mybir.AluOpType
+ACT = mybir.ActivationFunctionType
+AX = mybir.AxisListType
+
+P = 128
+YSUM = ("dve", "pe")
+
+
+def tile_picked_ywien_wien_p_kernel(tc, x_words, x_scales, e_words, e_scales, w1, unit, w2, offs, out):
+    nc = tc.nc
+    with ExitStack() as ctx:
+        sb = ctx.enter_context(tc.tile_pool(name="sb", bufs=1))
+        ps = ctx.enter_context(tc.psum_pool(name="ps", bufs=1))
+
+        def tile(name, shape, dt):
+            return sb.tile(shape, dt, name=name, align_bytes=64)
+
+        offsets = sb.tile([P, S // 16], U16, name="offsets")
+        hb = [ps.tile([P, 512], F32, name="hb%d" % b) for b in range(4)]
+        yb = [ps.tile([P, 512], F32, name="yb%d" % b) for b in range(4)]
+
+        es_win = tile("es_win", [P, T], U8)
+        xs_win = tile("xs_win", [P, T], U8)
+        ew_win = tile("ew_win", [P, T], I32)
+        xw_win = tile("xw_win", [P, T], I32)
+        w1_raw = [tile("w1_raw%d" % a, [P, 4, 256], F32) for a in range(2)]
+        w2_raw = tile("w2_raw", [P, 4, N], F32)
+        unit_sb = tile("unit_sb", [P, 4], F32)
+        ident = tile("ident", [P, P], F32)
+        warm = tile("warm", [P, 1], F32)
+
+        nc.gpsimd.memset(es_win[:].bitcast(I32), 0)
+        nc.vector.memset(xs_win[:].bitcast(I32), 0)
+        nc.vector.memset(warm[:], 1.0)
+        nc.scalar.activation(warm[:], warm[:], ACT.Abs_reciprocal_sqrt)
+        make_identity(nc, ident[:])
+
+        def load_scales(win, src):
+            for q in range(4):
+                nc.sync.dma_start(win[32 * q : 32 * q + 4, :].bitcast(I32), src[0, 4 * q : 4 * q + 4, :].bitcast(I32))
+
+        def load_words(win, src):
+            nc.sync.dma_start(win[:], src[0].rearrange("p n t -> p (n t)").bitcast(I32))
+
+        w1_rows = w1.rearrange("(p j) c -> p j c", j=4)
+        nc.sync.dma_start(offsets[:], offs)
+        load_scales(es_win, e_scales)
+        nc.sync.dma_start(w1_raw[0][:], w1_rows[:, :, 0:256])
+        nc.sync.dma_start(w1_raw[1][:], w1_rows[:, :, 256:512])
+        load_scales(xs_win, x_scales)
+        load_words(ew_win, e_words)
+        nc.sync.dma_start(w2_raw[:], w2.rearrange("(p j) m -> p j m", j=4))
+        load_words(xw_win, x_words)
+        nc.sync.dma_start(unit_sb[:], unit.rearrange("(p t) o -> p (t o)", t=4))
+
+        w1_bf = [tile("w1_bf%d" % a, [P, 4, 64, 4], BF16) for a in range(2)]
+        w1_codes = tile("w1_codes", [P, 4, P], U32)
+        w1_sc = tile("w1_sc", [P, 4, P], U8)
+        es = tile("es", [P, S], U8)
+        xs = tile("xs", [P, S], U8)
+        ew = [tile("ew%d" % a, [P, 256], U32) for a in range(2)]
+        xw = [tile("xw%d" % a, [P, 256], U32) for a in range(2)]
+
+        def cast_w1(eng, a, m0, m1):
+            src = w1_raw[a][:].rearrange("p j (m t) -> p m t j", t=4)[:, m0:m1]
+            dst = w1_bf[a][:].rearrange("p t m j -> p m t j")[:, m0:m1]
+            if eng == "act":
+                nc.scalar.copy(dst, src)
+            else:
+                nc.vector.tensor_copy(dst, src)
+
+        def quant_w1(a):
+            for t in range(4):
+                nc.vector.quantize_mx(
+                    out=w1_codes[:, t, 64 * a : 64 * a + 64].bitcast(FP8X4),
+                    scales=w1_sc[:, t, 64 * a : 64 * a + 64],
+                    in_=w1_bf[a][:, t].rearrange("p m j -> p (m j)"),
+                )
+
+        def gather_words(dst, win, a):
+            nc.vector.tensor_copy(dst[a][:], win[:].bitcast(U32).indirect(offsets[:, 16 * a : 16 * a + 16]))
+
+        nc.vector.tensor_copy(es[:], es_win[:].indirect(offsets[:]))
+        cast_w1("act", 0, 0, 64)
+        cast_w1("act", 1, 0, 32)
+        cast_w1("dve", 1, 32, 64)
+        quant_w1(0)
+        quant_w1(1)
+        nc.vector.tensor_copy(xs[:], xs_win[:].indirect(offsets[:]))
+        gather_words(ew, ew_win, 0)
+        gather_words(ew, ew_win, 1)
+
+        s_h = tile("s_h", [P, 2, P], F32)
+        dev = [tile("dev%d" % a, [P, 8, P], F32) for a in range(2)]
+        sq = [tile("sq%d" % a, [P, 8, P], F32) for a in range(2)]
+
+        def mm_h(a):
+            for t in range(4):
+                nc.tensor.matmul_mx(
+                    out=hb[2 * a + t // 2][:, 256 * (t % 2) : 256 * (t % 2) + 256],
+                    lhsT=w1_codes[:, t, :].bitcast(FP8X4), lhsT_scale=w1_sc[:, t, :],
+                    rhs=ew[a][:].bitcast(FP8X4), rhs_scale=es[:, 256 * a : 256 * a + 256],
+                    start=True, stop=True,
+                )
+
+        def mm_y(c):
+            for t in range(4):
+                nc.tensor.matmul_mx(
+                    out=yb[c][:, P * t : P * t + P],
+                    lhsT=w1_codes[:, t, :].bitcast(FP8X4), lhsT_scale=w1_sc[:, t, :],
+                    rhs=xw[c // 2][:, P * (c % 2) : P * (c % 2) + P].bitcast(FP8X4), rhs_scale=xs[:, P * c : P * c + P],
+                    start=True, stop=True,
+                )
+
+        def red_h(a, b):
+            nc.vector.tensor_reduce(s_h[:, a, 64 * b : 64 * b + 64], hb[2 * a + b][:].rearrange("p (g d) -> p g d", d=D), AX.X, ALU.add)
+
+        def ctr_h(a, b):
+            nc.vector.scalar_tensor_tensor(
+                out=dev[a][:, :, 64 * b : 64 * b + 64],
+                in0=s_h[:, a, 64 * b : 64 * b + 64].unsqueeze(1).to_broadcast([P, D, 64]),
+                scalar=-1.0 / D,
+                in1=hb[2 * a + b][:].rearrange("p (g d) -> p d g", d=D),
+                op0=ALU.mult, op1=ALU.add,
+            )
+            nc.scalar.activation(sq[a][:, :, 64 * b : 64 * b + 64], dev[a][:, :, 64 * b : 64 * b + 64], ACT.Square)
+
+        def sum_t(dst, src):
+            for d in range(D):
+                nc.tensor.matmul(dst, lhsT=src[:, d, :], rhs=ident[:], start=(d == 0), stop=(d == D - 1), is_transpose=True)
+
+        s_y = tile("s_y", [P, 2, 32, 4], F32)
+        ys = [tile("ys%d" % a, [P, 8, P], F32) for a in range(2) ]
+        syt = [tile("syt%d" % a, [P, P], F32) for a in range(2)]
+
+        def red_y(c):
+            nc.vector.tensor_reduce(s_y[:, c // 2, 16 * (c % 2) : 16 * (c % 2) + 16, :], yb[c][:].rearrange("p (t v d) -> p v t d", t=4, d=D), AX.X, ALU.add)
+
+        def evac_y(c):
+            nc.scalar.copy(ys[c // 2][:, :, 64 * (c % 2) : 64 * (c % 2) + 64].rearrange("p d (v t) -> p d v t", t=4), yb[c][:].rearrange("p (t v d) -> p d v t", t=4, d=D))
+
+        r1 = [tile("r1%d" % a, [P, P], F32) for a in range(2)]
+        r1s = [tile("r1s%d" % a, [P, P], F32) for a in range(2)]
+        g1t = [tile("g1t%d" % a, [P, P], F32) for a in range(2)]
+        a_g = [tile("a_g%d" % a, [P, 32, 4], F32) for a in range(2)]
+        c_g = [tile("c_g%d" % a, [P, 32, 4], F32) for a in range(2)]
+        b_g = [tile("b_g%d" % a, [P, 32, 4], F32) for a in range(2)]
+        m2 = tile("m2", [P, 2, P], F32)
+        m2u = tile("m2u", [P, 2, 4, 32], F32)
+        r0 = tile("r0", [P, 2, P], F32)
+        r0s = tile("r0s", [P, 2, P], F32)
+        g0u = tile("g0u", [P, 2, 32, 4], F32)
+        u = [tile("u%d" % c, [P, 16, D, 4], F32) for c in range(4)]
+        z_bf = [tile("z_bf%d" % c, [P, 16, D, 4], BF16) for c in range(4)]
+        z_codes = [tile("z_codes%d" % c, [P, P], U32) for c in range(4)]
+        z_sc = [tile("z_sc%d" % c, [P, P], U8) for c in range(4)]
+        res = [tile("res%d" % c, [P, P], F32) for c in range(4)]
+        w2_bf = tile("w2_bf", [P, N, 4], BF16)
+        w2_codes = tile("w2_codes", [P, N], U32)
+        w2_sc = tile("w2_sc", [P, N], U8)
+
+        def var_chain(a):
+            qt = hb[2 * a][:, 0:P]
+            sum_t(qt, sq[a])
+            nc.scalar.activation(r1[a][:], qt, ACT.Abs_reciprocal_sqrt, bias=0.3, scale=1.0 / D)
+            nc.scalar.activation(r1s[a][:], r1[a][:], ACT.Square)
+            nc.vector.scalar_tensor_tensor(out=g1t[a][:], in0=qt, scalar=1.0 / D, in1=r1s[a][:], op0=ALU.mult, op1=ALU.mult)
+            nc.tensor.transpose(hb[2 * a + 1][:, 0:P], g1t[a][:], ident[:])
+
+        def mean_chain():
+            nc.scalar.activation(m2[:], s_h[:], ACT.Square, scale=1.0 / D)
+            nc.scalar.activation(r0[:], m2[:], ACT.Abs_reciprocal_sqrt, bias=0.2)
+            for t in range(4):
+                nc.scalar.activation(m2u[:, :, t, :], m2[:, :, 32 * t : 32 * t + 32], ACT.Copy, scale=unit_sb[:, t : t + 1])
+            nc.scalar.activation(r0s[:], r0[:], ACT.Square)
+            nc.vector.tensor_tensor(g0u[:], m2u[:].rearrange("p a t v -> p a v t"), r0s[:].rearrange("p a (t v) -> p a v t", t=4), ALU.mult)
+
+        def mean_half(a):
+            nc.scalar.activation(m2[:, a], s_h[:, a], ACT.Square, scale=1.0 / D)
+            nc.scalar.activation(r0[:, a], m2[:, a], ACT.Abs_reciprocal_sqrt, bias=0.2)
+            nc.scalar.activation(r0s[:, a], r0[:, a], ACT.Square)
+            nc.gpsimd.tensor_tensor(m2u[:, a], m2[:, a].rearrange("p (t v) -> p t v", t=4), unit_sb[:].unsqueeze(2).to_broadcast([P, 4, 32]), ALU.mult)
+            nc.gpsimd.tensor_tensor(g0u[:, a], m2u[:, a].rearrange("p t v -> p v t"), r0s[:, a].rearrange("p (t v) -> p v t", t=4), ALU.mult)
+
+        def ysum_pe(a, bank_t, bank_back):
+            sum_t(bank_t, ys[a])
+            nc.scalar.copy(syt[a][:], bank_t)
+            nc.tensor.transpose(bank_back, syt[a][:], ident[:])
+
+        def gain_a(a):
+            nc.vector.tensor_tensor(a_g[a][:], hb[2 * a + 1][:, 0:P].rearrange("p (t v) -> p v t", t=4), unit_sb[:].unsqueeze(1).to_broadcast([P, 32, 4]), ALU.mult)
+
+        def gain_c(a):
+            nc.vector.tensor_tensor(c_g[a][:], g0u[:, a], a_g[a][:], ALU.subtract)
+
+        def gain_b(a, sy):
+            nc.vector.scalar_tensor_tensor(out=b_g[a][:].rearrange("p v t -> p (v t)"), in0=sy, scalar=1.0 / D, in1=c_g[a][:].rearrange("p v t -> p (v t)"), op0=ALU.mult, op1=ALU.mult)
+
+        def per_group(g, c):
+            return g[c // 2][:, 16 * (c % 2) : 16 * (c % 2) + 16, :].unsqueeze(2).to_broadcast([P, 16, D, 4])
+
+        def mult_y(c):
+            nc.vector.tensor_tensor(u[c][:], yb[c][:].rearrange("p (t v d) -> p v d t", t=4, d=D), per_group(a_g, c), ALU.mult)
+
+        def add_b(c, eng=nc.vector):
+            eng.tensor_tensor(z_bf[c][:], u[c][:], per_group(b_g, c), ALU.add)
+
+        def finish(c):
+            nc.vector.quantize_mx(out=z_codes[c][:].bitcast(FP8X4), scales=z_sc[c][:], in_=z_bf[c][:].rearrange("p v d t -> p (v d t)"))
+            nc.tensor.matmul_mx(out=yb[c][:, 0:P], lhsT=w2_codes[:].bitcast(FP8X4), lhsT_scale=w2_sc[:], rhs=z_codes[c][:].bitcast(FP8X4), rhs_scale=z_sc[c][:], start=True, stop=True)
+            nc.scalar.copy(res[c][:], yb[c][:, 0:P])
+            nc.sync.dma_start(out[:, P * c : P * c + P], res[c][:])
+
+        mm_h(0)
+        mm_h(1)
+        nc.scalar.copy(w2_bf[:], w2_raw[:].rearrange("p j m -> p m j"))
+        nc.vector.quantize_mx(out=w2_codes[:].bitcast(FP8X4), scales=w2_sc[:], in_=w2_bf[:].rearrange("p m j -> p (m j)"))
+        red_h(0, 0)
+        red_h(0, 1)
+        ctr_h(0, 0)
+        ctr_h(0, 1)
+        var_chain(0)
+        red_h(1, 0)
+        red_h(1, 1)
+        ctr_h(1, 0)
+        ctr_h(1, 1)
+        gather_words(xw, xw_win, 0)
+        mm_y(0)
+        mm_y(1)
+        var_chain(1)
+        mean_half(0)
+        mean_half(1)
+        red_y(0)
+        red_y(1)
+        gain_a(0)
+        mult_y(0)
+        gain_c(0)
+        mult_y(1)
+        gain_b(0, s_y[:, 0].rearrange("p v t -> p (v t)"))
+        gather_words(xw, xw_win, 1)
+        mm_y(2)
+        mm_y(3)
+        evac_y(2)
+        evac_y(3)
+        ysum_pe(1, hb[0][:, P : 2 * P], hb[0][:, 2 * P : 3 * P])
+        add_b(0)
+        add_b(1)
+        finish(0)
+        finish(1)
+        gain_a(1)
+        mult_y(2)
+        gain_c(1)
+        mult_y(3)
+        gain_b(1, hb[0][:, 2 * P : 3 * P])
+        add_b(2)
+        add_b(3)
+        finish(2)
+        finish(3)

@@ -47,28 +47,28 @@ def tile_picked_ywien_wien_p_kernel(tc, x_words, x_scales, e_words, e_scales, w1
         nc.gpsimd.memset(es_win[:].bitcast(I32), 0)
         nc.vector.memset(xs_win[:].bitcast(I32), 0)
         nc.vector.memset(warm[:], 1.0)
-        nc.scalar.activation(warm[:], warm[:], ACT.Abs_reciprocal_sqrt)
-        make_identity(nc, ident[:])
 
-        def load_scales(win, src):
+        def load_scales(win, src, eng):
             for q in range(4):
-                nc.sync.dma_start(win[32 * q : 32 * q + 4, :].bitcast(I32), src[0, 4 * q : 4 * q + 4, :].bitcast(I32))
+                eng.dma_start(win[32 * q : 32 * q + 4, :].bitcast(I32), src[0, 4 * q : 4 * q + 4, :].bitcast(I32))
 
         def load_words(win, src):
             nc.sync.dma_start(win[:], src[0].rearrange("p n t -> p (n t)").bitcast(I32))
 
         w1_rows = w1.rearrange("(p j) c -> p j c", j=4)
+        nc.scalar.activation(warm[:], warm[:], ACT.Abs_reciprocal_sqrt)
+        make_identity(nc, ident[:])
+        load_words(ew_win, e_words)
         nc.sync.dma_start(offsets[:], offs)
-        load_scales(es_win, e_scales)
+        load_scales(es_win, e_scales, nc.sync)
         nc.sync.dma_start(w1_raw[0][:], w1_rows[:, :, 0:256])
         nc.sync.dma_start(w1_raw[1][:], w1_rows[:, :, 256:512])
-        load_scales(xs_win, x_scales)
-        load_words(ew_win, e_words)
-        nc.sync.dma_start(w2_raw[:], w2.rearrange("(p j) m -> p j m", j=4))
+        load_scales(xs_win, x_scales, nc.sync)
         load_words(xw_win, x_words)
         nc.sync.dma_start(unit_sb[:], unit.rearrange("(p t) o -> p (t o)", t=4))
+        nc.sync.dma_start(w2_raw[:], w2.rearrange("(p j) m -> p j m", j=4))
 
-        w1_bf = [tile("w1_bf%d" % a, [P, 4, 64, 4], BF16) for a in range(2)]
+        w1_bf = tile("w1_bf", [P, 4, P, 4], BF16)
         w1_codes = tile("w1_codes", [P, 4, P], U32)
         w1_sc = tile("w1_sc", [P, 4, P], U8)
         es = tile("es", [P, S], U8)
@@ -78,32 +78,31 @@ def tile_picked_ywien_wien_p_kernel(tc, x_words, x_scales, e_words, e_scales, w1
 
         def cast_w1(eng, a, m0, m1):
             src = w1_raw[a][:].rearrange("p j (m t) -> p m t j", t=4)[:, m0:m1]
-            dst = w1_bf[a][:].rearrange("p t m j -> p m t j")[:, m0:m1]
+            dst = w1_bf[:].rearrange("p t m j -> p m t j")[:, 64 * a + m0 : 64 * a + m1]
             if eng == "act":
                 nc.scalar.copy(dst, src)
             else:
                 nc.vector.tensor_copy(dst, src)
 
         def quant_w1(a):
-            for t in range(4):
-                nc.vector.quantize_mx(
-                    out=w1_codes[:, t, 64 * a : 64 * a + 64].bitcast(FP8X4),
-                    scales=w1_sc[:, t, 64 * a : 64 * a + 64],
-                    in_=w1_bf[a][:, t].rearrange("p m j -> p (m j)"),
-                )
+            nc.vector.quantize_mx(
+                out=w1_codes[:, 2 * a : 2 * a + 2, :].rearrange("p t m -> p (t m)").bitcast(FP8X4),
+                scales=w1_sc[:, 2 * a : 2 * a + 2, :].rearrange("p t m -> p (t m)"),
+                in_=w1_bf[:, 2 * a : 2 * a + 2].rearrange("p t m j -> p (t m j)"),
+            )
 
         def gather_words(dst, win, a):
             nc.vector.tensor_copy(dst[a][:], win[:].bitcast(U32).indirect(offsets[:, 16 * a : 16 * a + 16]))
 
         nc.vector.tensor_copy(es[:], es_win[:].indirect(offsets[:]))
+        gather_words(ew, ew_win, 0)
+        gather_words(ew, ew_win, 1)
         cast_w1("act", 0, 0, 64)
-        cast_w1("act", 1, 0, 32)
-        cast_w1("dve", 1, 32, 64)
+        cast_w1("act", 1, 0, 20)
+        cast_w1("dve", 1, 20, 64)
         quant_w1(0)
         quant_w1(1)
         nc.vector.tensor_copy(xs[:], xs_win[:].indirect(offsets[:]))
-        gather_words(ew, ew_win, 0)
-        gather_words(ew, ew_win, 1)
 
         s_h = tile("s_h", [P, 2, P], F32)
         dev = [tile("dev%d" % a, [P, 8, P], F32) for a in range(2)]
@@ -205,11 +204,17 @@ def tile_picked_ywien_wien_p_kernel(tc, x_words, x_scales, e_words, e_scales, w1
         def gain_a(a):
             nc.vector.tensor_tensor(a_g[a][:], hb[2 * a + 1][:, 0:P].rearrange("p (t v) -> p v t", t=4), unit_sb[:].unsqueeze(1).to_broadcast([P, 32, 4]), ALU.mult)
 
-        def gain_c(a):
-            nc.vector.tensor_tensor(c_g[a][:], g0u[:, a], a_g[a][:], ALU.subtract)
+        def gain_c(a, eng=nc.gpsimd):
+            eng.tensor_tensor(c_g[a][:], g0u[:, a], a_g[a][:], ALU.subtract)
 
         def gain_b(a, sy):
             nc.vector.scalar_tensor_tensor(out=b_g[a][:].rearrange("p v t -> p (v t)"), in0=sy, scalar=1.0 / D, in1=c_g[a][:].rearrange("p v t -> p (v t)"), op0=ALU.mult, op1=ALU.mult)
+
+        mc0 = tile("mc0", [P, 32, 4], F32)
+
+        def gain_b_pool():
+            nc.scalar.activation(mc0[:], s_y[:, 0], ACT.Copy, scale=1.0 / D)
+            nc.gpsimd.tensor_tensor(b_g[0][:], mc0[:], c_g[0][:], ALU.mult)
 
         def per_group(g, c):
             return g[c // 2][:, 16 * (c % 2) : 16 * (c % 2) + 16, :].unsqueeze(2).to_broadcast([P, 16, D, 4])
@@ -224,49 +229,49 @@ def tile_picked_ywien_wien_p_kernel(tc, x_words, x_scales, e_words, e_scales, w1
             nc.vector.quantize_mx(out=z_codes[c][:].bitcast(FP8X4), scales=z_sc[c][:], in_=z_bf[c][:].rearrange("p v d t -> p (v d t)"))
             nc.tensor.matmul_mx(out=yb[c][:, 0:P], lhsT=w2_codes[:].bitcast(FP8X4), lhsT_scale=w2_sc[:], rhs=z_codes[c][:].bitcast(FP8X4), rhs_scale=z_sc[c][:], start=True, stop=True)
             nc.scalar.copy(res[c][:], yb[c][:, 0:P])
-            nc.sync.dma_start(out[:, P * c : P * c + P], res[c][:])
+            (nc.scalar if c == 3 else nc.sync).dma_start(out[:, P * c : P * c + P], res[c][:])
 
         mm_h(0)
         mm_h(1)
-        nc.scalar.copy(w2_bf[:], w2_raw[:].rearrange("p j m -> p m j"))
-        nc.vector.quantize_mx(out=w2_codes[:].bitcast(FP8X4), scales=w2_sc[:], in_=w2_bf[:].rearrange("p m j -> p (m j)"))
-        red_h(0, 0)
-        red_h(0, 1)
-        ctr_h(0, 0)
-        ctr_h(0, 1)
+        red_h(0,0)
+        red_h(0,1)
+        ctr_h(0,0)
+        ctr_h(0,1)
+        mean_half(0)
         var_chain(0)
-        red_h(1, 0)
-        red_h(1, 1)
-        ctr_h(1, 0)
-        ctr_h(1, 1)
+        gain_a(0)
+        red_h(1,0)
+        red_h(1,1)
+        ctr_h(1,0)
+        ctr_h(1,1)
         gather_words(xw, xw_win, 0)
         mm_y(0)
         mm_y(1)
-        var_chain(1)
-        mean_half(0)
-        mean_half(1)
-        red_y(0)
-        red_y(1)
-        gain_a(0)
-        mult_y(0)
-        gain_c(0)
-        mult_y(1)
-        gain_b(0, s_y[:, 0].rearrange("p v t -> p (v t)"))
         gather_words(xw, xw_win, 1)
         mm_y(2)
         mm_y(3)
+        mean_half(1)
+        var_chain(1)
+        nc.scalar.copy(w2_bf[:], w2_raw[:].rearrange("p j m -> p m j"))
+        nc.vector.quantize_mx(out=w2_codes[:].bitcast(FP8X4), scales=w2_sc[:], in_=w2_bf[:].rearrange("p m j -> p (m j)"))
+        red_y(0)
+        red_y(1)
+        mult_y(0)
+        gain_c(0, nc.vector)
+        mult_y(1)
+        gain_b(0, s_y[:, 0].rearrange("p v t -> p (v t)"))
         evac_y(2)
         evac_y(3)
         ysum_pe(1, hb[0][:, P : 2 * P], hb[0][:, 2 * P : 3 * P])
+        gain_a(1)
         add_b(0)
         add_b(1)
-        finish(0)
-        finish(1)
-        gain_a(1)
         mult_y(2)
-        gain_c(1)
+        gain_c(1, nc.vector)
         mult_y(3)
         gain_b(1, hb[0][:, 2 * P : 3 * P])
+        finish(0)
+        finish(1)
         add_b(2)
         add_b(3)
         finish(2)

@@ -1,3 +1,4 @@
+import math
 from contextlib import ExitStack
 
 import concourse.mybir as mybir
@@ -18,7 +19,6 @@ ACT = mybir.ActivationFunctionType
 AX = mybir.AxisListType
 
 P = 128
-YSUM = ("dve", "pe")
 
 
 def tile_picked_ywien_wien_p_kernel(tc, x_words, x_scales, e_words, e_scales, w1, unit, w2, offs, out):
@@ -44,9 +44,10 @@ def tile_picked_ywien_wien_p_kernel(tc, x_words, x_scales, e_words, e_scales, w1
         ident = tile("ident", [P, P], F32)
         warm = tile("warm", [P, 1], F32)
 
+
         nc.gpsimd.memset(es_win[:].bitcast(I32), 0)
-        nc.vector.memset(xs_win[:].bitcast(I32), 0)
         nc.vector.memset(warm[:], 1.0)
+        nc.vector.memset(xs_win[:].bitcast(I32), 0)
 
         def load_scales(win, src, eng):
             for q in range(4):
@@ -58,11 +59,11 @@ def tile_picked_ywien_wien_p_kernel(tc, x_words, x_scales, e_words, e_scales, w1
         w1_rows = w1.rearrange("(p j) c -> p j c", j=4)
         nc.scalar.activation(warm[:], warm[:], ACT.Abs_reciprocal_sqrt)
         make_identity(nc, ident[:])
-        load_words(ew_win, e_words)
-        nc.sync.dma_start(offsets[:], offs)
-        load_scales(es_win, e_scales, nc.sync)
         nc.sync.dma_start(w1_raw[0][:], w1_rows[:, :, 0:256])
+        load_scales(es_win, e_scales, nc.sync)
+        nc.sync.dma_start(offsets[:], offs)
         nc.sync.dma_start(w1_raw[1][:], w1_rows[:, :, 256:512])
+        load_words(ew_win, e_words)
         load_scales(xs_win, x_scales, nc.sync)
         load_words(xw_win, x_words)
         nc.sync.dma_start(unit_sb[:], unit.rearrange("(p t) o -> p (t o)", t=4))
@@ -74,7 +75,7 @@ def tile_picked_ywien_wien_p_kernel(tc, x_words, x_scales, e_words, e_scales, w1
         es = tile("es", [P, S], U8)
         xs = tile("xs", [P, S], U8)
         ew = [tile("ew%d" % a, [P, 256], U32) for a in range(2)]
-        xw = [tile("xw%d" % a, [P, 256], U32) for a in range(2)]
+        xw = []
 
         def cast_w1(eng, a, m0, m1):
             src = w1_raw[a][:].rearrange("p j (m t) -> p m t j", t=4)[:, m0:m1]
@@ -94,19 +95,31 @@ def tile_picked_ywien_wien_p_kernel(tc, x_words, x_scales, e_words, e_scales, w1
         def gather_words(dst, win, a):
             nc.vector.tensor_copy(dst[a][:], win[:].bitcast(U32).indirect(offsets[:, 16 * a : 16 * a + 16]))
 
-        nc.vector.tensor_copy(es[:], es_win[:].indirect(offsets[:]))
-        gather_words(ew, ew_win, 0)
-        gather_words(ew, ew_win, 1)
-        cast_w1("act", 0, 0, 64)
-        cast_w1("act", 1, 0, 20)
-        cast_w1("dve", 1, 20, 64)
-        quant_w1(0)
-        quant_w1(1)
-        nc.vector.tensor_copy(xs[:], xs_win[:].indirect(offsets[:]))
+        h8 = [sb.tile([P, P], F32, name="h8%d" % a, tag="hold%d" % a, align_bytes=64) for a in range(2)]
+        dev = [tile("dev%d" % a, [P, D - 1, P], F32) for a in range(2)]
+        sq = [tile("sq%d" % a, [P, D - 1, P], F32) for a in range(2)]
+        small = {}
+        for nm in ("e1", "x1", "r1", "q1", "x0", "r0", "q0", "nq0", "a_g", "b_g", "umc", "s_y", "h8t", "m8"):
+            small[nm] = [tile("%s_%d" % (nm, a), [P, P], F32) for a in range(2)]
+        e1, x1, r1, q1 = small["e1"], small["x1"], small["r1"], small["q1"]
+        x0, r0, q0, nq0 = small["x0"], small["r0"], small["q0"], small["nq0"]
+        a_g, b_g, umc, s_y = small["a_g"], small["b_g"], small["umc"], small["s_y"]
+        h8t, m8 = small["h8t"], small["m8"]
+        negu = tile("negu", [P, 4], F32)
+        u = [tile("u%d" % c, [P, 16, D, 4], F32) for c in range(4)]
+        z_bf = [tile("z_bf%d" % c, [P, 16, D, 4], BF16) for c in range(4)]
+        z_codes = [tile("z_codes%d" % c, [P, P], U32) for c in range(4)]
+        z_sc = [tile("z_sc%d" % c, [P, P], U8) for c in range(4)]
+        res = [tile("res%d" % c, [P, P], F32) for c in range(4)]
+        w2_bf = tile("w2_bf", [P, N, 4], BF16)
+        w2_codes = tile("w2_codes", [P, N], U32)
+        w2_sc = tile("w2_sc", [P, N], U8)
 
-        s_h = tile("s_h", [P, 2, P], F32)
-        dev = [tile("dev%d" % a, [P, 8, P], F32) for a in range(2)]
-        sq = [tile("sq%d" % a, [P, 8, P], F32) for a in range(2)]
+        def vt(x):
+            return x.rearrange("p (v t) -> p v t", t=4)
+
+        def tv_as_vt(x):
+            return x.rearrange("p (t v) -> p v t", t=4)
 
         def mm_h(a):
             for t in range(4):
@@ -126,98 +139,65 @@ def tile_picked_ywien_wien_p_kernel(tc, x_words, x_scales, e_words, e_scales, w1
                     start=True, stop=True,
                 )
 
-        def red_h(a, b):
-            nc.vector.tensor_reduce(s_h[:, a, 64 * b : 64 * b + 64], hb[2 * a + b][:].rearrange("p (g d) -> p g d", d=D), AX.X, ALU.add)
+        def pivot(a, b):
+            nc.scalar.activation(h8[a][:, 64 * b : 64 * b + 64], hb[2 * a + b][:].rearrange("p (g d) -> p d g", d=D)[:, 0, :], ACT.Copy, scale=float(D))
 
-        def ctr_h(a, b):
+        def deviate(a, b):
             nc.vector.scalar_tensor_tensor(
                 out=dev[a][:, :, 64 * b : 64 * b + 64],
-                in0=s_h[:, a, 64 * b : 64 * b + 64].unsqueeze(1).to_broadcast([P, D, 64]),
+                in0=h8[a][:, 64 * b : 64 * b + 64].unsqueeze(1).to_broadcast([P, D - 1, 64]),
                 scalar=-1.0 / D,
-                in1=hb[2 * a + b][:].rearrange("p (g d) -> p d g", d=D),
+                in1=hb[2 * a + b][:].rearrange("p (g d) -> p d g", d=D)[:, 1:D, :],
                 op0=ALU.mult, op1=ALU.add,
             )
             nc.scalar.activation(sq[a][:, :, 64 * b : 64 * b + 64], dev[a][:, :, 64 * b : 64 * b + 64], ACT.Square)
 
+        def turn(dst, src, start, stop):
+            nc.tensor.matmul(dst, lhsT=src, rhs=ident[:], start=start, stop=stop, is_transpose=True)
+
         def sum_t(dst, src):
-            for d in range(D):
-                nc.tensor.matmul(dst, lhsT=src[:, d, :], rhs=ident[:], start=(d == 0), stop=(d == D - 1), is_transpose=True)
+            for d in range(D - 1):
+                turn(dst, src[:, d, :], d == 0, d == D - 2)
 
-        s_y = tile("s_y", [P, 2, 32, 4], F32)
-        ys = [tile("ys%d" % a, [P, 8, P], F32) for a in range(2) ]
-        syt = [tile("syt%d" % a, [P, P], F32) for a in range(2)]
+        def turn_pivot(a):
+            turn(hb[2 * a + 1][:, 2 * P : 3 * P], h8[a][:], True, True)
+            nc.scalar.copy(h8t[a][:], hb[2 * a + 1][:, 2 * P : 3 * P])
 
-        def red_y(c):
-            nc.vector.tensor_reduce(s_y[:, c // 2, 16 * (c % 2) : 16 * (c % 2) + 16, :], yb[c][:].rearrange("p (t v d) -> p v t d", t=4, d=D), AX.X, ALU.add)
-
-        def evac_y(c):
-            nc.scalar.copy(ys[c // 2][:, :, 64 * (c % 2) : 64 * (c % 2) + 64].rearrange("p d (v t) -> p d v t", t=4), yb[c][:].rearrange("p (t v d) -> p d v t", t=4, d=D))
-
-        r1 = [tile("r1%d" % a, [P, P], F32) for a in range(2)]
-        r1s = [tile("r1s%d" % a, [P, P], F32) for a in range(2)]
-        g1t = [tile("g1t%d" % a, [P, P], F32) for a in range(2)]
-        a_g = [tile("a_g%d" % a, [P, 32, 4], F32) for a in range(2)]
-        c_g = [tile("c_g%d" % a, [P, 32, 4], F32) for a in range(2)]
-        b_g = [tile("b_g%d" % a, [P, 32, 4], F32) for a in range(2)]
-        m2 = tile("m2", [P, 2, P], F32)
-        m2u = tile("m2u", [P, 2, 4, 32], F32)
-        r0 = tile("r0", [P, 2, P], F32)
-        r0s = tile("r0s", [P, 2, P], F32)
-        g0u = tile("g0u", [P, 2, 32, 4], F32)
-        u = [tile("u%d" % c, [P, 16, D, 4], F32) for c in range(4)]
-        z_bf = [tile("z_bf%d" % c, [P, 16, D, 4], BF16) for c in range(4)]
-        z_codes = [tile("z_codes%d" % c, [P, P], U32) for c in range(4)]
-        z_sc = [tile("z_sc%d" % c, [P, P], U8) for c in range(4)]
-        res = [tile("res%d" % c, [P, P], F32) for c in range(4)]
-        w2_bf = tile("w2_bf", [P, N, 4], BF16)
-        w2_codes = tile("w2_codes", [P, N], U32)
-        w2_sc = tile("w2_sc", [P, N], U8)
-
-        def var_chain(a):
-            qt = hb[2 * a][:, 0:P]
-            sum_t(qt, sq[a])
-            nc.scalar.activation(r1[a][:], qt, ACT.Abs_reciprocal_sqrt, bias=0.3, scale=1.0 / D)
-            nc.scalar.activation(r1s[a][:], r1[a][:], ACT.Square)
-            nc.vector.scalar_tensor_tensor(out=g1t[a][:], in0=qt, scalar=1.0 / D, in1=r1s[a][:], op0=ALU.mult, op1=ALU.mult)
-            nc.tensor.transpose(hb[2 * a + 1][:, 0:P], g1t[a][:], ident[:])
-
-        def mean_chain():
-            nc.scalar.activation(m2[:], s_h[:], ACT.Square, scale=1.0 / D)
-            nc.scalar.activation(r0[:], m2[:], ACT.Abs_reciprocal_sqrt, bias=0.2)
-            for t in range(4):
-                nc.scalar.activation(m2u[:, :, t, :], m2[:, :, 32 * t : 32 * t + 32], ACT.Copy, scale=unit_sb[:, t : t + 1])
-            nc.scalar.activation(r0s[:], r0[:], ACT.Square)
-            nc.vector.tensor_tensor(g0u[:], m2u[:].rearrange("p a t v -> p a v t"), r0s[:].rearrange("p a (t v) -> p a v t", t=4), ALU.mult)
-
-        def mean_half(a):
-            nc.scalar.activation(m2[:, a], s_h[:, a], ACT.Square, scale=1.0 / D)
-            nc.scalar.activation(r0[:, a], m2[:, a], ACT.Abs_reciprocal_sqrt, bias=0.2)
-            nc.scalar.activation(r0s[:, a], r0[:, a], ACT.Square)
-            nc.gpsimd.tensor_tensor(m2u[:, a], m2[:, a].rearrange("p (t v) -> p t v", t=4), unit_sb[:].unsqueeze(2).to_broadcast([P, 4, 32]), ALU.mult)
-            nc.gpsimd.tensor_tensor(g0u[:, a], m2u[:, a].rearrange("p t v -> p v t"), r0s[:, a].rearrange("p (t v) -> p v t", t=4), ALU.mult)
-
-        def ysum_pe(a, bank_t, bank_back):
-            sum_t(bank_t, ys[a])
-            nc.scalar.copy(syt[a][:], bank_t)
-            nc.tensor.transpose(bank_back, syt[a][:], ident[:])
+        def sums(a):
+            bank_a, bank_b = hb[2 * a], hb[2 * a + 1]
+            turn_pivot(a)
+            sum_t(bank_a[:, 0:P], dev[a])
+            nc.scalar.activation(e1[a][:], bank_a[:, 0:P], ACT.Square, scale=1.0 / (D * math.sqrt(0.3)))
+            sum_t(bank_b[:, 0:P], sq[a])
 
         def gain_a(a):
-            nc.vector.tensor_tensor(a_g[a][:], hb[2 * a + 1][:, 0:P].rearrange("p (t v) -> p v t", t=4), unit_sb[:].unsqueeze(1).to_broadcast([P, 32, 4]), ALU.mult)
+            bank_b = hb[2 * a + 1]
+            nc.vector.scalar_tensor_tensor(out=x1[a][:], in0=bank_b[:, 0:P], scalar=1.0 / (D * 0.3), in1=e1[a][:], op0=ALU.mult, op1=ALU.subtract)
+            nc.scalar.activation(r1[a][:], x1[a][:], ACT.Abs_reciprocal_sqrt, bias=1.0)
+            nc.scalar.activation(q1[a][:], r1[a][:], ACT.Square)
+            turn(bank_b[:, P : 2 * P], q1[a][:], True, True)
+            nc.vector.scalar_tensor_tensor(out=vt(a_g[a][:]), in0=tv_as_vt(bank_b[:, P : 2 * P]), scalar=-1.0, in1=negu[:].unsqueeze(1).to_broadcast([P, 32, 4]), op0=ALU.add, op1=ALU.mult)
 
-        def gain_c(a, eng=nc.gpsimd):
-            eng.tensor_tensor(c_g[a][:], g0u[:, a], a_g[a][:], ALU.subtract)
+        def mean_gain(a):
+            nc.vector.tensor_tensor(m8[a][:], hb[2 * a][:, 0:P], h8t[a][:], ALU.add)
+            nc.scalar.activation(x0[a][:], m8[a][:], ACT.Square, scale=1.0 / (D * math.sqrt(0.2)))
+            nc.scalar.activation(r0[a][:], x0[a][:], ACT.Abs_reciprocal_sqrt, bias=1.0)
+            nc.scalar.activation(q0[a][:], r0[a][:], ACT.Square)
+            nc.scalar.activation(nq0[a][:], q0[a][:], ACT.Copy, scale=-1.0)
 
-        def gain_b(a, sy):
-            nc.vector.scalar_tensor_tensor(out=b_g[a][:].rearrange("p v t -> p (v t)"), in0=sy, scalar=1.0 / D, in1=c_g[a][:].rearrange("p v t -> p (v t)"), op0=ALU.mult, op1=ALU.mult)
+        def gain_diff(a):
+            turn(hb[2 * a][:, P : 2 * P], q1[a][:], True, False)
+            turn(hb[2 * a][:, P : 2 * P], nq0[a][:], False, True)
 
-        mc0 = tile("mc0", [P, 32, 4], F32)
+        def red_y(c):
+            nc.vector.tensor_reduce(vt(s_y[c // 2][:])[:, 16 * (c % 2) : 16 * (c % 2) + 16, :], yb[c][:].rearrange("p (t v d) -> p v t d", t=4, d=D), AX.X, ALU.add)
 
-        def gain_b_pool():
-            nc.scalar.activation(mc0[:], s_y[:, 0], ACT.Copy, scale=1.0 / D)
-            nc.gpsimd.tensor_tensor(b_g[0][:], mc0[:], c_g[0][:], ALU.mult)
+        def offset_b(a):
+            nc.gpsimd.tensor_tensor(vt(umc[a][:]), vt(s_y[a][:]), negu[:].unsqueeze(1).to_broadcast([P, 32, 4]), ALU.mult)
+            nc.vector.scalar_tensor_tensor(out=vt(b_g[a][:]), in0=tv_as_vt(hb[2 * a][:, P : 2 * P]), scalar=-1.0 / D, in1=vt(umc[a][:]), op0=ALU.mult, op1=ALU.mult)
 
         def per_group(g, c):
-            return g[c // 2][:, 16 * (c % 2) : 16 * (c % 2) + 16, :].unsqueeze(2).to_broadcast([P, 16, D, 4])
+            return vt(g[c // 2][:])[:, 16 * (c % 2) : 16 * (c % 2) + 16, :].unsqueeze(2).to_broadcast([P, 16, D, 4])
 
         def mult_y(c):
             nc.vector.tensor_tensor(u[c][:], yb[c][:].rearrange("p (t v d) -> p v d t", t=4, d=D), per_group(a_g, c), ALU.mult)
@@ -231,46 +211,57 @@ def tile_picked_ywien_wien_p_kernel(tc, x_words, x_scales, e_words, e_scales, w1
             nc.scalar.copy(res[c][:], yb[c][:, 0:P])
             (nc.scalar if c == 3 else nc.sync).dma_start(out[:, P * c : P * c + P], res[c][:])
 
+
+        cast_w1("act", 0, 0, 64)
+        cast_w1("act", 1, 0, 32)
+        cast_w1("dve", 1, 32, 64)
+        quant_w1(0)
+        quant_w1(1)
+        nc.vector.tensor_copy(es[:], es_win[:].indirect(offsets[:]))
+        gather_words(ew, ew_win, 0)
         mm_h(0)
+        gather_words(ew, ew_win, 1)
         mm_h(1)
-        red_h(0,0)
-        red_h(0,1)
-        ctr_h(0,0)
-        ctr_h(0,1)
-        mean_half(0)
-        var_chain(0)
+        nc.vector.tensor_copy(xs[:], xs_win[:].indirect(offsets[:]))
+        nc.gpsimd.tensor_scalar(negu[:], unit_sb[:], -1.0, 0.0, ALU.mult, ALU.add)
+        for a in range(2):
+            pivot(a, 0)
+            pivot(a, 1)
+        for a in range(2):
+            deviate(a, 0)
+            deviate(a, 1)
+
+        def products_y(a):
+            xw.append(sb.tile([P, 256], U32, name="xw%d" % a, tag="hold%d" % a, align_bytes=64))
+            gather_words(xw, xw_win, a)
+            mm_y(2 * a)
+            mm_y(2 * a + 1)
+
+        nc.gpsimd.tensor_copy(w2_bf[:], w2_raw[:].rearrange("p j m -> p m j"))
+        sums(0)
+        products_y(0)
+        sums(1)
         gain_a(0)
-        red_h(1,0)
-        red_h(1,1)
-        ctr_h(1,0)
-        ctr_h(1,1)
-        gather_words(xw, xw_win, 0)
-        mm_y(0)
-        mm_y(1)
-        gather_words(xw, xw_win, 1)
-        mm_y(2)
-        mm_y(3)
-        mean_half(1)
-        var_chain(1)
-        nc.scalar.copy(w2_bf[:], w2_raw[:].rearrange("p j m -> p m j"))
+        mean_gain(0)
+        gain_diff(0)
+        products_y(1)
         nc.vector.quantize_mx(out=w2_codes[:].bitcast(FP8X4), scales=w2_sc[:], in_=w2_bf[:].rearrange("p m j -> p (m j)"))
         red_y(0)
         red_y(1)
-        mult_y(0)
-        gain_c(0, nc.vector)
-        mult_y(1)
-        gain_b(0, s_y[:, 0].rearrange("p v t -> p (v t)"))
-        evac_y(2)
-        evac_y(3)
-        ysum_pe(1, hb[0][:, P : 2 * P], hb[0][:, 2 * P : 3 * P])
         gain_a(1)
+        mean_gain(1)
+        gain_diff(1)
+        mult_y(0)
+        offset_b(0)
+        mult_y(1)
+        red_y(2)
+        red_y(3)
         add_b(0)
         add_b(1)
         mult_y(2)
-        gain_c(1, nc.vector)
-        mult_y(3)
-        gain_b(1, hb[0][:, 2 * P : 3 * P])
+        offset_b(1)
         finish(0)
+        mult_y(3)
         finish(1)
         add_b(2)
         add_b(3)

@@ -37,7 +37,7 @@ def tile_picked_ywien_wien_p_kernel(tc, x_words, x_scales, e_words, e_scales, w1
         es_win = tile("es_win", [P, T], U8)
         xs_win = tile("xs_win", [P, T], U8)
         ew_win = tile("ew_win", [P, T], I32)
-        xw_win = tile("xw_win", [P, T], I32)
+        xw_win = sb.tile([P, T], I32, name="xw_win", tag="hold", align_bytes=64)
         w1_raw = [tile("w1_raw%d" % a, [P, 4, 256], F32) for a in range(2)]
         w2_raw = tile("w2_raw", [P, 4, N], F32)
         unit_sb = tile("unit_sb", [P, 4], F32)
@@ -75,7 +75,7 @@ def tile_picked_ywien_wien_p_kernel(tc, x_words, x_scales, e_words, e_scales, w1
         es = tile("es", [P, S], U8)
         xs = tile("xs", [P, S], U8)
         ew = [tile("ew%d" % a, [P, 256], U32) for a in range(2)]
-        xw = []
+        xw = [tile("xw%d" % a, [P, 256], U32) for a in range(2)]
 
         def cast_w1(eng, a, m0, m1):
             src = w1_raw[a][:].rearrange("p j (m t) -> p m t j", t=4)[:, m0:m1]
@@ -95,8 +95,8 @@ def tile_picked_ywien_wien_p_kernel(tc, x_words, x_scales, e_words, e_scales, w1
         def gather_words(dst, win, a):
             nc.vector.tensor_copy(dst[a][:], win[:].bitcast(U32).indirect(offsets[:, 16 * a : 16 * a + 16]))
 
-        h8 = [sb.tile([P, P], F32, name="h8%d" % a, tag="hold%d" % a, align_bytes=64) for a in range(2)]
-        dev = [tile("dev%d" % a, [P, D - 1, P], F32) for a in range(2)]
+        h8 = [tile("h8%d" % a, [P, P], F32) for a in range(2)]
+        dev = []
         sq = [tile("sq%d" % a, [P, D - 1, P], F32) for a in range(2)]
         small = {}
         for nm in ("e1", "x1", "r1", "q1", "x0", "r0", "q0", "nq0", "a_g", "b_g", "umc", "s_y", "h8t", "m8"):
@@ -118,37 +118,34 @@ def tile_picked_ywien_wien_p_kernel(tc, x_words, x_scales, e_words, e_scales, w1
         def vt(x):
             return x.rearrange("p (v t) -> p v t", t=4)
 
-        def tv_as_vt(x):
-            return x.rearrange("p (t v) -> p v t", t=4)
+        def product(bank, words, scales, c):
+            for t in range(4):
+                nc.tensor.matmul_mx(
+                    out=bank[:, P * t : P * t + P],
+                    lhsT=w1_codes[:, t, :].bitcast(FP8X4), lhsT_scale=w1_sc[:, t, :],
+                    rhs=words[c // 2][:, P * (c % 2) : P * (c % 2) + P].bitcast(FP8X4), rhs_scale=scales[:, P * c : P * c + P],
+                    start=True, stop=True,
+                )
 
         def mm_h(a):
-            for t in range(4):
-                nc.tensor.matmul_mx(
-                    out=hb[2 * a + t // 2][:, 256 * (t % 2) : 256 * (t % 2) + 256],
-                    lhsT=w1_codes[:, t, :].bitcast(FP8X4), lhsT_scale=w1_sc[:, t, :],
-                    rhs=ew[a][:].bitcast(FP8X4), rhs_scale=es[:, 256 * a : 256 * a + 256],
-                    start=True, stop=True,
-                )
+            product(hb[2 * a], ew, es, 2 * a)
+            product(hb[2 * a + 1], ew, es, 2 * a + 1)
 
         def mm_y(c):
-            for t in range(4):
-                nc.tensor.matmul_mx(
-                    out=yb[c][:, P * t : P * t + P],
-                    lhsT=w1_codes[:, t, :].bitcast(FP8X4), lhsT_scale=w1_sc[:, t, :],
-                    rhs=xw[c // 2][:, P * (c % 2) : P * (c % 2) + P].bitcast(FP8X4), rhs_scale=xs[:, P * c : P * c + P],
-                    start=True, stop=True,
-                )
+            product(yb[c], xw, xs, c)
+
+        def members(bank):
+            return bank[:].rearrange("p (t v d) -> p d v t", t=4, d=D)
 
         def pivot(a, b):
-            nc.scalar.activation(h8[a][:, 64 * b : 64 * b + 64], hb[2 * a + b][:].rearrange("p (g d) -> p d g", d=D)[:, 0, :], ACT.Copy, scale=float(D))
+            nc.scalar.copy(vt(h8[a][:, 64 * b : 64 * b + 64]), members(hb[2 * a + b])[:, 0])
 
         def deviate(a, b):
-            nc.vector.scalar_tensor_tensor(
-                out=dev[a][:, :, 64 * b : 64 * b + 64],
-                in0=h8[a][:, 64 * b : 64 * b + 64].unsqueeze(1).to_broadcast([P, D - 1, 64]),
-                scalar=-1.0 / D,
-                in1=hb[2 * a + b][:].rearrange("p (g d) -> p d g", d=D)[:, 1:D, :],
-                op0=ALU.mult, op1=ALU.add,
+            nc.vector.tensor_tensor(
+                dev[a][:, :, 64 * b : 64 * b + 64].rearrange("p d (v t) -> p d v t", t=4),
+                members(hb[2 * a + b])[:, 1:D],
+                vt(h8[a][:, 64 * b : 64 * b + 64]).unsqueeze(1).to_broadcast([P, D - 1, 16, 4]),
+                ALU.subtract,
             )
             nc.scalar.activation(sq[a][:, :, 64 * b : 64 * b + 64], dev[a][:, :, 64 * b : 64 * b + 64], ACT.Square)
 
@@ -161,7 +158,7 @@ def tile_picked_ywien_wien_p_kernel(tc, x_words, x_scales, e_words, e_scales, w1
 
         def turn_pivot(a):
             turn(hb[2 * a + 1][:, 2 * P : 3 * P], h8[a][:], True, True)
-            nc.scalar.copy(h8t[a][:], hb[2 * a + 1][:, 2 * P : 3 * P])
+            nc.scalar.activation(h8t[a][:], hb[2 * a + 1][:, 2 * P : 3 * P], ACT.Copy, scale=float(D))
 
         def sums(a):
             bank_a, bank_b = hb[2 * a], hb[2 * a + 1]
@@ -176,7 +173,7 @@ def tile_picked_ywien_wien_p_kernel(tc, x_words, x_scales, e_words, e_scales, w1
             nc.scalar.activation(r1[a][:], x1[a][:], ACT.Abs_reciprocal_sqrt, bias=1.0)
             nc.scalar.activation(q1[a][:], r1[a][:], ACT.Square)
             turn(bank_b[:, P : 2 * P], q1[a][:], True, True)
-            nc.vector.scalar_tensor_tensor(out=vt(a_g[a][:]), in0=tv_as_vt(bank_b[:, P : 2 * P]), scalar=-1.0, in1=negu[:].unsqueeze(1).to_broadcast([P, 32, 4]), op0=ALU.add, op1=ALU.mult)
+            nc.vector.scalar_tensor_tensor(out=vt(a_g[a][:]), in0=vt(bank_b[:, P : 2 * P]), scalar=-1.0, in1=negu[:].unsqueeze(1).to_broadcast([P, 32, 4]), op0=ALU.add, op1=ALU.mult)
 
         def mean_gain(a):
             nc.vector.tensor_tensor(m8[a][:], hb[2 * a][:, 0:P], h8t[a][:], ALU.add)
@@ -194,7 +191,7 @@ def tile_picked_ywien_wien_p_kernel(tc, x_words, x_scales, e_words, e_scales, w1
 
         def offset_b(a):
             nc.gpsimd.tensor_tensor(vt(umc[a][:]), vt(s_y[a][:]), negu[:].unsqueeze(1).to_broadcast([P, 32, 4]), ALU.mult)
-            nc.vector.scalar_tensor_tensor(out=vt(b_g[a][:]), in0=tv_as_vt(hb[2 * a][:, P : 2 * P]), scalar=-1.0 / D, in1=vt(umc[a][:]), op0=ALU.mult, op1=ALU.mult)
+            nc.vector.scalar_tensor_tensor(out=vt(b_g[a][:]), in0=vt(hb[2 * a][:, P : 2 * P]), scalar=-1.0 / D, in1=vt(umc[a][:]), op0=ALU.mult, op1=ALU.mult)
 
         def per_group(g, c):
             return vt(g[c // 2][:])[:, 16 * (c % 2) : 16 * (c % 2) + 16, :].unsqueeze(2).to_broadcast([P, 16, D, 4])
@@ -228,34 +225,26 @@ def tile_picked_ywien_wien_p_kernel(tc, x_words, x_scales, e_words, e_scales, w1
             pivot(a, 0)
             pivot(a, 1)
         for a in range(2):
-            deviate(a, 0)
-            deviate(a, 1)
-
-        def products_y(a):
-            xw.append(sb.tile([P, 256], U32, name="xw%d" % a, tag="hold%d" % a, align_bytes=64))
             gather_words(xw, xw_win, a)
             mm_y(2 * a)
             mm_y(2 * a + 1)
-
+        dev_all = sb.tile([P, 2, D - 1, P], F32, name="dev_all", tag="hold", align_bytes=64)
+        dev.extend([dev_all[:, 0], dev_all[:, 1]])
+        for a in range(2):
+            deviate(a, 0)
+            deviate(a, 1)
         nc.gpsimd.tensor_copy(w2_bf[:], w2_raw[:].rearrange("p j m -> p m j"))
-        sums(0)
-        products_y(0)
-        sums(1)
-        gain_a(0)
-        mean_gain(0)
-        gain_diff(0)
-        products_y(1)
+        for a in range(2):
+            sums(a)
+            mean_gain(a)
+            gain_a(a)
+            gain_diff(a)
         nc.vector.quantize_mx(out=w2_codes[:].bitcast(FP8X4), scales=w2_sc[:], in_=w2_bf[:].rearrange("p m j -> p (m j)"))
-        red_y(0)
-        red_y(1)
-        gain_a(1)
-        mean_gain(1)
-        gain_diff(1)
+        for c in range(4):
+            red_y(c)
         mult_y(0)
         offset_b(0)
         mult_y(1)
-        red_y(2)
-        red_y(3)
         add_b(0)
         add_b(1)
         mult_y(2)

@@ -167,6 +167,19 @@ def tile_picked_ywien_wien_p_kernel(tc, x_words, x_scales, e_words, e_scales, w1
             nc.scalar.activation(e1[a][:], bank_a[:, 0:P], ACT.Square, scale=1.0 / (D * math.sqrt(0.3)))
             sum_t(bank_b[:, 0:P], sq[a])
 
+        s_h = tile("s_h", [P, P], F32)
+        nh8 = tile("nh8", [P, P], F32)
+
+        def sums_late():
+            nc.scalar.activation(nh8[:], h8[1][:], ACT.Copy, scale=-float(D))
+            for b in (1, 0):
+                nc.vector.tensor_reduce(vt(s_h[:, 64 * b : 64 * b + 64]), hb[2 + b][:].rearrange("p (t v d) -> p v t d", t=4, d=D), AX.X, ALU.add)
+            sum_t(hb[3][:, 0:P], sq[1])
+            turn(hb[2][:, 0:P], s_h[:], True, False)
+            turn(hb[2][:, 0:P], nh8[:], False, True)
+            turn(hb[2][:, 2 * P : 3 * P], s_h[:], True, True)
+            nc.scalar.activation(e1[1][:], hb[2][:, 0:P], ACT.Square, scale=1.0 / (D * math.sqrt(0.3)))
+
         def gain_a(a):
             bank_b = hb[2 * a + 1]
             nc.vector.scalar_tensor_tensor(out=x1[a][:], in0=bank_b[:, 0:P], scalar=1.0 / (D * 0.3), in1=e1[a][:], op0=ALU.mult, op1=ALU.subtract)
@@ -176,8 +189,9 @@ def tile_picked_ywien_wien_p_kernel(tc, x_words, x_scales, e_words, e_scales, w1
             nc.vector.scalar_tensor_tensor(out=vt(a_g[a][:]), in0=vt(bank_b[:, P : 2 * P]), scalar=-1.0, in1=negu[:].unsqueeze(1).to_broadcast([P, 32, 4]), op0=ALU.add, op1=ALU.mult)
 
         def mean_gain(a):
-            nc.vector.tensor_tensor(m8[a][:], hb[2 * a][:, 0:P], h8t[a][:], ALU.add)
-            nc.scalar.activation(x0[a][:], m8[a][:], ACT.Square, scale=1.0 / (D * math.sqrt(0.2)))
+            if a == 0:
+                nc.vector.tensor_tensor(m8[a][:], hb[2 * a][:, 0:P], h8t[a][:], ALU.add)
+            nc.scalar.activation(x0[a][:], (m8[0][:], hb[2][:, 2 * P : 3 * P])[a], ACT.Square, scale=1.0 / (D * math.sqrt(0.2)))
             nc.scalar.activation(r0[a][:], x0[a][:], ACT.Abs_reciprocal_sqrt, bias=1.0)
             nc.scalar.activation(q0[a][:], r0[a][:], ACT.Square)
             nc.scalar.activation(nq0[a][:], q0[a][:], ACT.Copy, scale=-1.0)
@@ -234,25 +248,26 @@ def tile_picked_ywien_wien_p_kernel(tc, x_words, x_scales, e_words, e_scales, w1
             deviate(a, 0)
             deviate(a, 1)
         nc.gpsimd.tensor_copy(w2_bf[:], w2_raw[:].rearrange("p j m -> p m j"))
-        for a in range(2):
-            sums(a)
-            mean_gain(a)
-            gain_a(a)
-            gain_diff(a)
+        sums(0)
+        mean_gain(0)
+        gain_a(0)
+        gain_diff(0)
+        sums_late()
+        mean_gain(1)
+        gain_a(1)
+        gain_diff(1)
         nc.vector.quantize_mx(out=w2_codes[:].bitcast(FP8X4), scales=w2_sc[:], in_=w2_bf[:].rearrange("p m j -> p (m j)"))
         for c in range(4):
             red_y(c)
         mult_y(0)
         offset_b(0)
         mult_y(1)
-        add_b(0)
-        add_b(1)
+        add_b(0, nc.gpsimd)
+        add_b(1, nc.gpsimd)
         mult_y(2)
         offset_b(1)
-        finish(0)
         mult_y(3)
-        finish(1)
         add_b(2)
         add_b(3)
-        finish(2)
-        finish(3)
+        for c in range(4):
+            finish(c)

@@ -25,6 +25,7 @@ def tile_picked_ywien_wien_p_kernel(tc, x_words, x_scales, e_words, e_scales, w1
     nc = tc.nc
     with ExitStack() as ctx:
         sb = ctx.enter_context(tc.tile_pool(name="sb", bufs=1))
+        reuse = ctx.enter_context(tc.tile_pool(name="reuse", bufs=1))
         ps = ctx.enter_context(tc.psum_pool(name="ps", bufs=1))
 
         def tile(name, shape, dt):
@@ -35,9 +36,9 @@ def tile_picked_ywien_wien_p_kernel(tc, x_words, x_scales, e_words, e_scales, w1
         yb = [ps.tile([P, 512], F32, name="yb%d" % b) for b in range(4)]
 
         es_win = tile("es_win", [P, T], U8)
-        xs_win = tile("xs_win", [P, T], U8)
+        xs_win = sb.tile([P, T], U8, name="xs_win", tag="hold_s", align_bytes=64)
         ew_win = tile("ew_win", [P, T], I32)
-        xw_win = sb.tile([P, T], I32, name="xw_win", tag="hold", align_bytes=64)
+        xw_win = reuse.tile([P, T], I32, name="xw_win", offset=0)
         w1_raw = [tile("w1_raw%d" % a, [P, 4, 256], F32) for a in range(2)]
         w2_raw = tile("w2_raw", [P, 4, N], F32)
         unit_sb = tile("unit_sb", [P, 4], F32)
@@ -203,6 +204,21 @@ def tile_picked_ywien_wien_p_kernel(tc, x_words, x_scales, e_words, e_scales, w1
         def red_y(c):
             nc.vector.tensor_reduce(vt(s_y[c // 2][:])[:, 16 * (c % 2) : 16 * (c % 2) + 16, :], yb[c][:].rearrange("p (t v d) -> p v t d", t=4, d=D), AX.X, ALU.add)
 
+        ys = tile("ys", [P, D, P], F32)
+        syt = tile("syt", [P, P], F32)
+
+        def sum_y_tensor():
+            for c in (2, 3):
+                nc.scalar.copy(ys[:, :, 64 * (c % 2) : 64 * (c % 2) + 64].rearrange("p d (v t) -> p d v t", t=4), members(yb[c]))
+            for d in range(D):
+                turn(hb[1][:, 0:P], ys[:, d, :], d == 0, d == D - 1)
+            nc.scalar.copy(syt[:], hb[1][:, 0:P])
+            turn(hb[1][:, P : 2 * P], syt[:], True, True)
+
+        def offset_b_late():
+            nc.vector.tensor_tensor(vt(umc[1][:]), vt(hb[2][:, P : 2 * P]), negu[:].unsqueeze(1).to_broadcast([P, 32, 4]), ALU.mult)
+            nc.vector.scalar_tensor_tensor(out=b_g[1][:], in0=hb[1][:, P : 2 * P], scalar=-1.0 / D, in1=umc[1][:], op0=ALU.mult, op1=ALU.mult)
+
         def offset_b(a):
             nc.gpsimd.tensor_tensor(vt(umc[a][:]), vt(s_y[a][:]), negu[:].unsqueeze(1).to_broadcast([P, 32, 4]), ALU.mult)
             nc.vector.scalar_tensor_tensor(out=vt(b_g[a][:]), in0=vt(hb[2 * a][:, P : 2 * P]), scalar=-1.0 / D, in1=vt(umc[a][:]), op0=ALU.mult, op1=ALU.mult)
@@ -238,36 +254,42 @@ def tile_picked_ywien_wien_p_kernel(tc, x_words, x_scales, e_words, e_scales, w1
         for a in range(2):
             pivot(a, 0)
             pivot(a, 1)
+        dev.append(sb.tile([P, D - 1, P], F32, name="dev0", tag="hold_s", align_bytes=64))
+        deviate(0, 0)
+        deviate(0, 1)
         for a in range(2):
             gather_words(xw, xw_win, a)
-            mm_y(2 * a)
-            mm_y(2 * a + 1)
-        dev_all = sb.tile([P, 2, D - 1, P], F32, name="dev_all", tag="hold", align_bytes=64)
-        dev.extend([dev_all[:, 0], dev_all[:, 1]])
-        for a in range(2):
-            deviate(a, 0)
-            deviate(a, 1)
-        nc.gpsimd.tensor_copy(w2_bf[:], w2_raw[:].rearrange("p j m -> p m j"))
+        dev.append(reuse.tile([P, D - 1, P], F32, name="dev1", offset=0))
+        m8[0:1] = [reuse.tile([P, P], F32, name="m8_late", offset=4096)]
+        x1[0:1] = [reuse.tile([P, P], F32, name="x1_late", offset=4608)]
+        deviate(1, 0)
+        deviate(1, 1)
         sums(0)
         mean_gain(0)
         gain_a(0)
         gain_diff(0)
+        for c in range(4):
+            mm_y(c)
+        nc.gpsimd.tensor_copy(w2_bf[:], w2_raw[:].rearrange("p j m -> p m j"))
         sums_late()
         mean_gain(1)
         gain_a(1)
         gain_diff(1)
         nc.vector.quantize_mx(out=w2_codes[:].bitcast(FP8X4), scales=w2_sc[:], in_=w2_bf[:].rearrange("p m j -> p (m j)"))
-        for c in range(4):
-            red_y(c)
+        red_y(0)
+        red_y(1)
+        sum_y_tensor()
         mult_y(0)
         offset_b(0)
         mult_y(1)
-        add_b(0, nc.gpsimd)
-        add_b(1, nc.gpsimd)
+        add_b(0)
+        add_b(1)
         mult_y(2)
-        offset_b(1)
+        finish(0)
         mult_y(3)
+        offset_b_late()
+        finish(1)
         add_b(2)
         add_b(3)
-        for c in range(4):
-            finish(c)
+        finish(2)
+        finish(3)

@@ -38,7 +38,7 @@ def tile_picked_ywien_wien_p_kernel(tc, x_words, x_scales, e_words, e_scales, w1
         es_win = tile("es_win", [P, T], U8)
         xs_win = sb.tile([P, T], U8, name="xs_win", tag="hold_s", align_bytes=64)
         ew_win = tile("ew_win", [P, T], I32)
-        xw_win = reuse.tile([P, T], I32, name="xw_win", offset=0)
+        xw_win = reuse.tile([P, T], I32, name="xw_win", offset=0, align_bytes=64)
         w1_raw = [tile("w1_raw%d" % a, [P, 4, 256], F32) for a in range(2)]
         w2_raw = tile("w2_raw", [P, 4, N], F32)
         unit_sb = tile("unit_sb", [P, 4], F32)
@@ -50,9 +50,9 @@ def tile_picked_ywien_wien_p_kernel(tc, x_words, x_scales, e_words, e_scales, w1
         nc.vector.memset(warm[:], 1.0)
         nc.vector.memset(xs_win[:].bitcast(I32), 0)
 
-        def load_scales(win, src, eng):
+        def load_scales(win, src, eng, k=0):
             for q in range(4):
-                eng.dma_start(win[32 * q : 32 * q + 4, :].bitcast(I32), src[0, 4 * q : 4 * q + 4, :].bitcast(I32))
+                eng.dma_start(win[32 * q + k : 32 * q + k + 4, :].bitcast(I32), src[0, 4 * q : 4 * q + 4, :].bitcast(I32))
 
         def load_words(win, src):
             nc.sync.dma_start(win[:], src[0].rearrange("p n t -> p (n t)").bitcast(I32))
@@ -65,7 +65,7 @@ def tile_picked_ywien_wien_p_kernel(tc, x_words, x_scales, e_words, e_scales, w1
         nc.sync.dma_start(offsets[:], offs)
         nc.sync.dma_start(w1_raw[1][:], w1_rows[:, :, 256:512])
         load_words(ew_win, e_words)
-        load_scales(xs_win, x_scales, nc.sync)
+        load_scales(xs_win, x_scales, nc.sync, 4)
         load_words(xw_win, x_words)
         nc.sync.dma_start(unit_sb[:], unit.rearrange("(p t) o -> p (t o)", t=4))
         nc.sync.dma_start(w2_raw[:], w2.rearrange("(p j) m -> p j m", j=4))
@@ -112,19 +112,18 @@ def tile_picked_ywien_wien_p_kernel(tc, x_words, x_scales, e_words, e_scales, w1
         z_codes = [tile("z_codes%d" % c, [P, P], U32) for c in range(4)]
         z_sc = [tile("z_sc%d" % c, [P, P], U8) for c in range(4)]
         res = [tile("res%d" % c, [P, P], F32) for c in range(4)]
-        w2_bf = tile("w2_bf", [P, N, 4], BF16)
         w2_codes = tile("w2_codes", [P, N], U32)
         w2_sc = tile("w2_sc", [P, N], U8)
 
         def vt(x):
             return x.rearrange("p (v t) -> p v t", t=4)
 
-        def product(bank, words, scales, c):
+        def product(bank, words, scales, c, k=0):
             for t in range(4):
                 nc.tensor.matmul_mx(
                     out=bank[:, P * t : P * t + P],
                     lhsT=w1_codes[:, t, :].bitcast(FP8X4), lhsT_scale=w1_sc[:, t, :],
-                    rhs=words[c // 2][:, P * (c % 2) : P * (c % 2) + P].bitcast(FP8X4), rhs_scale=scales[:, P * c : P * c + P],
+                    rhs=words[c // 2][:, P * (c % 2) : P * (c % 2) + P].bitcast(FP8X4), rhs_scale=scales[k:P, P * c : P * c + P],
                     start=True, stop=True,
                 )
 
@@ -133,7 +132,7 @@ def tile_picked_ywien_wien_p_kernel(tc, x_words, x_scales, e_words, e_scales, w1
             product(hb[2 * a + 1], ew, es, 2 * a + 1)
 
         def mm_y(c):
-            product(yb[c], xw, xs, c)
+            product(yb[c], xw, xs, c, 4)
 
         def members(bank):
             return bank[:].rearrange("p (t v d) -> p d v t", t=4, d=D)
@@ -169,22 +168,26 @@ def tile_picked_ywien_wien_p_kernel(tc, x_words, x_scales, e_words, e_scales, w1
             sum_t(bank_b[:, 0:P], sq[a])
 
         s_h = tile("s_h", [P, P], F32)
-        nh8 = tile("nh8", [P, P], F32)
+        s_dev = tile("s_dev", [P, P], F32)
+        neg_sq = tile("neg_sq", [P, P], F32)
 
         def sums_late():
-            nc.scalar.activation(nh8[:], h8[1][:], ACT.Copy, scale=-float(D))
-            for b in (1, 0):
+            for b in (0, 1):
                 nc.vector.tensor_reduce(vt(s_h[:, 64 * b : 64 * b + 64]), hb[2 + b][:].rearrange("p (t v d) -> p v t d", t=4, d=D), AX.X, ALU.add)
-            sum_t(hb[3][:, 0:P], sq[1])
-            turn(hb[2][:, 0:P], s_h[:], True, False)
-            turn(hb[2][:, 0:P], nh8[:], False, True)
+            nc.vector.scalar_tensor_tensor(out=s_dev[:], in0=h8[1][:], scalar=-float(D), in1=s_h[:], op0=ALU.mult, op1=ALU.add)
+            nc.vector.scalar_tensor_tensor(out=neg_sq[:], in0=s_dev[:], scalar=-1.0 / D, in1=s_dev[:], op0=ALU.mult, op1=ALU.mult)
+            for d in range(D - 1):
+                turn(hb[3][:, 0:P], sq[1][:, d, :], d == 0, False)
+            turn(hb[3][:, 0:P], neg_sq[:], False, True)
             turn(hb[2][:, 2 * P : 3 * P], s_h[:], True, True)
-            nc.scalar.activation(e1[1][:], hb[2][:, 0:P], ACT.Square, scale=1.0 / (D * math.sqrt(0.3)))
 
         def gain_a(a):
             bank_b = hb[2 * a + 1]
-            nc.vector.scalar_tensor_tensor(out=x1[a][:], in0=bank_b[:, 0:P], scalar=1.0 / (D * 0.3), in1=e1[a][:], op0=ALU.mult, op1=ALU.subtract)
-            nc.scalar.activation(r1[a][:], x1[a][:], ACT.Abs_reciprocal_sqrt, bias=1.0)
+            if a == 0:
+                nc.vector.scalar_tensor_tensor(out=x1[a][:], in0=bank_b[:, 0:P], scalar=1.0 / (D * 0.3), in1=e1[a][:], op0=ALU.mult, op1=ALU.subtract)
+                nc.scalar.activation(r1[a][:], x1[a][:], ACT.Abs_reciprocal_sqrt, bias=1.0)
+            else:
+                nc.scalar.activation(r1[a][:], bank_b[:, 0:P], ACT.Abs_reciprocal_sqrt, bias=1.0, scale=1.0 / (D * 0.3))
             nc.scalar.activation(q1[a][:], r1[a][:], ACT.Square)
             turn(bank_b[:, P : 2 * P], q1[a][:], True, True)
             nc.vector.scalar_tensor_tensor(out=vt(a_g[a][:]), in0=vt(bank_b[:, P : 2 * P]), scalar=-1.0, in1=negu[:].unsqueeze(1).to_broadcast([P, 32, 4]), op0=ALU.add, op1=ALU.mult)
@@ -257,7 +260,7 @@ def tile_picked_ywien_wien_p_kernel(tc, x_words, x_scales, e_words, e_scales, w1
         dev.append(sb.tile([P, D - 1, P], F32, name="dev0", tag="hold_s", align_bytes=64))
         deviate(0, 0)
         deviate(0, 1)
-        for a in range(2):
+        for a in (1, 0):
             gather_words(xw, xw_win, a)
         dev.append(reuse.tile([P, D - 1, P], F32, name="dev1", offset=0))
         m8[0:1] = [reuse.tile([P, P], F32, name="m8_late", offset=4096)]
@@ -268,12 +271,13 @@ def tile_picked_ywien_wien_p_kernel(tc, x_words, x_scales, e_words, e_scales, w1
         mean_gain(0)
         gain_a(0)
         gain_diff(0)
-        for c in range(4):
+        for c in (2, 3, 0, 1):
             mm_y(c)
+        w2_bf = reuse.tile([P, N, 4], BF16, name="w2_bf", offset=5120)
         nc.gpsimd.tensor_copy(w2_bf[:], w2_raw[:].rearrange("p j m -> p m j"))
         sums_late()
-        mean_gain(1)
         gain_a(1)
+        mean_gain(1)
         gain_diff(1)
         nc.vector.quantize_mx(out=w2_codes[:].bitcast(FP8X4), scales=w2_sc[:], in_=w2_bf[:].rearrange("p m j -> p (m j)"))
         red_y(0)

@@ -19,6 +19,13 @@ ACT = mybir.ActivationFunctionType
 AX = mybir.AxisListType
 
 P = 128
+SLOTS = 4
+GROUPS = P // D
+CHUNK_COLS = GROUPS * SLOTS
+HALF = 2 * P
+MEAN_NOISE, VAR_NOISE = 0.2, 0.3
+E_PLANE, X_PLANE = 0, 4
+SCALAR_SHARE = 32
 
 
 def tile_picked_ywien_wien_p_kernel(tc, x_words, x_scales, e_words, e_scales, w1, unit, w2, offs, out):
@@ -28,272 +35,251 @@ def tile_picked_ywien_wien_p_kernel(tc, x_words, x_scales, e_words, e_scales, w1
         reuse = ctx.enter_context(tc.tile_pool(name="reuse", bufs=1))
         ps = ctx.enter_context(tc.psum_pool(name="ps", bufs=1))
 
-        def tile(name, shape, dt):
+        def tile(name, shape, dt=F32):
             return sb.tile(shape, dt, name=name, align_bytes=64)
 
+        def per_half(name):
+            return [tile("%s%d" % (name, a), [P, P]) for a in range(2)]
+
         offsets = sb.tile([P, S // 16], U16, name="offsets")
-        hb = [ps.tile([P, 512], F32, name="hb%d" % b) for b in range(4)]
-        yb = [ps.tile([P, 512], F32, name="yb%d" % b) for b in range(4)]
+        h_bank = [ps.tile([P, SLOTS * P], F32, name="h_bank%d" % c) for c in range(4)]
+        y_bank = [ps.tile([P, SLOTS * P], F32, name="y_bank%d" % c) for c in range(4)]
 
-        es_win = tile("es_win", [P, T], U8)
-        xs_win = sb.tile([P, T], U8, name="xs_win", tag="hold_s", align_bytes=64)
-        ew_win = tile("ew_win", [P, T], I32)
-        xw_win = reuse.tile([P, T], I32, name="xw_win", offset=0, align_bytes=64)
-        w1_raw = [tile("w1_raw%d" % a, [P, 4, 256], F32) for a in range(2)]
-        w2_raw = tile("w2_raw", [P, 4, N], F32)
-        unit_sb = tile("unit_sb", [P, 4], F32)
-        ident = tile("ident", [P, P], F32)
-        warm = tile("warm", [P, 1], F32)
+        e_scale_win = tile("e_scale_win", [P, T], U8)
+        x_scale_win = sb.tile([P, T], U8, name="x_scale_win", tag="x_scale_bytes", align_bytes=64)
+        e_word_win = tile("e_word_win", [P, T], I32)
+        x_word_win = reuse.tile([P, T], I32, name="x_word_win", offset=0, align_bytes=64)
+        w1_raw = [tile("w1_raw%d" % part, [P, SLOTS, H // 2]) for part in range(2)]
+        w2_raw = tile("w2_raw", [P, SLOTS, N])
+        unit_sb = tile("unit_sb", [P, SLOTS])
+        ident = tile("ident", [P, P])
+        warm = tile("warm", [P, 1])
 
-
-        nc.gpsimd.memset(es_win[:].bitcast(I32), 0)
+        nc.gpsimd.memset(e_scale_win[:].bitcast(I32), 0)
         nc.vector.memset(warm[:], 1.0)
-        nc.vector.memset(xs_win[:].bitcast(I32), 0)
+        nc.vector.memset(x_scale_win[:].bitcast(I32), 0)
 
-        def load_scales(win, src, eng, k=0):
+        def load_scales(win, src, plane):
             for q in range(4):
-                eng.dma_start(win[32 * q + k : 32 * q + k + 4, :].bitcast(I32), src[0, 4 * q : 4 * q + 4, :].bitcast(I32))
+                rows = slice(32 * q + plane, 32 * q + plane + 4)
+                nc.sync.dma_start(win[rows, :].bitcast(I32), src[0, 4 * q : 4 * q + 4, :].bitcast(I32))
 
         def load_words(win, src):
             nc.sync.dma_start(win[:], src[0].rearrange("p n t -> p (n t)").bitcast(I32))
 
-        w1_rows = w1.rearrange("(p j) c -> p j c", j=4)
         nc.scalar.activation(warm[:], warm[:], ACT.Abs_reciprocal_sqrt)
         make_identity(nc, ident[:])
-        nc.sync.dma_start(w1_raw[0][:], w1_rows[:, :, 0:256])
-        load_scales(es_win, e_scales, nc.sync)
+
+        w1_rows = w1.rearrange("(p j) c -> p j c", j=SLOTS)
+        nc.sync.dma_start(w1_raw[0][:], w1_rows[:, :, 0 : H // 2])
+        load_scales(e_scale_win, e_scales, E_PLANE)
         nc.sync.dma_start(offsets[:], offs)
-        nc.sync.dma_start(w1_raw[1][:], w1_rows[:, :, 256:512])
-        load_words(ew_win, e_words)
-        load_scales(xs_win, x_scales, nc.sync, 4)
-        load_words(xw_win, x_words)
-        nc.sync.dma_start(unit_sb[:], unit.rearrange("(p t) o -> p (t o)", t=4))
-        nc.sync.dma_start(w2_raw[:], w2.rearrange("(p j) m -> p j m", j=4))
+        nc.sync.dma_start(w1_raw[1][:], w1_rows[:, :, H // 2 : H])
+        load_words(e_word_win, e_words)
+        load_scales(x_scale_win, x_scales, X_PLANE)
+        load_words(x_word_win, x_words)
+        nc.sync.dma_start(unit_sb[:], unit.rearrange("(p t) o -> p (t o)", t=SLOTS))
+        nc.sync.dma_start(w2_raw[:], w2.rearrange("(p j) m -> p j m", j=SLOTS))
 
-        w1_bf = tile("w1_bf", [P, 4, P, 4], BF16)
-        w1_codes = tile("w1_codes", [P, 4, P], U32)
-        w1_sc = tile("w1_sc", [P, 4, P], U8)
-        es = tile("es", [P, S], U8)
-        xs = tile("xs", [P, S], U8)
-        ew = [tile("ew%d" % a, [P, 256], U32) for a in range(2)]
-        xw = [tile("xw%d" % a, [P, 256], U32) for a in range(2)]
-
-        def cast_w1(eng, a, m0, m1):
-            src = w1_raw[a][:].rearrange("p j (m t) -> p m t j", t=4)[:, m0:m1]
-            dst = w1_bf[:].rearrange("p t m j -> p m t j")[:, 64 * a + m0 : 64 * a + m1]
-            if eng == "act":
-                nc.scalar.copy(dst, src)
-            else:
-                nc.vector.tensor_copy(dst, src)
-
-        def quant_w1(a):
-            nc.vector.quantize_mx(
-                out=w1_codes[:, 2 * a : 2 * a + 2, :].rearrange("p t m -> p (t m)").bitcast(FP8X4),
-                scales=w1_sc[:, 2 * a : 2 * a + 2, :].rearrange("p t m -> p (t m)"),
-                in_=w1_bf[:, 2 * a : 2 * a + 2].rearrange("p t m j -> p (t m j)"),
-            )
-
-        def gather_words(dst, win, a):
-            nc.vector.tensor_copy(dst[a][:], win[:].bitcast(U32).indirect(offsets[:, 16 * a : 16 * a + 16]))
-
-        h8 = [tile("h8%d" % a, [P, P], F32) for a in range(2)]
-        dev = []
-        sq = [tile("sq%d" % a, [P, D - 1, P], F32) for a in range(2)]
-        small = {}
-        for nm in ("e1", "x1", "r1", "q1", "x0", "r0", "q0", "nq0", "a_g", "b_g", "umc", "s_y", "h8t", "m8"):
-            small[nm] = [tile("%s_%d" % (nm, a), [P, P], F32) for a in range(2)]
-        e1, x1, r1, q1 = small["e1"], small["x1"], small["r1"], small["q1"]
-        x0, r0, q0, nq0 = small["x0"], small["r0"], small["q0"], small["nq0"]
-        a_g, b_g, umc, s_y = small["a_g"], small["b_g"], small["umc"], small["s_y"]
-        h8t, m8 = small["h8t"], small["m8"]
-        negu = tile("negu", [P, 4], F32)
-        u = [tile("u%d" % c, [P, 16, D, 4], F32) for c in range(4)]
-        z_bf = [tile("z_bf%d" % c, [P, 16, D, 4], BF16) for c in range(4)]
+        w1_bf = tile("w1_bf", [P, SLOTS, P, SLOTS], BF16)
+        w1_codes = tile("w1_codes", [P, SLOTS, P], U32)
+        w1_sc = tile("w1_sc", [P, SLOTS, P], U8)
+        e_sc = tile("e_sc", [P, S], U8)
+        x_sc = tile("x_sc", [P, S], U8)
+        e_codes = [tile("e_codes%d" % a, [P, HALF], U32) for a in range(2)]
+        x_codes = [tile("x_codes%d" % a, [P, HALF], U32) for a in range(2)]
+        h0 = per_half("h0")
+        sq = [tile("sq%d" % a, [P, D - 1, P]) for a in range(2)]
+        root1, q1, mean_sq, root0, q0, neg_q0 = (per_half(nm) for nm in ("root1", "q1", "mean_sq", "root0", "q0", "neg_q0"))
+        gain_a, offset_b = per_half("gain_a"), per_half("offset_b")
+        neg_unit = tile("neg_unit", [P, SLOTS])
+        ay = [tile("ay%d" % c, [P, GROUPS, D, SLOTS]) for c in range(4)]
+        z_bf = [tile("z_bf%d" % c, [P, GROUPS, D, SLOTS], BF16) for c in range(4)]
         z_codes = [tile("z_codes%d" % c, [P, P], U32) for c in range(4)]
         z_sc = [tile("z_sc%d" % c, [P, P], U8) for c in range(4)]
-        res = [tile("res%d" % c, [P, P], F32) for c in range(4)]
+        res = [tile("res%d" % c, [P, P]) for c in range(4)]
         w2_codes = tile("w2_codes", [P, N], U32)
         w2_sc = tile("w2_sc", [P, N], U8)
 
-        def vt(x):
-            return x.rearrange("p (v t) -> p v t", t=4)
+        def by_slot(x):
+            return x.rearrange("p (v t) -> p v t", t=SLOTS)
 
-        def product(bank, words, scales, c, k=0):
-            for t in range(4):
+        def chunk_cols(c):
+            return slice(CHUNK_COLS * (c % 2), CHUNK_COLS * (c % 2 + 1))
+
+        def region(bank, r):
+            return bank[:, P * r : P * (r + 1)]
+
+        def members(bank):
+            return bank[:].rearrange("p (t v d) -> p d v t", t=SLOTS, d=D)
+
+        neg_unit_cols = neg_unit[:].unsqueeze(1).to_broadcast([P, 2 * GROUPS, SLOTS])
+
+        def cast_w1(copy, part, m0, m1):
+            first = part * (P // 2)
+            copy(w1_bf[:].rearrange("p t m j -> p m t j")[:, first + m0 : first + m1],
+                 w1_raw[part][:].rearrange("p j (m t) -> p m t j", t=SLOTS)[:, m0:m1])
+
+        def quantise_w1(t0):
+            nc.vector.quantize_mx(
+                out=w1_codes[:, t0 : t0 + 2, :].rearrange("p t m -> p (t m)").bitcast(FP8X4),
+                scales=w1_sc[:, t0 : t0 + 2, :].rearrange("p t m -> p (t m)"),
+                in_=w1_bf[:, t0 : t0 + 2].rearrange("p t m j -> p (t m j)"),
+            )
+
+        def gather_words(dst, win, a):
+            cols = HALF // 16
+            nc.vector.tensor_copy(dst[a][:], win[:].bitcast(U32).indirect(offsets[:, cols * a : cols * (a + 1)]))
+
+        def first_product(bank, codes, scales, plane, c):
+            for t in range(SLOTS):
                 nc.tensor.matmul_mx(
-                    out=bank[:, P * t : P * t + P],
+                    out=region(bank[c], t),
                     lhsT=w1_codes[:, t, :].bitcast(FP8X4), lhsT_scale=w1_sc[:, t, :],
-                    rhs=words[c // 2][:, P * (c % 2) : P * (c % 2) + P].bitcast(FP8X4), rhs_scale=scales[k:P, P * c : P * c + P],
+                    rhs=codes[c // 2][:, P * (c % 2) : P * (c % 2 + 1)].bitcast(FP8X4),
+                    rhs_scale=scales[plane:P, P * c : P * (c + 1)],
                     start=True, stop=True,
                 )
 
-        def mm_h(a):
-            product(hb[2 * a], ew, es, 2 * a)
-            product(hb[2 * a + 1], ew, es, 2 * a + 1)
-
-        def mm_y(c):
-            product(yb[c], xw, xs, c, 4)
-
-        def members(bank):
-            return bank[:].rearrange("p (t v d) -> p d v t", t=4, d=D)
-
-        def pivot(a, b):
-            nc.scalar.copy(vt(h8[a][:, 64 * b : 64 * b + 64]), members(hb[2 * a + b])[:, 0])
-
-        def deviate(a, b):
+        def deviate(dev, c):
+            cols = chunk_cols(c)
             nc.vector.tensor_tensor(
-                dev[a][:, :, 64 * b : 64 * b + 64].rearrange("p d (v t) -> p d v t", t=4),
-                members(hb[2 * a + b])[:, 1:D],
-                vt(h8[a][:, 64 * b : 64 * b + 64]).unsqueeze(1).to_broadcast([P, D - 1, 16, 4]),
+                dev[:, :, cols].rearrange("p d (v t) -> p d v t", t=SLOTS),
+                members(h_bank[c])[:, 1:D],
+                by_slot(h0[c // 2][:, cols]).unsqueeze(1).to_broadcast([P, D - 1, GROUPS, SLOTS]),
                 ALU.subtract,
             )
-            nc.scalar.activation(sq[a][:, :, 64 * b : 64 * b + 64], dev[a][:, :, 64 * b : 64 * b + 64], ACT.Square)
+            nc.scalar.activation(sq[c // 2][:, :, cols], dev[:, :, cols], ACT.Square)
 
-        def turn(dst, src, start, stop):
-            nc.tensor.matmul(dst, lhsT=src, rhs=ident[:], start=start, stop=stop, is_transpose=True)
+        def turned_sum(dst, parts):
+            for n, part in enumerate(parts):
+                nc.tensor.matmul(dst, lhsT=part, rhs=ident[:], start=(n == 0), stop=(n == len(parts) - 1), is_transpose=True)
 
-        def sum_t(dst, src):
-            for d in range(D - 1):
-                turn(dst, src[:, d, :], d == 0, d == D - 2)
+        def rows_of(x, count):
+            return [x[:, d, :] for d in range(count)]
 
-        def turn_pivot(a):
-            turn(hb[2 * a + 1][:, 2 * P : 3 * P], h8[a][:], True, True)
-            nc.scalar.activation(h8t[a][:], hb[2 * a + 1][:, 2 * P : 3 * P], ACT.Copy, scale=float(D))
+        def group_sums(dst, bank, c):
+            nc.vector.tensor_reduce(by_slot(dst[:, chunk_cols(c)]), bank[c][:].rearrange("p (t v d) -> p v t d", t=SLOTS, d=D), AX.X, ALU.add)
 
-        def sums(a):
-            bank_a, bank_b = hb[2 * a], hb[2 * a + 1]
-            turn_pivot(a)
-            sum_t(bank_a[:, 0:P], dev[a])
-            nc.scalar.activation(e1[a][:], bank_a[:, 0:P], ACT.Square, scale=1.0 / (D * math.sqrt(0.3)))
-            sum_t(bank_b[:, 0:P], sq[a])
+        def spread_gain(a, var, scale):
+            back = region(h_bank[2 * a + 1], 1)
+            nc.scalar.activation(root1[a][:], var, ACT.Abs_reciprocal_sqrt, bias=1.0, scale=scale)
+            nc.scalar.activation(q1[a][:], root1[a][:], ACT.Square)
+            turned_sum(back, [q1[a][:]])
+            nc.vector.scalar_tensor_tensor(out=by_slot(gain_a[a][:]), in0=by_slot(back), scalar=-1.0, in1=neg_unit_cols, op0=ALU.add, op1=ALU.mult)
 
-        s_h = tile("s_h", [P, P], F32)
-        s_dev = tile("s_dev", [P, P], F32)
-        neg_sq = tile("neg_sq", [P, P], F32)
+        def mean_gain(a, h_sum):
+            nc.scalar.activation(mean_sq[a][:], h_sum, ACT.Square, scale=1.0 / (D * math.sqrt(MEAN_NOISE)))
+            nc.scalar.activation(root0[a][:], mean_sq[a][:], ACT.Abs_reciprocal_sqrt, bias=1.0)
+            nc.scalar.activation(q0[a][:], root0[a][:], ACT.Square)
+            nc.scalar.activation(neg_q0[a][:], q0[a][:], ACT.Copy, scale=-1.0)
 
-        def sums_late():
-            for b in (0, 1):
-                nc.vector.tensor_reduce(vt(s_h[:, 64 * b : 64 * b + 64]), hb[2 + b][:].rearrange("p (t v d) -> p v t d", t=4, d=D), AX.X, ALU.add)
-            nc.vector.scalar_tensor_tensor(out=s_dev[:], in0=h8[1][:], scalar=-float(D), in1=s_h[:], op0=ALU.mult, op1=ALU.add)
-            nc.vector.scalar_tensor_tensor(out=neg_sq[:], in0=s_dev[:], scalar=-1.0 / D, in1=s_dev[:], op0=ALU.mult, op1=ALU.mult)
-            for d in range(D - 1):
-                turn(hb[3][:, 0:P], sq[1][:, d, :], d == 0, False)
-            turn(hb[3][:, 0:P], neg_sq[:], False, True)
-            turn(hb[2][:, 2 * P : 3 * P], s_h[:], True, True)
+        def q_diff(a):
+            return region(h_bank[2 * a], 1)
 
-        def gain_a(a):
-            bank_b = hb[2 * a + 1]
-            if a == 0:
-                nc.vector.scalar_tensor_tensor(out=x1[a][:], in0=bank_b[:, 0:P], scalar=1.0 / (D * 0.3), in1=e1[a][:], op0=ALU.mult, op1=ALU.subtract)
-                nc.scalar.activation(r1[a][:], x1[a][:], ACT.Abs_reciprocal_sqrt, bias=1.0)
-            else:
-                nc.scalar.activation(r1[a][:], bank_b[:, 0:P], ACT.Abs_reciprocal_sqrt, bias=1.0, scale=1.0 / (D * 0.3))
-            nc.scalar.activation(q1[a][:], r1[a][:], ACT.Square)
-            turn(bank_b[:, P : 2 * P], q1[a][:], True, True)
-            nc.vector.scalar_tensor_tensor(out=vt(a_g[a][:]), in0=vt(bank_b[:, P : 2 * P]), scalar=-1.0, in1=negu[:].unsqueeze(1).to_broadcast([P, 32, 4]), op0=ALU.add, op1=ALU.mult)
+        def per_member(g, c):
+            return by_slot(g[c // 2][:, chunk_cols(c)]).unsqueeze(2).to_broadcast([P, GROUPS, D, SLOTS])
 
-        def mean_gain(a):
-            if a == 0:
-                nc.vector.tensor_tensor(m8[a][:], hb[2 * a][:, 0:P], h8t[a][:], ALU.add)
-            nc.scalar.activation(x0[a][:], (m8[0][:], hb[2][:, 2 * P : 3 * P])[a], ACT.Square, scale=1.0 / (D * math.sqrt(0.2)))
-            nc.scalar.activation(r0[a][:], x0[a][:], ACT.Abs_reciprocal_sqrt, bias=1.0)
-            nc.scalar.activation(q0[a][:], r0[a][:], ACT.Square)
-            nc.scalar.activation(nq0[a][:], q0[a][:], ACT.Copy, scale=-1.0)
+        def times_a(c):
+            nc.vector.tensor_tensor(ay[c][:], y_bank[c][:].rearrange("p (t v d) -> p v d t", t=SLOTS, d=D), per_member(gain_a, c), ALU.mult)
 
-        def gain_diff(a):
-            turn(hb[2 * a][:, P : 2 * P], q1[a][:], True, False)
-            turn(hb[2 * a][:, P : 2 * P], nq0[a][:], False, True)
+        def plus_b(c):
+            nc.vector.tensor_tensor(z_bf[c][:], ay[c][:], per_member(offset_b, c), ALU.add)
 
-        def red_y(c):
-            nc.vector.tensor_reduce(vt(s_y[c // 2][:])[:, 16 * (c % 2) : 16 * (c % 2) + 16, :], yb[c][:].rearrange("p (t v d) -> p v t d", t=4, d=D), AX.X, ALU.add)
-
-        ys = tile("ys", [P, D, P], F32)
-        syt = tile("syt", [P, P], F32)
-
-        def sum_y_tensor():
-            for c in (2, 3):
-                nc.scalar.copy(ys[:, :, 64 * (c % 2) : 64 * (c % 2) + 64].rearrange("p d (v t) -> p d v t", t=4), members(yb[c]))
-            for d in range(D):
-                turn(hb[1][:, 0:P], ys[:, d, :], d == 0, d == D - 1)
-            nc.scalar.copy(syt[:], hb[1][:, 0:P])
-            turn(hb[1][:, P : 2 * P], syt[:], True, True)
-
-        def offset_b_late():
-            nc.vector.tensor_tensor(vt(umc[1][:]), vt(hb[2][:, P : 2 * P]), negu[:].unsqueeze(1).to_broadcast([P, 32, 4]), ALU.mult)
-            nc.vector.scalar_tensor_tensor(out=b_g[1][:], in0=hb[1][:, P : 2 * P], scalar=-1.0 / D, in1=umc[1][:], op0=ALU.mult, op1=ALU.mult)
-
-        def offset_b(a):
-            nc.gpsimd.tensor_tensor(vt(umc[a][:]), vt(s_y[a][:]), negu[:].unsqueeze(1).to_broadcast([P, 32, 4]), ALU.mult)
-            nc.vector.scalar_tensor_tensor(out=vt(b_g[a][:]), in0=vt(hb[2 * a][:, P : 2 * P]), scalar=-1.0 / D, in1=vt(umc[a][:]), op0=ALU.mult, op1=ALU.mult)
-
-        def per_group(g, c):
-            return vt(g[c // 2][:])[:, 16 * (c % 2) : 16 * (c % 2) + 16, :].unsqueeze(2).to_broadcast([P, 16, D, 4])
-
-        def mult_y(c):
-            nc.vector.tensor_tensor(u[c][:], yb[c][:].rearrange("p (t v d) -> p v d t", t=4, d=D), per_group(a_g, c), ALU.mult)
-
-        def add_b(c, eng=nc.vector):
-            eng.tensor_tensor(z_bf[c][:], u[c][:], per_group(b_g, c), ALU.add)
-
-        def finish(c):
+        def second_product(c):
             nc.vector.quantize_mx(out=z_codes[c][:].bitcast(FP8X4), scales=z_sc[c][:], in_=z_bf[c][:].rearrange("p v d t -> p (v d t)"))
-            nc.tensor.matmul_mx(out=yb[c][:, 0:P], lhsT=w2_codes[:].bitcast(FP8X4), lhsT_scale=w2_sc[:], rhs=z_codes[c][:].bitcast(FP8X4), rhs_scale=z_sc[c][:], start=True, stop=True)
-            nc.scalar.copy(res[c][:], yb[c][:, 0:P])
-            (nc.scalar if c == 3 else nc.sync).dma_start(out[:, P * c : P * c + P], res[c][:])
+            nc.tensor.matmul_mx(out=region(y_bank[c], 0), lhsT=w2_codes[:].bitcast(FP8X4), lhsT_scale=w2_sc[:],
+                                rhs=z_codes[c][:].bitcast(FP8X4), rhs_scale=z_sc[c][:], start=True, stop=True)
+            nc.scalar.copy(res[c][:], region(y_bank[c], 0))
+            (nc.scalar if c == 3 else nc.sync).dma_start(out[:, P * c : P * (c + 1)], res[c][:])
 
-
-        cast_w1("act", 0, 0, 64)
-        cast_w1("act", 1, 0, 32)
-        cast_w1("dve", 1, 32, 64)
-        quant_w1(0)
-        quant_w1(1)
-        nc.vector.tensor_copy(es[:], es_win[:].indirect(offsets[:]))
-        gather_words(ew, ew_win, 0)
-        mm_h(0)
-        gather_words(ew, ew_win, 1)
-        mm_h(1)
-        nc.vector.tensor_copy(xs[:], xs_win[:].indirect(offsets[:]))
-        nc.gpsimd.tensor_scalar(negu[:], unit_sb[:], -1.0, 0.0, ALU.mult, ALU.add)
+        cast_w1(nc.scalar.copy, 0, 0, P // 2)
+        cast_w1(nc.scalar.copy, 1, 0, SCALAR_SHARE)
+        cast_w1(nc.vector.tensor_copy, 1, SCALAR_SHARE, P // 2)
+        quantise_w1(0)
+        quantise_w1(2)
+        nc.vector.tensor_copy(e_sc[:], e_scale_win[:].indirect(offsets[:]))
         for a in range(2):
-            pivot(a, 0)
-            pivot(a, 1)
-        dev.append(sb.tile([P, D - 1, P], F32, name="dev0", tag="hold_s", align_bytes=64))
-        deviate(0, 0)
-        deviate(0, 1)
-        for a in (1, 0):
-            gather_words(xw, xw_win, a)
-        dev.append(reuse.tile([P, D - 1, P], F32, name="dev1", offset=0))
-        m8[0:1] = [reuse.tile([P, P], F32, name="m8_late", offset=4096)]
-        x1[0:1] = [reuse.tile([P, P], F32, name="x1_late", offset=4608)]
-        deviate(1, 0)
-        deviate(1, 1)
-        sums(0)
-        mean_gain(0)
-        gain_a(0)
-        gain_diff(0)
+            gather_words(e_codes, e_word_win, a)
+            first_product(h_bank, e_codes, e_sc, E_PLANE, 2 * a)
+            first_product(h_bank, e_codes, e_sc, E_PLANE, 2 * a + 1)
+        nc.vector.tensor_copy(x_sc[:], x_scale_win[:].indirect(offsets[:]))
+        nc.gpsimd.tensor_scalar(neg_unit[:], unit_sb[:], -1.0, 0.0, ALU.mult, ALU.add)
+        for c in range(4):
+            nc.scalar.copy(by_slot(h0[c // 2][:, chunk_cols(c)]), members(h_bank[c])[:, 0])
+
+        dev0 = sb.tile([P, D - 1, P], F32, name="dev0", tag="x_scale_bytes", align_bytes=64)
+        deviate(dev0, 0)
+        deviate(dev0, 1)
+        gather_words(x_codes, x_word_win, 1)
+        gather_words(x_codes, x_word_win, 0)
+        tile_bytes = 4 * P
+        dev1 = reuse.tile([P, D - 1, P], F32, name="dev1", offset=0)
+        h_sum0 = reuse.tile([P, P], F32, name="h_sum0", offset=D * tile_bytes)
+        var0 = reuse.tile([P, P], F32, name="var0", offset=(D + 1) * tile_bytes)
+        w2_bf = reuse.tile([P, N, SLOTS], BF16, name="w2_bf", offset=(D + 2) * tile_bytes)
+        deviate(dev1, 2)
+        deviate(dev1, 3)
+
+        h0_turned = tile("h0_turned", [P, P])
+        dev_sum_sq = tile("dev_sum_sq", [P, P])
+        dev_sum0, sq_sum0 = region(h_bank[0], 0), region(h_bank[1], 0)
+        turned_sum(region(h_bank[1], 2), [h0[0][:]])
+        nc.scalar.activation(h0_turned[:], region(h_bank[1], 2), ACT.Copy, scale=float(D))
+        turned_sum(dev_sum0, rows_of(dev0, D - 1))
+        nc.scalar.activation(dev_sum_sq[:], dev_sum0, ACT.Square, scale=1.0 / (D * math.sqrt(VAR_NOISE)))
+        turned_sum(sq_sum0, rows_of(sq[0], D - 1))
+        nc.vector.tensor_tensor(h_sum0[:], dev_sum0, h0_turned[:], ALU.add)
+        mean_gain(0, h_sum0[:])
+        nc.vector.scalar_tensor_tensor(out=var0[:], in0=sq_sum0, scalar=1.0 / (D * VAR_NOISE), in1=dev_sum_sq[:], op0=ALU.mult, op1=ALU.subtract)
+        spread_gain(0, var0[:], 1.0)
+        turned_sum(q_diff(0), [q1[0][:], neg_q0[0][:]])
+
         for c in (2, 3, 0, 1):
-            mm_y(c)
-        w2_bf = reuse.tile([P, N, 4], BF16, name="w2_bf", offset=5120)
+            first_product(y_bank, x_codes, x_sc, X_PLANE, c)
         nc.gpsimd.tensor_copy(w2_bf[:], w2_raw[:].rearrange("p j m -> p m j"))
-        sums_late()
-        gain_a(1)
-        mean_gain(1)
-        gain_diff(1)
+
+        h_sum1 = tile("h_sum1", [P, P])
+        dev_sum1 = tile("dev_sum1", [P, P])
+        neg_sq = tile("neg_sq", [P, P])
+        group_sums(h_sum1, h_bank, 2)
+        group_sums(h_sum1, h_bank, 3)
+        nc.vector.scalar_tensor_tensor(out=dev_sum1[:], in0=h0[1][:], scalar=-float(D), in1=h_sum1[:], op0=ALU.mult, op1=ALU.add)
+        nc.vector.scalar_tensor_tensor(out=neg_sq[:], in0=dev_sum1[:], scalar=-1.0 / D, in1=dev_sum1[:], op0=ALU.mult, op1=ALU.mult)
+        turned_sum(region(h_bank[3], 0), rows_of(sq[1], D - 1) + [neg_sq[:]])
+        turned_sum(region(h_bank[2], 2), [h_sum1[:]])
+        spread_gain(1, region(h_bank[3], 0), 1.0 / (D * VAR_NOISE))
+        mean_gain(1, region(h_bank[2], 2))
+        turned_sum(q_diff(1), [q1[1][:], neg_q0[1][:]])
         nc.vector.quantize_mx(out=w2_codes[:].bitcast(FP8X4), scales=w2_sc[:], in_=w2_bf[:].rearrange("p m j -> p (m j)"))
-        red_y(0)
-        red_y(1)
-        sum_y_tensor()
-        mult_y(0)
-        offset_b(0)
-        mult_y(1)
-        add_b(0)
-        add_b(1)
-        mult_y(2)
-        finish(0)
-        mult_y(3)
-        offset_b_late()
-        finish(1)
-        add_b(2)
-        add_b(3)
-        finish(2)
-        finish(3)
+
+        y_sum0 = tile("y_sum0", [P, P])
+        y_rows = tile("y_rows", [P, D, P])
+        y_sum_turned = tile("y_sum_turned", [P, P])
+        y_sum1 = region(h_bank[1], 1)
+        group_sums(y_sum0, y_bank, 0)
+        group_sums(y_sum0, y_bank, 1)
+        for c in (2, 3):
+            nc.scalar.copy(y_rows[:, :, chunk_cols(c)].rearrange("p d (v t) -> p d v t", t=SLOTS), members(y_bank[c]))
+        turned_sum(region(h_bank[1], 0), rows_of(y_rows, D))
+        nc.scalar.copy(y_sum_turned[:], region(h_bank[1], 0))
+        turned_sum(y_sum1, [y_sum_turned[:]])
+
+        unit_y_sum = tile("unit_y_sum", [P, P])
+        unit_q_diff = tile("unit_q_diff", [P, P])
+        times_a(0)
+        nc.gpsimd.tensor_tensor(by_slot(unit_y_sum[:]), by_slot(y_sum0[:]), neg_unit_cols, ALU.mult)
+        nc.vector.scalar_tensor_tensor(out=offset_b[0][:], in0=q_diff(0), scalar=-1.0 / D, in1=unit_y_sum[:], op0=ALU.mult, op1=ALU.mult)
+        times_a(1)
+        plus_b(0)
+        plus_b(1)
+        times_a(2)
+        second_product(0)
+        times_a(3)
+        nc.vector.tensor_tensor(by_slot(unit_q_diff[:]), by_slot(q_diff(1)), neg_unit_cols, ALU.mult)
+        nc.vector.scalar_tensor_tensor(out=offset_b[1][:], in0=y_sum1, scalar=-1.0 / D, in1=unit_q_diff[:], op0=ALU.mult, op1=ALU.mult)
+        second_product(1)
+        plus_b(2)
+        plus_b(3)
+        second_product(2)
+        second_product(3)

@@ -25,7 +25,7 @@ CHUNK_COLS = GROUPS * SLOTS
 HALF = 2 * P
 MEAN_NOISE, VAR_NOISE = 0.2, 0.3
 E_PLANE, X_PLANE = 0, 4
-SCALAR_SHARE = 32
+FIRST_ROWS = 4
 
 
 def tile_picked_ywien_wien_p_kernel(tc, x_words, x_scales, e_words, e_scales, w1, unit, w2, offs, out):
@@ -45,38 +45,47 @@ def tile_picked_ywien_wien_p_kernel(tc, x_words, x_scales, e_words, e_scales, w1
         h_bank = [ps.tile([P, SLOTS * P], F32, name="h_bank%d" % c) for c in range(4)]
         y_bank = [ps.tile([P, SLOTS * P], F32, name="y_bank%d" % c) for c in range(4)]
 
+        win_bytes = 4 * T
         e_scale_win = tile("e_scale_win", [P, T], U8)
-        x_scale_win = sb.tile([P, T], U8, name="x_scale_win", tag="x_scale_bytes", align_bytes=64)
-        e_word_win = tile("e_word_win", [P, T], I32)
-        x_word_win = reuse.tile([P, T], I32, name="x_word_win", offset=0, align_bytes=64)
+        x_scale_win = tile("x_scale_win", [P, T], U8)
+        e_word_win = reuse.tile([P, T], I32, name="e_word_win", offset=0, align_bytes=64)
+        x_word_win = reuse.tile([P, T], I32, name="x_word_win", offset=win_bytes, align_bytes=64)
         w1_raw = [tile("w1_raw%d" % part, [P, SLOTS, H // 2]) for part in range(2)]
         w2_raw = tile("w2_raw", [P, SLOTS, N])
         unit_sb = tile("unit_sb", [P, SLOTS])
         ident = tile("ident", [P, P])
         warm = tile("warm", [P, 1])
+        e_sc = tile("e_sc", [P, S], U8)
+        e_sc_picked = tile("e_sc_picked", [P, S], U8)
+        x_sc_picked = tile("x_sc_picked", [P, S], U8)
 
         nc.gpsimd.memset(e_scale_win[:].bitcast(I32), 0)
         nc.vector.memset(warm[:], 1.0)
         nc.vector.memset(x_scale_win[:].bitcast(I32), 0)
+        nc.gpsimd.memset(e_sc[:].bitcast(I32), 0)
+        nc.scalar.activation(warm[:], warm[:], ACT.Abs_reciprocal_sqrt)
+        make_identity(nc, ident[:])
 
         def load_scales(win, src, plane):
-            for q in range(4):
-                rows = slice(32 * q + plane, 32 * q + plane + 4)
-                nc.sync.dma_start(win[rows, :].bitcast(I32), src[0, 4 * q : 4 * q + 4, :].bitcast(I32))
+            nc.sync.dma_start(win[plane:P:8, :].bitcast(I32), src[0].bitcast(I32))
+
+        def place_scales(queue, dst, picked, plane, rows):
+            for r in rows:
+                queue.dma_start(dst[plane + r : P : 32, :].bitcast(I32), picked[plane + 8 * r : P : 32, :].bitcast(I32))
 
         def load_words(win, src):
             nc.sync.dma_start(win[:], src[0].rearrange("p n t -> p (n t)").bitcast(I32))
 
-        nc.scalar.activation(warm[:], warm[:], ACT.Abs_reciprocal_sqrt)
-        make_identity(nc, ident[:])
-
         w1_rows = w1.rearrange("(p j) c -> p j c", j=SLOTS)
         nc.sync.dma_start(w1_raw[0][:], w1_rows[:, :, 0 : H // 2])
-        load_scales(e_scale_win, e_scales, E_PLANE)
         nc.sync.dma_start(offsets[:], offs)
+        load_scales(e_scale_win, e_scales, E_PLANE)
+        load_scales(x_scale_win, x_scales, X_PLANE)
         nc.sync.dma_start(w1_raw[1][:], w1_rows[:, :, H // 2 : H])
         load_words(e_word_win, e_words)
-        load_scales(x_scale_win, x_scales, X_PLANE)
+        nc.vector.tensor_copy(e_sc_picked[:], e_scale_win[:].indirect(offsets[:]))
+        nc.vector.tensor_copy(x_sc_picked[:], x_scale_win[:].indirect(offsets[:]))
+        place_scales(nc.sync, e_sc, e_sc_picked, E_PLANE, range(4))
         load_words(x_word_win, x_words)
         nc.sync.dma_start(unit_sb[:], unit.rearrange("(p t) o -> p (t o)", t=SLOTS))
         nc.sync.dma_start(w2_raw[:], w2.rearrange("(p j) m -> p j m", j=SLOTS))
@@ -84,20 +93,21 @@ def tile_picked_ywien_wien_p_kernel(tc, x_words, x_scales, e_words, e_scales, w1
         w1_bf = tile("w1_bf", [P, SLOTS, P, SLOTS], BF16)
         w1_codes = tile("w1_codes", [P, SLOTS, P], U32)
         w1_sc = tile("w1_sc", [P, SLOTS, P], U8)
-        e_sc = tile("e_sc", [P, S], U8)
-        x_sc = tile("x_sc", [P, S], U8)
         e_codes = [tile("e_codes%d" % a, [P, HALF], U32) for a in range(2)]
         x_codes = [tile("x_codes%d" % a, [P, HALF], U32) for a in range(2)]
         h0 = per_half("h0")
         sq = [tile("sq%d" % a, [P, D - 1, P]) for a in range(2)]
-        root1, q1, mean_sq, root0, q0, neg_q0 = (per_half(nm) for nm in ("root1", "q1", "mean_sq", "root0", "q0", "neg_q0"))
-        gain_a, offset_b = per_half("gain_a"), per_half("offset_b")
+        h0_turned, dev_sum, dev_sum_sq, neg_sq_sum = (per_half(nm) for nm in ("h0_turned", "dev_sum", "dev_sum_sq", "neg_sq_sum"))
+        root1, q1, mean_sq, root0, q0, q_diff = (per_half(nm) for nm in ("root1", "q1", "mean_sq", "root0", "q0", "q_diff"))
+        offset_b = per_half("offset_b")
         neg_unit = tile("neg_unit", [P, SLOTS])
+        unit8 = tile("unit8", [P, SLOTS])
         ay = [tile("ay%d" % c, [P, GROUPS, D, SLOTS]) for c in range(4)]
         z_bf = [tile("z_bf%d" % c, [P, GROUPS, D, SLOTS], BF16) for c in range(4)]
         z_codes = [tile("z_codes%d" % c, [P, P], U32) for c in range(4)]
         z_sc = [tile("z_sc%d" % c, [P, P], U8) for c in range(4)]
         res = [tile("res%d" % c, [P, P]) for c in range(4)]
+        w2_bf = tile("w2_bf", [P, N, SLOTS], BF16)
         w2_codes = tile("w2_codes", [P, N], U32)
         w2_sc = tile("w2_sc", [P, N], U8)
 
@@ -113,12 +123,13 @@ def tile_picked_ywien_wien_p_kernel(tc, x_words, x_scales, e_words, e_scales, w1
         def members(bank):
             return bank[:].rearrange("p (t v d) -> p d v t", t=SLOTS, d=D)
 
-        neg_unit_cols = neg_unit[:].unsqueeze(1).to_broadcast([P, 2 * GROUPS, SLOTS])
+        def over_groups(x, groups):
+            return x[:].unsqueeze(1).to_broadcast([P, groups, SLOTS])
 
-        def cast_w1(copy, part, m0, m1):
+        def cast_w1(part):
             first = part * (P // 2)
-            copy(w1_bf[:].rearrange("p t m j -> p m t j")[:, first + m0 : first + m1],
-                 w1_raw[part][:].rearrange("p j (m t) -> p m t j", t=SLOTS)[:, m0:m1])
+            nc.scalar.copy(w1_bf[:].rearrange("p t m j -> p m t j")[:, first : first + P // 2],
+                           w1_raw[part][:].rearrange("p j (m t) -> p m t j", t=SLOTS))
 
         def quantise_w1(t0):
             nc.vector.quantize_mx(
@@ -141,15 +152,18 @@ def tile_picked_ywien_wien_p_kernel(tc, x_words, x_scales, e_words, e_scales, w1
                     start=True, stop=True,
                 )
 
-        def deviate(dev, c):
+        def deviate(dev, c, r0, r1):
             cols = chunk_cols(c)
             nc.vector.tensor_tensor(
-                dev[:, :, cols].rearrange("p d (v t) -> p d v t", t=SLOTS),
-                members(h_bank[c])[:, 1:D],
-                by_slot(h0[c // 2][:, cols]).unsqueeze(1).to_broadcast([P, D - 1, GROUPS, SLOTS]),
+                dev[:, r0:r1, cols].rearrange("p d (v t) -> p d v t", t=SLOTS),
+                members(h_bank[c])[:, 1 + r0 : 1 + r1],
+                by_slot(h0[c // 2][:, cols]).unsqueeze(1).to_broadcast([P, r1 - r0, GROUPS, SLOTS]),
                 ALU.subtract,
             )
-            nc.scalar.activation(sq[c // 2][:, :, cols], dev[:, :, cols], ACT.Square)
+
+        def square(dev, c, r0, r1):
+            cols = chunk_cols(c)
+            nc.scalar.activation(sq[c // 2][:, r0:r1, cols], dev[:, r0:r1, cols], ACT.Square)
 
         def turned_sum(dst, parts):
             for n, part in enumerate(parts):
@@ -158,24 +172,30 @@ def tile_picked_ywien_wien_p_kernel(tc, x_words, x_scales, e_words, e_scales, w1
         def rows_of(x, count):
             return [x[:, d, :] for d in range(count)]
 
-        def group_sums(dst, bank, c):
-            nc.vector.tensor_reduce(by_slot(dst[:, chunk_cols(c)]), bank[c][:].rearrange("p (t v d) -> p v t d", t=SLOTS, d=D), AX.X, ALU.add)
+        def pivots(a):
+            for c in (2 * a, 2 * a + 1):
+                nc.scalar.copy(by_slot(h0[a][:, chunk_cols(c)]), members(h_bank[c])[:, 0])
+            turned_sum(region(y_bank[3], a), [h0[a][:]])
+            nc.scalar.activation(h0_turned[a][:], region(y_bank[3], a), ACT.Copy, scale=float(D))
 
-        def spread_gain(a, var, scale):
-            back = region(h_bank[2 * a + 1], 1)
-            nc.scalar.activation(root1[a][:], var, ACT.Abs_reciprocal_sqrt, bias=1.0, scale=scale)
+        def gains(a, dev, gain):
+            lo, hi = h_bank[2 * a], h_bank[2 * a + 1]
+            turned_sum(region(lo, 0), rows_of(dev, D - 1))
+            turned_sum(region(hi, 0), rows_of(sq[a], D - 1))
+            nc.scalar.activation(dev_sum_sq[a][:], region(lo, 0), ACT.Square, scale=1.0 / (D * math.sqrt(VAR_NOISE)))
+            nc.scalar.activation(neg_sq_sum[a][:], region(hi, 0), ACT.Copy, scale=-1.0 / (D * VAR_NOISE))
+            turned_sum(region(hi, 1), [dev_sum_sq[a][:], neg_sq_sum[a][:]])
+            nc.scalar.activation(root1[a][:], region(hi, 1), ACT.Abs_reciprocal_sqrt, bias=1.0, scale=-1.0)
             nc.scalar.activation(q1[a][:], root1[a][:], ACT.Square)
-            turned_sum(back, [q1[a][:]])
-            nc.vector.scalar_tensor_tensor(out=by_slot(gain_a[a][:]), in0=by_slot(back), scalar=-1.0, in1=neg_unit_cols, op0=ALU.add, op1=ALU.mult)
-
-        def mean_gain(a, h_sum):
-            nc.scalar.activation(mean_sq[a][:], h_sum, ACT.Square, scale=1.0 / (D * math.sqrt(MEAN_NOISE)))
+            nc.scalar.copy(dev_sum[a][:], region(lo, 0))
+            turned_sum(region(lo, 1), [dev_sum[a][:], h0_turned[a][:]])
+            nc.scalar.activation(mean_sq[a][:], region(lo, 1), ACT.Square, scale=1.0 / (D * math.sqrt(MEAN_NOISE)))
             nc.scalar.activation(root0[a][:], mean_sq[a][:], ACT.Abs_reciprocal_sqrt, bias=1.0)
-            nc.scalar.activation(q0[a][:], root0[a][:], ACT.Square)
-            nc.scalar.activation(neg_q0[a][:], q0[a][:], ACT.Copy, scale=-1.0)
+            nc.gpsimd.tensor_tensor(q0[a][:], root0[a][:], root0[a][:], ALU.mult)
+            nc.gpsimd.tensor_tensor(q_diff[a][:], q1[a][:], q0[a][:], ALU.subtract)
 
-        def q_diff(a):
-            return region(h_bank[2 * a], 1)
+        def make_a(a, gain):
+            nc.vector.scalar_tensor_tensor(out=by_slot(gain[:]), in0=by_slot(q1[a][:]), scalar=-1.0, in1=over_groups(neg_unit, 2 * GROUPS), op0=ALU.add, op1=ALU.mult)
 
         def per_member(g, c):
             return by_slot(g[c // 2][:, chunk_cols(c)]).unsqueeze(2).to_broadcast([P, GROUPS, D, SLOTS])
@@ -193,92 +213,73 @@ def tile_picked_ywien_wien_p_kernel(tc, x_words, x_scales, e_words, e_scales, w1
             nc.scalar.copy(res[c][:], region(y_bank[c], 0))
             (nc.scalar if c == 3 else nc.sync).dma_start(out[:, P * c : P * (c + 1)], res[c][:])
 
-        cast_w1(nc.scalar.copy, 0, 0, P // 2)
-        cast_w1(nc.scalar.copy, 1, 0, SCALAR_SHARE)
-        cast_w1(nc.vector.tensor_copy, 1, SCALAR_SHARE, P // 2)
+        cast_w1(0)
+        cast_w1(1)
         quantise_w1(0)
         quantise_w1(2)
-        nc.vector.tensor_copy(e_sc[:], e_scale_win[:].indirect(offsets[:]))
         for a in range(2):
             gather_words(e_codes, e_word_win, a)
             first_product(h_bank, e_codes, e_sc, E_PLANE, 2 * a)
             first_product(h_bank, e_codes, e_sc, E_PLANE, 2 * a + 1)
-        nc.vector.tensor_copy(x_sc[:], x_scale_win[:].indirect(offsets[:]))
+        x_sc = reuse.tile([P, S], U8, name="x_sc", offset=0, align_bytes=64)
+        nc.vector.tensor_copy(x_sc[:].bitcast(I32), x_sc_picked[:].bitcast(I32))
+        place_scales(nc.scalar, x_sc, x_sc_picked, X_PLANE, range(1, 4))
         nc.gpsimd.tensor_scalar(neg_unit[:], unit_sb[:], -1.0, 0.0, ALU.mult, ALU.add)
-        for c in range(4):
-            nc.scalar.copy(by_slot(h0[c // 2][:, chunk_cols(c)]), members(h_bank[c])[:, 0])
+        nc.gpsimd.tensor_scalar(unit8[:], unit_sb[:], 1.0 / D, 0.0, ALU.mult, ALU.add)
 
-        dev0 = sb.tile([P, D - 1, P], F32, name="dev0", tag="x_scale_bytes", align_bytes=64)
-        deviate(dev0, 0)
-        deviate(dev0, 1)
-        gather_words(x_codes, x_word_win, 1)
+        dev0 = tile("dev0", [P, D - 1, P])
+        pivots(0)
+        deviate(dev0, 0, 0, D - 1)
+        deviate(dev0, 1, 0, FIRST_ROWS)
+        deviate(dev0, 1, FIRST_ROWS, D - 1)
+        square(dev0, 0, 0, D - 1)
+        square(dev0, 1, 0, FIRST_ROWS)
+        square(dev0, 1, FIRST_ROWS, D - 1)
+        pivots(1)
         gather_words(x_codes, x_word_win, 0)
-        tile_bytes = 4 * P
-        dev1 = reuse.tile([P, D - 1, P], F32, name="dev1", offset=0)
-        h_sum0 = reuse.tile([P, P], F32, name="h_sum0", offset=D * tile_bytes)
-        var0 = reuse.tile([P, P], F32, name="var0", offset=(D + 1) * tile_bytes)
-        w2_bf = reuse.tile([P, N, SLOTS], BF16, name="w2_bf", offset=(D + 2) * tile_bytes)
-        deviate(dev1, 2)
-        deviate(dev1, 3)
-
-        h0_turned = tile("h0_turned", [P, P])
-        dev_sum_sq = tile("dev_sum_sq", [P, P])
-        dev_sum0, sq_sum0 = region(h_bank[0], 0), region(h_bank[1], 0)
-        turned_sum(region(h_bank[1], 2), [h0[0][:]])
-        nc.scalar.activation(h0_turned[:], region(h_bank[1], 2), ACT.Copy, scale=float(D))
-        turned_sum(dev_sum0, rows_of(dev0, D - 1))
-        nc.scalar.activation(dev_sum_sq[:], dev_sum0, ACT.Square, scale=1.0 / (D * math.sqrt(VAR_NOISE)))
-        turned_sum(sq_sum0, rows_of(sq[0], D - 1))
-        nc.vector.tensor_tensor(h_sum0[:], dev_sum0, h0_turned[:], ALU.add)
-        mean_gain(0, h_sum0[:])
-        nc.vector.scalar_tensor_tensor(out=var0[:], in0=sq_sum0, scalar=1.0 / (D * VAR_NOISE), in1=dev_sum_sq[:], op0=ALU.mult, op1=ALU.subtract)
-        spread_gain(0, var0[:], 1.0)
-        turned_sum(q_diff(0), [q1[0][:], neg_q0[0][:]])
-
-        for c in (2, 3, 0, 1):
+        gather_words(x_codes, x_word_win, 1)
+        gains(0, dev0, None)
+        for c in range(4):
             first_product(y_bank, x_codes, x_sc, X_PLANE, c)
+        dev1 = reuse.tile([P, D - 1, P], F32, name="dev1", offset=win_bytes)
+        deviate(dev1, 2, 0, D - 1)
+        deviate(dev1, 3, 0, D - 1)
+
+        y_sum = [reuse.tile([P, CHUNK_COLS], F32, name="y_sum%d" % c, offset=1024 + 1024 * c) for c in range(2)]
+        unit_y_sum = tile("unit_y_sum", [P, P])
+        for c in range(2):
+            nc.vector.tensor_reduce(by_slot(y_sum[c][:]), y_bank[c][:].rearrange("p (t v d) -> p v t d", t=SLOTS, d=D), AX.X, ALU.add)
+            nc.gpsimd.tensor_tensor(by_slot(unit_y_sum[:, chunk_cols(c)]), by_slot(y_sum[c][:]), over_groups(unit8, GROUPS), ALU.mult)
+        nc.gpsimd.tensor_tensor(offset_b[0][:], q_diff[0][:], unit_y_sum[:], ALU.mult)
         nc.gpsimd.tensor_copy(w2_bf[:], w2_raw[:].rearrange("p j m -> p m j"))
+        gain_a = [reuse.tile([P, P], F32, name="gain_a0", offset=1024), tile("gain_a1", [P, P])]
+        make_a(0, gain_a[0])
 
-        h_sum1 = tile("h_sum1", [P, P])
-        dev_sum1 = tile("dev_sum1", [P, P])
-        neg_sq = tile("neg_sq", [P, P])
-        group_sums(h_sum1, h_bank, 2)
-        group_sums(h_sum1, h_bank, 3)
-        nc.vector.scalar_tensor_tensor(out=dev_sum1[:], in0=h0[1][:], scalar=-float(D), in1=h_sum1[:], op0=ALU.mult, op1=ALU.add)
-        nc.vector.scalar_tensor_tensor(out=neg_sq[:], in0=dev_sum1[:], scalar=-1.0 / D, in1=dev_sum1[:], op0=ALU.mult, op1=ALU.mult)
-        turned_sum(region(h_bank[3], 0), rows_of(sq[1], D - 1) + [neg_sq[:]])
-        turned_sum(region(h_bank[2], 2), [h_sum1[:]])
-        spread_gain(1, region(h_bank[3], 0), 1.0 / (D * VAR_NOISE))
-        mean_gain(1, region(h_bank[2], 2))
-        turned_sum(q_diff(1), [q1[1][:], neg_q0[1][:]])
-        nc.vector.quantize_mx(out=w2_codes[:].bitcast(FP8X4), scales=w2_sc[:], in_=w2_bf[:].rearrange("p m j -> p (m j)"))
-
-        y_sum0 = tile("y_sum0", [P, P])
+        square(dev1, 2, 0, D - 1)
+        square(dev1, 3, 0, D - 1)
+        gains(1, dev1, None)
         y_rows = tile("y_rows", [P, D, P])
         y_sum_turned = tile("y_sum_turned", [P, P])
-        y_sum1 = region(h_bank[1], 1)
-        group_sums(y_sum0, y_bank, 0)
-        group_sums(y_sum0, y_bank, 1)
+        unit_q_diff = tile("unit_q_diff", [P, P])
+        y_sum1 = region(h_bank[0], 3)
         for c in (2, 3):
             nc.scalar.copy(y_rows[:, :, chunk_cols(c)].rearrange("p d (v t) -> p d v t", t=SLOTS), members(y_bank[c]))
-        turned_sum(region(h_bank[1], 0), rows_of(y_rows, D))
-        nc.scalar.copy(y_sum_turned[:], region(h_bank[1], 0))
+        turned_sum(region(h_bank[1], 2), rows_of(y_rows, D))
+        nc.scalar.copy(y_sum_turned[:], region(h_bank[1], 2))
         turned_sum(y_sum1, [y_sum_turned[:]])
+        nc.gpsimd.tensor_tensor(by_slot(unit_q_diff[:]), by_slot(q_diff[1][:]), over_groups(unit8, 2 * GROUPS), ALU.mult)
 
-        unit_y_sum = tile("unit_y_sum", [P, P])
-        unit_q_diff = tile("unit_q_diff", [P, P])
         times_a(0)
-        nc.gpsimd.tensor_tensor(by_slot(unit_y_sum[:]), by_slot(y_sum0[:]), neg_unit_cols, ALU.mult)
-        nc.vector.scalar_tensor_tensor(out=offset_b[0][:], in0=q_diff(0), scalar=-1.0 / D, in1=unit_y_sum[:], op0=ALU.mult, op1=ALU.mult)
         times_a(1)
+        nc.vector.quantize_mx(out=w2_codes[:].bitcast(FP8X4), scales=w2_sc[:], in_=w2_bf[:].rearrange("p m j -> p (m j)"))
         plus_b(0)
         plus_b(1)
-        times_a(2)
+        make_a(1, gain_a[1])
         second_product(0)
-        times_a(3)
-        nc.vector.tensor_tensor(by_slot(unit_q_diff[:]), by_slot(q_diff(1)), neg_unit_cols, ALU.mult)
-        nc.vector.scalar_tensor_tensor(out=offset_b[1][:], in0=y_sum1, scalar=-1.0 / D, in1=unit_q_diff[:], op0=ALU.mult, op1=ALU.mult)
+        times_a(2)
         second_product(1)
+        times_a(3)
+        nc.vector.tensor_tensor(offset_b[1][:], y_sum1, unit_q_diff[:], ALU.mult)
         plus_b(2)
         plus_b(3)
         second_product(2)

@@ -57,12 +57,14 @@ def tile_picked_ywien_wien_p_kernel(tc, x_words, x_scales, e_words, e_scales, w1
         warm = tile("warm", [P, 1])
         e_sc = tile("e_sc", [P, S], U8)
         e_sc_picked = tile("e_sc_picked", [P, S], U8)
+        x_sc = tile("x_sc", [P, S], U8)
         x_sc_picked = tile("x_sc_picked", [P, S], U8)
 
         nc.gpsimd.memset(e_scale_win[:].bitcast(I32), 0)
         nc.vector.memset(warm[:], 1.0)
         nc.vector.memset(x_scale_win[:].bitcast(I32), 0)
         nc.gpsimd.memset(e_sc[:].bitcast(I32), 0)
+        nc.gpsimd.memset(x_sc[:].bitcast(I32), 0)
         nc.scalar.activation(warm[:], warm[:], ACT.Abs_reciprocal_sqrt)
         make_identity(nc, ident[:])
 
@@ -85,27 +87,30 @@ def tile_picked_ywien_wien_p_kernel(tc, x_words, x_scales, e_words, e_scales, w1
         load_words(e_word_win, e_words)
         nc.vector.tensor_copy(e_sc_picked[:], e_scale_win[:].indirect(offsets[:]))
         nc.vector.tensor_copy(x_sc_picked[:], x_scale_win[:].indirect(offsets[:]))
+        nc.sync.dma_start(w2_raw[:], w2.rearrange("(p j) m -> p j m", j=SLOTS))
         place_scales(nc.sync, e_sc, e_sc_picked, E_PLANE, range(4))
         load_words(x_word_win, x_words)
+        place_scales(nc.sync, x_sc, x_sc_picked, X_PLANE, range(4))
         nc.sync.dma_start(unit_sb[:], unit.rearrange("(p t) o -> p (t o)", t=SLOTS))
-        nc.sync.dma_start(w2_raw[:], w2.rearrange("(p j) m -> p j m", j=SLOTS))
 
         w1_bf = tile("w1_bf", [P, SLOTS, P, SLOTS], BF16)
         w1_codes = tile("w1_codes", [P, SLOTS, P], U32)
         w1_sc = tile("w1_sc", [P, SLOTS, P], U8)
         e_codes = [tile("e_codes%d" % a, [P, HALF], U32) for a in range(2)]
+        h0 = [reuse.tile([P, P], F32, name="h00", offset=2 * win_bytes), tile("h01", [P, P])]
         x_codes = [tile("x_codes%d" % a, [P, HALF], U32) for a in range(2)]
-        h0 = per_half("h0")
-        sq = [tile("sq%d" % a, [P, D - 1, P]) for a in range(2)]
-        h0_turned, dev_sum, dev_sum_sq, neg_sq_sum = (per_half(nm) for nm in ("h0_turned", "dev_sum", "dev_sum_sq", "neg_sq_sum"))
-        root1, q1, mean_sq, root0, q0, q_diff = (per_half(nm) for nm in ("root1", "q1", "mean_sq", "root0", "q0", "q_diff"))
+        sq = [tile("sq0", [P, D - 1, P]), None]
+        h0_turned, dev_sum, dev_sum_sq = (per_half(nm) for nm in ("h0_turned", "dev_sum", "dev_sum_sq"))
+        neg_sq_sum = per_half("neg_sq_sum")
+        root1, q1, mean_sq, root0, q_diff = (per_half(nm) for nm in ("root1", "q1", "mean_sq", "root0", "q_diff"))
+        q0 = [tile("q00", [P, P]), reuse.tile([P, P], F32, name="q01", offset=3 * win_bytes + 1024)]
         offset_b = per_half("offset_b")
-        neg_unit = tile("neg_unit", [P, SLOTS])
+        neg_unit = reuse.tile([P, SLOTS], F32, name="neg_unit", offset=3 * win_bytes)
         unit8 = tile("unit8", [P, SLOTS])
         ay = [tile("ay%d" % c, [P, GROUPS, D, SLOTS]) for c in range(4)]
         z_bf = [tile("z_bf%d" % c, [P, GROUPS, D, SLOTS], BF16) for c in range(4)]
         z_codes = [tile("z_codes%d" % c, [P, P], U32) for c in range(4)]
-        z_sc = [tile("z_sc%d" % c, [P, P], U8) for c in range(4)]
+        z_sc = [None, None] + [tile("z_sc%d" % c, [P, P], U8) for c in (2, 3)]
         res = [tile("res%d" % c, [P, P]) for c in range(4)]
         w2_bf = tile("w2_bf", [P, N, SLOTS], BF16)
         w2_codes = tile("w2_codes", [P, N], U32)
@@ -172,27 +177,33 @@ def tile_picked_ywien_wien_p_kernel(tc, x_words, x_scales, e_words, e_scales, w1
         def rows_of(x, count):
             return [x[:, d, :] for d in range(count)]
 
-        def pivots(a):
-            for c in (2 * a, 2 * a + 1):
-                nc.scalar.copy(by_slot(h0[a][:, chunk_cols(c)]), members(h_bank[c])[:, 0])
-            turned_sum(region(y_bank[3], a), [h0[a][:]])
-            nc.scalar.activation(h0_turned[a][:], region(y_bank[3], a), ACT.Copy, scale=float(D))
+        def pivot(copy, c):
+            copy(by_slot(h0[c // 2][:, chunk_cols(c)]), members(h_bank[c])[:, 0])
 
-        def gains(a, dev, gain):
+        def turn_pivots(a):
+            turned_sum(region(h_bank[a], 2), [h0[a][:]])
+            nc.scalar.activation(h0_turned[a][:], region(h_bank[a], 2), ACT.Copy, scale=float(D))
+
+        def sums(a, dev):
             lo, hi = h_bank[2 * a], h_bank[2 * a + 1]
-            turned_sum(region(lo, 0), rows_of(dev, D - 1))
+            turned_sum(region(lo, 0), dev)
             turned_sum(region(hi, 0), rows_of(sq[a], D - 1))
             nc.scalar.activation(dev_sum_sq[a][:], region(lo, 0), ACT.Square, scale=1.0 / (D * math.sqrt(VAR_NOISE)))
+            nc.scalar.copy(dev_sum[a][:], region(lo, 0))
             nc.scalar.activation(neg_sq_sum[a][:], region(hi, 0), ACT.Copy, scale=-1.0 / (D * VAR_NOISE))
+
+        def spread_gain(a):
+            hi = h_bank[2 * a + 1]
             turned_sum(region(hi, 1), [dev_sum_sq[a][:], neg_sq_sum[a][:]])
             nc.scalar.activation(root1[a][:], region(hi, 1), ACT.Abs_reciprocal_sqrt, bias=1.0, scale=-1.0)
             nc.scalar.activation(q1[a][:], root1[a][:], ACT.Square)
-            nc.scalar.copy(dev_sum[a][:], region(lo, 0))
+
+        def mean_gain(a):
+            lo = h_bank[2 * a]
             turned_sum(region(lo, 1), [dev_sum[a][:], h0_turned[a][:]])
             nc.scalar.activation(mean_sq[a][:], region(lo, 1), ACT.Square, scale=1.0 / (D * math.sqrt(MEAN_NOISE)))
             nc.scalar.activation(root0[a][:], mean_sq[a][:], ACT.Abs_reciprocal_sqrt, bias=1.0)
-            nc.gpsimd.tensor_tensor(q0[a][:], root0[a][:], root0[a][:], ALU.mult)
-            nc.gpsimd.tensor_tensor(q_diff[a][:], q1[a][:], q0[a][:], ALU.subtract)
+            nc.scalar.activation(q0[a][:], root0[a][:], ACT.Square)
 
         def make_a(a, gain):
             nc.vector.scalar_tensor_tensor(out=by_slot(gain[:]), in0=by_slot(q1[a][:]), scalar=-1.0, in1=over_groups(neg_unit, 2 * GROUPS), op0=ALU.add, op1=ALU.mult)
@@ -221,65 +232,75 @@ def tile_picked_ywien_wien_p_kernel(tc, x_words, x_scales, e_words, e_scales, w1
             gather_words(e_codes, e_word_win, a)
             first_product(h_bank, e_codes, e_sc, E_PLANE, 2 * a)
             first_product(h_bank, e_codes, e_sc, E_PLANE, 2 * a + 1)
-        x_sc = reuse.tile([P, S], U8, name="x_sc", offset=0, align_bytes=64)
-        nc.vector.tensor_copy(x_sc[:].bitcast(I32), x_sc_picked[:].bitcast(I32))
-        place_scales(nc.scalar, x_sc, x_sc_picked, X_PLANE, range(1, 4))
         nc.gpsimd.tensor_scalar(neg_unit[:], unit_sb[:], -1.0, 0.0, ALU.mult, ALU.add)
         nc.gpsimd.tensor_scalar(unit8[:], unit_sb[:], 1.0 / D, 0.0, ALU.mult, ALU.add)
 
         dev0 = tile("dev0", [P, D - 1, P])
-        pivots(0)
-        deviate(dev0, 0, 0, D - 1)
-        deviate(dev0, 1, 0, FIRST_ROWS)
-        deviate(dev0, 1, FIRST_ROWS, D - 1)
-        square(dev0, 0, 0, D - 1)
-        square(dev0, 1, 0, FIRST_ROWS)
-        square(dev0, 1, FIRST_ROWS, D - 1)
-        pivots(1)
-        gather_words(x_codes, x_word_win, 0)
-        gather_words(x_codes, x_word_win, 1)
-        gains(0, dev0, None)
-        for c in range(4):
+        dev1 = tile("dev1", [P, D - 1, P])
+        y_sum, unit_y_sum, gain_a = per_half("y_sum"), per_half("unit_y_sum"), per_half("gain_a")
+
+        def sum_y(c):
+            nc.vector.tensor_reduce(by_slot(y_sum[c // 2][:, chunk_cols(c)]), y_bank[c][:].rearrange("p (t v d) -> p v t d", t=SLOTS, d=D), AX.X, ALU.add)
+
+        def scale_y_sum(a):
+            nc.gpsimd.tensor_tensor(by_slot(unit_y_sum[a][:]), by_slot(y_sum[a][:]), over_groups(unit8, 2 * GROUPS), ALU.mult)
+
+        def make_b(a):
+            nc.gpsimd.tensor_tensor(q_diff[a][:], q1[a][:], q0[a][:], ALU.subtract)
+            nc.gpsimd.tensor_tensor(offset_b[a][:], q_diff[a][:], unit_y_sum[a][:], ALU.mult)
+
+        def y_product(c):
             first_product(y_bank, x_codes, x_sc, X_PLANE, c)
-        dev1 = reuse.tile([P, D - 1, P], F32, name="dev1", offset=win_bytes)
+
+        nc.gpsimd.tensor_copy(w2_bf[:], w2_raw[:].rearrange("p j m -> p m j"))
+        nc.vector.quantize_mx(out=w2_codes[:].bitcast(FP8X4), scales=w2_sc[:], in_=w2_bf[:].rearrange("p m j -> p (m j)"))
+        pivot(nc.scalar.copy, 0)
+        pivot(nc.scalar.copy, 1)
+        deviate(dev0, 0, 0, D - 1)
+        deviate(dev0, 1, 0, D - 1)
+        square(dev0, 0, 0, D - 1)
+        square(dev0, 1, 0, D - 1)
+        pivot(nc.vector.tensor_copy, 2)
+        pivot(nc.vector.tensor_copy, 3)
+        gather_words(x_codes, x_word_win, 0)
         deviate(dev1, 2, 0, D - 1)
         deviate(dev1, 3, 0, D - 1)
-
-        y_sum = [reuse.tile([P, CHUNK_COLS], F32, name="y_sum%d" % c, offset=1024 + 1024 * c) for c in range(2)]
-        unit_y_sum = tile("unit_y_sum", [P, P])
-        for c in range(2):
-            nc.vector.tensor_reduce(by_slot(y_sum[c][:]), y_bank[c][:].rearrange("p (t v d) -> p v t d", t=SLOTS, d=D), AX.X, ALU.add)
-            nc.gpsimd.tensor_tensor(by_slot(unit_y_sum[:, chunk_cols(c)]), by_slot(y_sum[c][:]), over_groups(unit8, GROUPS), ALU.mult)
-        nc.gpsimd.tensor_tensor(offset_b[0][:], q_diff[0][:], unit_y_sum[:], ALU.mult)
-        nc.gpsimd.tensor_copy(w2_bf[:], w2_raw[:].rearrange("p j m -> p m j"))
-        gain_a = [reuse.tile([P, P], F32, name="gain_a0", offset=1024), tile("gain_a1", [P, P])]
-        make_a(0, gain_a[0])
-
+        gather_words(x_codes, x_word_win, 1)
+        sums(0, rows_of(dev0, D - 1))
+        turn_pivots(0)
+        y_product(0)
+        y_product(1)
+        spread_gain(0)
+        mean_gain(0)
+        sq[1] = reuse.tile([P, D - 1, P], F32, name="sq1", offset=2 * win_bytes)
         square(dev1, 2, 0, D - 1)
         square(dev1, 3, 0, D - 1)
-        gains(1, dev1, None)
-        y_rows = tile("y_rows", [P, D, P])
-        y_sum_turned = tile("y_sum_turned", [P, P])
-        unit_q_diff = tile("unit_q_diff", [P, P])
-        y_sum1 = region(h_bank[0], 3)
-        for c in (2, 3):
-            nc.scalar.copy(y_rows[:, :, chunk_cols(c)].rearrange("p d (v t) -> p d v t", t=SLOTS), members(y_bank[c]))
-        turned_sum(region(h_bank[1], 2), rows_of(y_rows, D))
-        nc.scalar.copy(y_sum_turned[:], region(h_bank[1], 2))
-        turned_sum(y_sum1, [y_sum_turned[:]])
-        nc.gpsimd.tensor_tensor(by_slot(unit_q_diff[:]), by_slot(q_diff[1][:]), over_groups(unit8, 2 * GROUPS), ALU.mult)
-
+        y_product(2)
+        y_product(3)
+        sum_y(0)
+        sum_y(1)
+        scale_y_sum(0)
+        make_a(0, gain_a[0])
+        make_b(0)
+        turn_pivots(1)
+        sums(1, rows_of(dev1, D - 1))
+        mean_gain(1)
+        spread_gain(1)
+        sum_y(2)
         times_a(0)
+        sum_y(3)
+        scale_y_sum(1)
         times_a(1)
-        nc.vector.quantize_mx(out=w2_codes[:].bitcast(FP8X4), scales=w2_sc[:], in_=w2_bf[:].rearrange("p m j -> p (m j)"))
         plus_b(0)
         plus_b(1)
         make_a(1, gain_a[1])
+        make_b(1)
+        z_sc[0] = reuse.tile([P, P], U8, name="z_sc0", offset=3 * win_bytes, align_bytes=64)
+        z_sc[1] = reuse.tile([P, P], U8, name="z_sc1", offset=3 * win_bytes + 1024, align_bytes=64)
         second_product(0)
         times_a(2)
         second_product(1)
         times_a(3)
-        nc.vector.tensor_tensor(offset_b[1][:], y_sum1, unit_q_diff[:], ALU.mult)
         plus_b(2)
         plus_b(3)
         second_product(2)

@@ -25,7 +25,7 @@ CHUNK_COLS = GROUPS * SLOTS
 HALF = 2 * P
 MEAN_NOISE, VAR_NOISE = 0.2, 0.3
 E_PLANE, X_PLANE = 0, 4
-FIRST_ROWS = 4
+W1_PARTS = (0, 48, 96, 128)
 
 
 def tile_picked_ywien_wien_p_kernel(tc, x_words, x_scales, e_words, e_scales, w1, unit, w2, offs, out):
@@ -50,7 +50,7 @@ def tile_picked_ywien_wien_p_kernel(tc, x_words, x_scales, e_words, e_scales, w1
         x_scale_win = tile("x_scale_win", [P, T], U8)
         e_word_win = reuse.tile([P, T], I32, name="e_word_win", offset=0, align_bytes=64)
         x_word_win = reuse.tile([P, T], I32, name="x_word_win", offset=win_bytes, align_bytes=64)
-        w1_raw = [tile("w1_raw%d" % part, [P, SLOTS, H // 2]) for part in range(2)]
+        w1_raw = [tile("w1_raw%d" % part, [P, SLOTS, SLOTS * (W1_PARTS[part + 1] - W1_PARTS[part])]) for part in range(3)]
         w2_raw = tile("w2_raw", [P, SLOTS, N])
         unit_sb = tile("unit_sb", [P, SLOTS])
         ident = tile("ident", [P, P])
@@ -67,6 +67,11 @@ def tile_picked_ywien_wien_p_kernel(tc, x_words, x_scales, e_words, e_scales, w1
         nc.gpsimd.memset(x_sc[:].bitcast(I32), 0)
         nc.scalar.activation(warm[:], warm[:], ACT.Abs_reciprocal_sqrt)
         make_identity(nc, ident[:])
+        neg_scale = [reuse.tile([P, 1], F32, name="neg_scale0", offset=2 * win_bytes + 1024), tile("neg_scale1", [P, 1])]
+        one = tile("one", [P, 1])
+        nc.gpsimd.memset(one[:], 1.0)
+        for a in range(2):
+            nc.gpsimd.tensor_scalar(neg_scale[a][:], one[:], -1.0 / (D * VAR_NOISE), 0.0, ALU.mult, ALU.add)
 
         def load_scales(win, src, plane):
             nc.sync.dma_start(win[plane:P:8, :].bitcast(I32), src[0].bitcast(I32))
@@ -79,11 +84,16 @@ def tile_picked_ywien_wien_p_kernel(tc, x_words, x_scales, e_words, e_scales, w1
             nc.sync.dma_start(win[:], src[0].rearrange("p n t -> p (n t)").bitcast(I32))
 
         w1_rows = w1.rearrange("(p j) c -> p j c", j=SLOTS)
-        nc.sync.dma_start(w1_raw[0][:], w1_rows[:, :, 0 : H // 2])
+
+        def load_w1(part):
+            nc.sync.dma_start(w1_raw[part][:], w1_rows[:, :, SLOTS * W1_PARTS[part] : SLOTS * W1_PARTS[part + 1]])
+
+        load_w1(0)
         nc.sync.dma_start(offsets[:], offs)
         load_scales(e_scale_win, e_scales, E_PLANE)
         load_scales(x_scale_win, x_scales, X_PLANE)
-        nc.sync.dma_start(w1_raw[1][:], w1_rows[:, :, H // 2 : H])
+        load_w1(1)
+        load_w1(2)
         load_words(e_word_win, e_words)
         nc.vector.tensor_copy(e_sc_picked[:], e_scale_win[:].indirect(offsets[:]))
         nc.vector.tensor_copy(x_sc_picked[:], x_scale_win[:].indirect(offsets[:]))
@@ -97,20 +107,22 @@ def tile_picked_ywien_wien_p_kernel(tc, x_words, x_scales, e_words, e_scales, w1
         w1_codes = tile("w1_codes", [P, SLOTS, P], U32)
         w1_sc = tile("w1_sc", [P, SLOTS, P], U8)
         e_codes = [tile("e_codes%d" % a, [P, HALF], U32) for a in range(2)]
-        h0 = [reuse.tile([P, P], F32, name="h00", offset=2 * win_bytes), tile("h01", [P, P])]
+        h0 = per_half("h0")
         x_codes = [tile("x_codes%d" % a, [P, HALF], U32) for a in range(2)]
         sq = [tile("sq0", [P, D - 1, P]), None]
         h0_turned, dev_sum, dev_sum_sq = (per_half(nm) for nm in ("h0_turned", "dev_sum", "dev_sum_sq"))
         neg_sq_sum = per_half("neg_sq_sum")
         root1, q1, mean_sq, root0, q_diff = (per_half(nm) for nm in ("root1", "q1", "mean_sq", "root0", "q_diff"))
-        q0 = [tile("q00", [P, P]), reuse.tile([P, P], F32, name="q01", offset=3 * win_bytes + 1024)]
+        q0 = per_half("q0")
+        q_diff[0] = reuse.tile([P, P], F32, name="q_diff_first", offset=2 * win_bytes)
+        root1[1] = reuse.tile([P, P], F32, name="root1_last", offset=3 * win_bytes)
         offset_b = per_half("offset_b")
-        neg_unit = reuse.tile([P, SLOTS], F32, name="neg_unit", offset=3 * win_bytes)
+        neg_unit = tile("neg_unit", [P, SLOTS])
         unit8 = tile("unit8", [P, SLOTS])
         ay = [tile("ay%d" % c, [P, GROUPS, D, SLOTS]) for c in range(4)]
         z_bf = [tile("z_bf%d" % c, [P, GROUPS, D, SLOTS], BF16) for c in range(4)]
         z_codes = [tile("z_codes%d" % c, [P, P], U32) for c in range(4)]
-        z_sc = [None, None] + [tile("z_sc%d" % c, [P, P], U8) for c in (2, 3)]
+        z_sc = [tile("z_sc%d" % c, [P, P], U8) if c != 1 else None for c in range(4)]
         res = [tile("res%d" % c, [P, P]) for c in range(4)]
         w2_bf = tile("w2_bf", [P, N, SLOTS], BF16)
         w2_codes = tile("w2_codes", [P, N], U32)
@@ -132,8 +144,7 @@ def tile_picked_ywien_wien_p_kernel(tc, x_words, x_scales, e_words, e_scales, w1
             return x[:].unsqueeze(1).to_broadcast([P, groups, SLOTS])
 
         def cast_w1(part):
-            first = part * (P // 2)
-            nc.scalar.copy(w1_bf[:].rearrange("p t m j -> p m t j")[:, first : first + P // 2],
+            nc.scalar.copy(w1_bf[:].rearrange("p t m j -> p m t j")[:, W1_PARTS[part] : W1_PARTS[part + 1]],
                            w1_raw[part][:].rearrange("p j (m t) -> p m t j", t=SLOTS))
 
         def quantise_w1(t0):
@@ -181,8 +192,8 @@ def tile_picked_ywien_wien_p_kernel(tc, x_words, x_scales, e_words, e_scales, w1
             copy(by_slot(h0[c // 2][:, chunk_cols(c)]), members(h_bank[c])[:, 0])
 
         def turn_pivots(a):
-            turned_sum(region(h_bank[a], 2), [h0[a][:]])
-            nc.scalar.activation(h0_turned[a][:], region(h_bank[a], 2), ACT.Copy, scale=float(D))
+            turned_sum(region(y_bank[2 + a], 0), [h0[a][:]])
+            nc.scalar.activation(h0_turned[a][:], region(y_bank[2 + a], 0), ACT.Copy, scale=float(D))
 
         def sums(a, dev):
             lo, hi = h_bank[2 * a], h_bank[2 * a + 1]
@@ -190,18 +201,16 @@ def tile_picked_ywien_wien_p_kernel(tc, x_words, x_scales, e_words, e_scales, w1
             turned_sum(region(hi, 0), rows_of(sq[a], D - 1))
             nc.scalar.activation(dev_sum_sq[a][:], region(lo, 0), ACT.Square, scale=1.0 / (D * math.sqrt(VAR_NOISE)))
             nc.scalar.copy(dev_sum[a][:], region(lo, 0))
-            nc.scalar.activation(neg_sq_sum[a][:], region(hi, 0), ACT.Copy, scale=-1.0 / (D * VAR_NOISE))
+            nc.scalar.activation(neg_sq_sum[a][:], region(hi, 0), ACT.Copy, scale=neg_scale[a][:])
 
-        def spread_gain(a):
-            hi = h_bank[2 * a + 1]
-            turned_sum(region(hi, 1), [dev_sum_sq[a][:], neg_sq_sum[a][:]])
-            nc.scalar.activation(root1[a][:], region(hi, 1), ACT.Abs_reciprocal_sqrt, bias=1.0, scale=-1.0)
+        def gains(a):
+            mean, spread = region(h_bank[2 * a], 1), region(h_bank[2 * a + 1], 1)
+            for first, (for_spread, for_mean) in ((True, (dev_sum_sq, h0_turned)), (False, (neg_sq_sum, dev_sum))):
+                nc.tensor.matmul(spread, lhsT=for_spread[a][:], rhs=ident[:], start=first, stop=not first, is_transpose=True)
+                nc.tensor.matmul(mean, lhsT=for_mean[a][:], rhs=ident[:], start=first, stop=not first, is_transpose=True)
+            nc.scalar.activation(root1[a][:], spread, ACT.Abs_reciprocal_sqrt, bias=1.0, scale=-1.0)
+            nc.scalar.activation(mean_sq[a][:], mean, ACT.Square, scale=1.0 / (D * math.sqrt(MEAN_NOISE)))
             nc.scalar.activation(q1[a][:], root1[a][:], ACT.Square)
-
-        def mean_gain(a):
-            lo = h_bank[2 * a]
-            turned_sum(region(lo, 1), [dev_sum[a][:], h0_turned[a][:]])
-            nc.scalar.activation(mean_sq[a][:], region(lo, 1), ACT.Square, scale=1.0 / (D * math.sqrt(MEAN_NOISE)))
             nc.scalar.activation(root0[a][:], mean_sq[a][:], ACT.Abs_reciprocal_sqrt, bias=1.0)
             nc.scalar.activation(q0[a][:], root0[a][:], ACT.Square)
 
@@ -219,15 +228,20 @@ def tile_picked_ywien_wien_p_kernel(tc, x_words, x_scales, e_words, e_scales, w1
 
         def second_product(c):
             nc.vector.quantize_mx(out=z_codes[c][:].bitcast(FP8X4), scales=z_sc[c][:], in_=z_bf[c][:].rearrange("p v d t -> p (v d t)"))
-            nc.tensor.matmul_mx(out=region(y_bank[c], 0), lhsT=w2_codes[:].bitcast(FP8X4), lhsT_scale=w2_sc[:],
+            acc = region(h_bank[3 - c], 3) if c < 2 else region(y_bank[c], 0)
+            nc.tensor.matmul_mx(out=acc, lhsT=w2_codes[:].bitcast(FP8X4), lhsT_scale=w2_sc[:],
                                 rhs=z_codes[c][:].bitcast(FP8X4), rhs_scale=z_sc[c][:], start=True, stop=True)
-            nc.scalar.copy(res[c][:], region(y_bank[c], 0))
+            nc.scalar.copy(res[c][:], acc)
             (nc.scalar if c == 3 else nc.sync).dma_start(out[:, P * c : P * (c + 1)], res[c][:])
 
-        cast_w1(0)
-        cast_w1(1)
+        for part in range(3):
+            cast_w1(part)
         quantise_w1(0)
         quantise_w1(2)
+        for n in range(4):
+            nc.tensor.matmul_mx(out=y_bank[2 + n // 2][:, HALF * (n % 2) : HALF * (n % 2 + 1)], lhsT=w1_codes[:, 0, :].bitcast(FP8X4), lhsT_scale=w1_sc[:, 0, :],
+                                rhs=w1_codes[:, 0:2, :].rearrange("p t m -> p (t m)").bitcast(FP8X4),
+                                rhs_scale=w1_sc[:, 0:2, :].rearrange("p t m -> p (t m)"), start=True, stop=True)
         for a in range(2):
             gather_words(e_codes, e_word_win, a)
             first_product(h_bank, e_codes, e_sc, E_PLANE, 2 * a)
@@ -252,7 +266,7 @@ def tile_picked_ywien_wien_p_kernel(tc, x_words, x_scales, e_words, e_scales, w1
         def y_product(c):
             first_product(y_bank, x_codes, x_sc, X_PLANE, c)
 
-        nc.gpsimd.tensor_copy(w2_bf[:], w2_raw[:].rearrange("p j m -> p m j"))
+        nc.scalar.copy(w2_bf[:].rearrange("p (c i) j -> p c j i", i=SLOTS), w2_raw[:].rearrange("p j (c i) -> p c j i", i=SLOTS))
         nc.vector.quantize_mx(out=w2_codes[:].bitcast(FP8X4), scales=w2_sc[:], in_=w2_bf[:].rearrange("p m j -> p (m j)"))
         pivot(nc.scalar.copy, 0)
         pivot(nc.scalar.copy, 1)
@@ -260,46 +274,44 @@ def tile_picked_ywien_wien_p_kernel(tc, x_words, x_scales, e_words, e_scales, w1
         deviate(dev0, 1, 0, D - 1)
         square(dev0, 0, 0, D - 1)
         square(dev0, 1, 0, D - 1)
-        pivot(nc.vector.tensor_copy, 2)
-        pivot(nc.vector.tensor_copy, 3)
+        pivot(nc.scalar.copy, 2)
+        pivot(nc.scalar.copy, 3)
+        turn_pivots(0)
+        turn_pivots(1)
         gather_words(x_codes, x_word_win, 0)
         deviate(dev1, 2, 0, D - 1)
         deviate(dev1, 3, 0, D - 1)
         gather_words(x_codes, x_word_win, 1)
         sums(0, rows_of(dev0, D - 1))
-        turn_pivots(0)
         y_product(0)
         y_product(1)
-        spread_gain(0)
-        mean_gain(0)
-        sq[1] = reuse.tile([P, D - 1, P], F32, name="sq1", offset=2 * win_bytes)
-        square(dev1, 2, 0, D - 1)
-        square(dev1, 3, 0, D - 1)
+        gains(0)
         y_product(2)
         y_product(3)
+        sq[1] = reuse.tile([P, D - 1, P], F32, name="sq1", offset=2 * win_bytes + 1024)
+        square(dev1, 2, 0, D - 1)
+        square(dev1, 3, 0, D - 1)
         sum_y(0)
         sum_y(1)
         scale_y_sum(0)
         make_a(0, gain_a[0])
         make_b(0)
-        turn_pivots(1)
         sums(1, rows_of(dev1, D - 1))
-        mean_gain(1)
-        spread_gain(1)
+        gains(1)
         sum_y(2)
         times_a(0)
         sum_y(3)
+        unit_y_sum[1] = reuse.tile([P, P], F32, name="unit_y_sum_last", offset=2 * win_bytes)
         scale_y_sum(1)
         times_a(1)
         plus_b(0)
         plus_b(1)
+        second_product(0)
         make_a(1, gain_a[1])
         make_b(1)
-        z_sc[0] = reuse.tile([P, P], U8, name="z_sc0", offset=3 * win_bytes, align_bytes=64)
-        z_sc[1] = reuse.tile([P, P], U8, name="z_sc1", offset=3 * win_bytes + 1024, align_bytes=64)
-        second_product(0)
-        times_a(2)
+        z_sc[1] = reuse.tile([P, P], U8, name="z_sc1", offset=3 * win_bytes, align_bytes=64)
         second_product(1)
+        times_a(2)
         times_a(3)
         plus_b(2)
         plus_b(3)

@@ -25,7 +25,7 @@ CHUNK_COLS = GROUPS * SLOTS
 HALF = 2 * P
 MEAN_NOISE, VAR_NOISE = 0.2, 0.3
 E_PLANE, X_PLANE = 0, 4
-W1_PARTS = (0, 48, 96, 128)
+W1_PARTS = (0, 64, 128)
 
 
 def tile_picked_ywien_wien_p_kernel(tc, x_words, x_scales, e_words, e_scales, w1, unit, w2, offs, out):
@@ -50,7 +50,7 @@ def tile_picked_ywien_wien_p_kernel(tc, x_words, x_scales, e_words, e_scales, w1
         x_scale_win = tile("x_scale_win", [P, T], U8)
         e_word_win = reuse.tile([P, T], I32, name="e_word_win", offset=0, align_bytes=64)
         x_word_win = reuse.tile([P, T], I32, name="x_word_win", offset=win_bytes, align_bytes=64)
-        w1_raw = [tile("w1_raw%d" % part, [P, SLOTS, SLOTS * (W1_PARTS[part + 1] - W1_PARTS[part])]) for part in range(3)]
+        w1_raw = [tile("w1_raw%d" % part, [P, SLOTS, SLOTS * (W1_PARTS[part + 1] - W1_PARTS[part])]) for part in range(2)]
         w2_raw = tile("w2_raw", [P, SLOTS, N])
         unit_sb = tile("unit_sb", [P, SLOTS])
         ident = tile("ident", [P, P])
@@ -93,7 +93,6 @@ def tile_picked_ywien_wien_p_kernel(tc, x_words, x_scales, e_words, e_scales, w1
         load_scales(e_scale_win, e_scales, E_PLANE)
         load_scales(x_scale_win, x_scales, X_PLANE)
         load_w1(1)
-        load_w1(2)
         load_words(e_word_win, e_words)
         nc.vector.tensor_copy(e_sc_picked[:], e_scale_win[:].indirect(offsets[:]))
         nc.vector.tensor_copy(x_sc_picked[:], x_scale_win[:].indirect(offsets[:]))
@@ -234,7 +233,7 @@ def tile_picked_ywien_wien_p_kernel(tc, x_words, x_scales, e_words, e_scales, w1
             nc.scalar.copy(res[c][:], acc)
             (nc.scalar if c == 3 else nc.sync).dma_start(out[:, P * c : P * (c + 1)], res[c][:])
 
-        for part in range(3):
+        for part in range(2):
             cast_w1(part)
         quantise_w1(0)
         quantise_w1(2)

@@ -113,7 +113,6 @@ def tile_picked_ywien_wien_p_kernel(tc, x_words, x_scales, e_words, e_scales, w1
         neg_sq_sum = per_half("neg_sq_sum")
         root1, q1, mean_sq, root0, q_diff = (per_half(nm) for nm in ("root1", "q1", "mean_sq", "root0", "q_diff"))
         q0 = per_half("q0")
-        q_diff[0] = reuse.tile([P, P], F32, name="q_diff_first", offset=2 * win_bytes)
         root1[1] = reuse.tile([P, P], F32, name="root1_last", offset=3 * win_bytes)
         offset_b = per_half("offset_b")
         neg_unit = tile("neg_unit", [P, SLOTS])
@@ -259,7 +258,7 @@ def tile_picked_ywien_wien_p_kernel(tc, x_words, x_scales, e_words, e_scales, w1
             nc.gpsimd.tensor_tensor(by_slot(unit_y_sum[a][:]), by_slot(y_sum[a][:]), over_groups(unit8, 2 * GROUPS), ALU.mult)
 
         def make_b(a):
-            nc.gpsimd.tensor_tensor(q_diff[a][:], q1[a][:], q0[a][:], ALU.subtract)
+            nc.vector.tensor_tensor(q_diff[a][:], q1[a][:], q0[a][:], ALU.subtract)
             nc.gpsimd.tensor_tensor(offset_b[a][:], q_diff[a][:], unit_y_sum[a][:], ALU.mult)
 
         def y_product(c):
@@ -293,15 +292,14 @@ def tile_picked_ywien_wien_p_kernel(tc, x_words, x_scales, e_words, e_scales, w1
         sum_y(0)
         sum_y(1)
         scale_y_sum(0)
+        sum_y(2)
+        sum_y(3)
+        scale_y_sum(1)
         make_a(0, gain_a[0])
         make_b(0)
         sums(1, rows_of(dev1, D - 1))
         gains(1)
-        sum_y(2)
         times_a(0)
-        sum_y(3)
-        unit_y_sum[1] = reuse.tile([P, P], F32, name="unit_y_sum_last", offset=2 * win_bytes)
-        scale_y_sum(1)
         times_a(1)
         plus_b(0)
         plus_b(1)

@@ -67,10 +67,10 @@ def tile_picked_ywien_wien_p_kernel(tc, x_words, x_scales, e_words, e_scales, w1
         nc.gpsimd.memset(x_sc[:].bitcast(I32), 0)
         nc.scalar.activation(warm[:], warm[:], ACT.Abs_reciprocal_sqrt)
         make_identity(nc, ident[:])
-        neg_scale = [reuse.tile([P, 1], F32, name="neg_scale0", offset=2 * win_bytes + 1024), tile("neg_scale1", [P, 1])]
+        neg_scale = [reuse.tile([P, 1], F32, name="neg_scale0", offset=2 * win_bytes + 1024)]
         one = tile("one", [P, 1])
         nc.gpsimd.memset(one[:], 1.0)
-        for a in range(2):
+        for a in range(1):
             nc.gpsimd.tensor_scalar(neg_scale[a][:], one[:], -1.0 / (D * VAR_NOISE), 0.0, ALU.mult, ALU.add)
 
         def load_scales(win, src, plane):
@@ -110,17 +110,17 @@ def tile_picked_ywien_wien_p_kernel(tc, x_words, x_scales, e_words, e_scales, w1
         x_codes = [tile("x_codes%d" % a, [P, HALF], U32) for a in range(2)]
         sq = [tile("sq0", [P, D - 1, P]), None]
         h0_turned, dev_sum, dev_sum_sq = (per_half(nm) for nm in ("h0_turned", "dev_sum", "dev_sum_sq"))
-        neg_sq_sum = per_half("neg_sq_sum")
+        dev_sum_sq[0] = reuse.tile([P, P], F32, name="dev_sum_sq_first", offset=3 * win_bytes + 1024)
+        neg_sq_sum = [reuse.tile([P, P], F32, name="neg_sq_sum0", offset=3 * win_bytes), tile("neg_sq_sum1", [P, P])]
         root1, q1, mean_sq, root0, q_diff = (per_half(nm) for nm in ("root1", "q1", "mean_sq", "root0", "q_diff"))
         q0 = per_half("q0")
-        root1[1] = reuse.tile([P, P], F32, name="root1_last", offset=3 * win_bytes)
         offset_b = per_half("offset_b")
         neg_unit = tile("neg_unit", [P, SLOTS])
         unit8 = tile("unit8", [P, SLOTS])
         ay = [tile("ay%d" % c, [P, GROUPS, D, SLOTS]) for c in range(4)]
         z_bf = [tile("z_bf%d" % c, [P, GROUPS, D, SLOTS], BF16) for c in range(4)]
         z_codes = [tile("z_codes%d" % c, [P, P], U32) for c in range(4)]
-        z_sc = [tile("z_sc%d" % c, [P, P], U8) if c != 1 else None for c in range(4)]
+        z_sc = [tile("z_sc%d" % c, [P, P], U8) for c in range(4)]
         res = [tile("res%d" % c, [P, P]) for c in range(4)]
         w2_bf = tile("w2_bf", [P, N, SLOTS], BF16)
         w2_codes = tile("w2_codes", [P, N], U32)
@@ -203,17 +203,16 @@ def tile_picked_ywien_wien_p_kernel(tc, x_words, x_scales, e_words, e_scales, w1
 
         def gains(a):
             mean, spread = region(h_bank[2 * a], 1), region(h_bank[2 * a + 1], 1)
-            for first, (for_spread, for_mean) in ((True, (dev_sum_sq, h0_turned)), (False, (neg_sq_sum, dev_sum))):
-                nc.tensor.matmul(spread, lhsT=for_spread[a][:], rhs=ident[:], start=first, stop=not first, is_transpose=True)
-                nc.tensor.matmul(mean, lhsT=for_mean[a][:], rhs=ident[:], start=first, stop=not first, is_transpose=True)
-            nc.scalar.activation(root1[a][:], spread, ACT.Abs_reciprocal_sqrt, bias=1.0, scale=-1.0)
+            turned_sum(mean, [h0_turned[a][:], dev_sum[a][:]])
+            turned_sum(spread, [dev_sum_sq[a][:], neg_sq_sum[a][:]])
             nc.scalar.activation(mean_sq[a][:], mean, ACT.Square, scale=1.0 / (D * math.sqrt(MEAN_NOISE)))
-            nc.scalar.activation(q1[a][:], root1[a][:], ACT.Square)
+            nc.scalar.activation(root1[a][:], spread, ACT.Abs_reciprocal_sqrt, bias=1.0, scale=-1.0)
             nc.scalar.activation(root0[a][:], mean_sq[a][:], ACT.Abs_reciprocal_sqrt, bias=1.0)
+            nc.scalar.activation(q1[a][:], root1[a][:], ACT.Square)
             nc.scalar.activation(q0[a][:], root0[a][:], ACT.Square)
 
         def make_a(a, gain):
-            nc.vector.scalar_tensor_tensor(out=by_slot(gain[:]), in0=by_slot(q1[a][:]), scalar=-1.0, in1=over_groups(neg_unit, 2 * GROUPS), op0=ALU.add, op1=ALU.mult)
+            nc.vector.scalar_tensor_tensor(out=by_slot(gain[:]), in0=by_slot(q1_back if a else q1[a][:]), scalar=-1.0, in1=over_groups(neg_unit, 2 * GROUPS), op0=ALU.add, op1=ALU.mult)
 
         def per_member(g, c):
             return by_slot(g[c // 2][:, chunk_cols(c)]).unsqueeze(2).to_broadcast([P, GROUPS, D, SLOTS])
@@ -226,7 +225,7 @@ def tile_picked_ywien_wien_p_kernel(tc, x_words, x_scales, e_words, e_scales, w1
 
         def second_product(c):
             nc.vector.quantize_mx(out=z_codes[c][:].bitcast(FP8X4), scales=z_sc[c][:], in_=z_bf[c][:].rearrange("p v d t -> p (v d t)"))
-            acc = region(h_bank[3 - c], 3) if c < 2 else region(y_bank[c], 0)
+            acc = region(h_bank[0], c) if c < 2 else region(y_bank[c], 0)
             nc.tensor.matmul_mx(out=acc, lhsT=w2_codes[:].bitcast(FP8X4), lhsT_scale=w2_sc[:],
                                 rhs=z_codes[c][:].bitcast(FP8X4), rhs_scale=z_sc[c][:], start=True, stop=True)
             nc.scalar.copy(res[c][:], acc)
@@ -258,8 +257,11 @@ def tile_picked_ywien_wien_p_kernel(tc, x_words, x_scales, e_words, e_scales, w1
             nc.gpsimd.tensor_tensor(by_slot(unit_y_sum[a][:]), by_slot(y_sum[a][:]), over_groups(unit8, 2 * GROUPS), ALU.mult)
 
         def make_b(a):
-            nc.vector.tensor_tensor(q_diff[a][:], q1[a][:], q0[a][:], ALU.subtract)
-            nc.gpsimd.tensor_tensor(offset_b[a][:], q_diff[a][:], unit_y_sum[a][:], ALU.mult)
+            nc.vector.tensor_tensor(q_diff[a][:], q1_back if a else q1[a][:], q0[a][:], ALU.subtract)
+            if a == 0:
+                nc.gpsimd.tensor_tensor(offset_b[a][:], q_diff[a][:], unit_y_sum[a][:], ALU.mult)
+            else:
+                nc.gpsimd.tensor_tensor(by_slot(unit_y_sum[a][:]), by_slot(q_diff[a][:]), over_groups(unit8, 2 * GROUPS), ALU.mult)
 
         def y_product(c):
             first_product(y_bank, x_codes, x_sc, X_PLANE, c)
@@ -275,11 +277,15 @@ def tile_picked_ywien_wien_p_kernel(tc, x_words, x_scales, e_words, e_scales, w1
         pivot(nc.scalar.copy, 2)
         pivot(nc.scalar.copy, 3)
         turn_pivots(0)
-        turn_pivots(1)
         gather_words(x_codes, x_word_win, 0)
         deviate(dev1, 2, 0, D - 1)
         deviate(dev1, 3, 0, D - 1)
+        h_sum = tile("h_sum", [P, P])
+        q1_back = region(h_bank[2], 1)
+        for c in (2, 3):
+            nc.vector.tensor_reduce(by_slot(h_sum[:, chunk_cols(c)]), h_bank[c][:].rearrange("p (t v d) -> p v t d", t=SLOTS, d=D), AX.X, ALU.add)
         gather_words(x_codes, x_word_win, 1)
+        nc.vector.scalar_tensor_tensor(out=dev_sum[1][:], in0=h0[1][:], scalar=-float(D), in1=h_sum[:], op0=ALU.mult, op1=ALU.add)
         sums(0, rows_of(dev0, D - 1))
         y_product(0)
         y_product(1)
@@ -289,26 +295,40 @@ def tile_picked_ywien_wien_p_kernel(tc, x_words, x_scales, e_words, e_scales, w1
         sq[1] = reuse.tile([P, D - 1, P], F32, name="sq1", offset=2 * win_bytes + 1024)
         square(dev1, 2, 0, D - 1)
         square(dev1, 3, 0, D - 1)
+        mean_sq[1] = reuse.tile([P, P], F32, name="mean_sq_last", offset=3 * win_bytes)
+        nc.scalar.activation(mean_sq[1][:], h_sum[:], ACT.Square, scale=1.0 / (D * math.sqrt(MEAN_NOISE)))
+        nc.scalar.activation(root0[1][:], mean_sq[1][:], ACT.Abs_reciprocal_sqrt, bias=1.0)
+        nc.scalar.activation(q0[1][:], root0[1][:], ACT.Square)
         sum_y(0)
         sum_y(1)
         scale_y_sum(0)
-        sum_y(2)
-        sum_y(3)
-        scale_y_sum(1)
+        neg_sq_sum[1] = reuse.tile([P, P], F32, name="neg_sq_sum_last", offset=3 * win_bytes + 1024)
+        nc.vector.scalar_tensor_tensor(out=neg_sq_sum[1][:], in0=dev_sum[1][:], scalar=-1.0 / D, in1=dev_sum[1][:], op0=ALU.mult, op1=ALU.mult)
         make_a(0, gain_a[0])
         make_b(0)
-        sums(1, rows_of(dev1, D - 1))
-        gains(1)
+        turned_sum(region(h_bank[3], 0), rows_of(sq[1], D - 1) + [neg_sq_sum[1][:]])
+        nc.scalar.activation(root1[1][:], region(h_bank[3], 0), ACT.Abs_reciprocal_sqrt, bias=1.0, scale=1.0 / (D * VAR_NOISE))
+        nc.scalar.activation(q1[1][:], root1[1][:], ACT.Square)
+        turned_sum(q1_back, [q1[1][:]])
+        y_rows = tile("y_rows", [P, D, P])
+        y_sum_turned = reuse.tile([P, P], F32, name="y_sum_turned", offset=3 * win_bytes + 2048)
+        y_sum_back = region(h_bank[0], 3)
+        for c in (2, 3):
+            nc.scalar.copy(y_rows[:, :, chunk_cols(c)].rearrange("p d (v t) -> p d v t", t=SLOTS), members(y_bank[c]))
+        turned_sum(region(h_bank[1], 2), rows_of(y_rows, D))
+        nc.scalar.copy(y_sum_turned[:], region(h_bank[1], 2))
+        turned_sum(y_sum_back, [y_sum_turned[:]])
         times_a(0)
         times_a(1)
         plus_b(0)
         plus_b(1)
-        second_product(0)
         make_a(1, gain_a[1])
         make_b(1)
-        z_sc[1] = reuse.tile([P, P], U8, name="z_sc1", offset=3 * win_bytes, align_bytes=64)
-        second_product(1)
         times_a(2)
+        nc.vector.tensor_tensor(offset_b[1][:], y_sum_back, unit_y_sum[1][:], ALU.mult)
+        second_product(0)
+        second_product(1)
+        ay[3] = reuse.tile([P, GROUPS, D, SLOTS], F32, name="ay_last", offset=3 * win_bytes + 2048)
         times_a(3)
         plus_b(2)
         plus_b(3)

@@ -25,7 +25,8 @@ CHUNK_COLS = GROUPS * SLOTS
 HALF = 2 * P
 MEAN_NOISE, VAR_NOISE = 0.2, 0.3
 E_PLANE, X_PLANE = 0, 4
-W1_PARTS = (0, 64, 128)
+WARM_PASSES = 4
+OWN_GROUPS = 8
 
 
 def tile_picked_ywien_wien_p_kernel(tc, x_words, x_scales, e_words, e_scales, w1, unit, w2, offs, out):
@@ -38,47 +39,37 @@ def tile_picked_ywien_wien_p_kernel(tc, x_words, x_scales, e_words, e_scales, w1
         def tile(name, shape, dt=F32):
             return sb.tile(shape, dt, name=name, align_bytes=64)
 
-        def per_half(name):
-            return [tile("%s%d" % (name, a), [P, P]) for a in range(2)]
+        def shared(name, shape, dt, place):
+            return reuse.tile(shape, dt, name=name, offset=place, align_bytes=64)
 
         offsets = sb.tile([P, S // 16], U16, name="offsets")
         h_bank = [ps.tile([P, SLOTS * P], F32, name="h_bank%d" % c) for c in range(4)]
         y_bank = [ps.tile([P, SLOTS * P], F32, name="y_bank%d" % c) for c in range(4)]
 
-        win_bytes = 4 * T
         e_scale_win = tile("e_scale_win", [P, T], U8)
         x_scale_win = tile("x_scale_win", [P, T], U8)
-        e_word_win = reuse.tile([P, T], I32, name="e_word_win", offset=0, align_bytes=64)
-        x_word_win = reuse.tile([P, T], I32, name="x_word_win", offset=win_bytes, align_bytes=64)
-        w1_raw = [tile("w1_raw%d" % part, [P, SLOTS, SLOTS * (W1_PARTS[part + 1] - W1_PARTS[part])]) for part in range(2)]
+        e_word_win = tile("e_word_win", [P, T], I32)
+        x_word_win = shared("x_word_win", [P, T], I32, 16384)
+        w1_raw = [tile("w1_raw%d" % part, [P, SLOTS, HALF]) for part in range(2)]
         w2_raw = tile("w2_raw", [P, SLOTS, N])
         unit_sb = tile("unit_sb", [P, SLOTS])
         ident = tile("ident", [P, P])
         warm = tile("warm", [P, 1])
-        e_sc = tile("e_sc", [P, S], U8)
-        e_sc_picked = tile("e_sc_picked", [P, S], U8)
-        x_sc = tile("x_sc", [P, S], U8)
-        x_sc_picked = tile("x_sc_picked", [P, S], U8)
+        e_sc, e_sc_picked, x_sc = (tile(nm, [P, S], U8) for nm in ("e_sc", "e_sc_picked", "x_sc"))
 
         nc.gpsimd.memset(e_scale_win[:].bitcast(I32), 0)
         nc.vector.memset(warm[:], 1.0)
         nc.vector.memset(x_scale_win[:].bitcast(I32), 0)
         nc.gpsimd.memset(e_sc[:].bitcast(I32), 0)
-        nc.gpsimd.memset(x_sc[:].bitcast(I32), 0)
         nc.scalar.activation(warm[:], warm[:], ACT.Abs_reciprocal_sqrt)
         make_identity(nc, ident[:])
-        neg_scale = [reuse.tile([P, 1], F32, name="neg_scale0", offset=2 * win_bytes + 1024)]
-        one = tile("one", [P, 1])
-        nc.gpsimd.memset(one[:], 1.0)
-        for a in range(1):
-            nc.gpsimd.tensor_scalar(neg_scale[a][:], one[:], -1.0 / (D * VAR_NOISE), 0.0, ALU.mult, ALU.add)
 
         def load_scales(win, src, plane):
             nc.sync.dma_start(win[plane:P:8, :].bitcast(I32), src[0].bitcast(I32))
 
-        def place_scales(queue, dst, picked, plane, rows):
-            for r in rows:
-                queue.dma_start(dst[plane + r : P : 32, :].bitcast(I32), picked[plane + 8 * r : P : 32, :].bitcast(I32))
+        def place_scales(dst, picked, plane):
+            for r in range(4):
+                nc.sync.dma_start(dst[plane + r : P : 32, :].bitcast(I32), picked[plane + 8 * r : P : 32, :].bitcast(I32))
 
         def load_words(win, src):
             nc.sync.dma_start(win[:], src[0].rearrange("p n t -> p (n t)").bitcast(I32))
@@ -86,45 +77,21 @@ def tile_picked_ywien_wien_p_kernel(tc, x_words, x_scales, e_words, e_scales, w1
         w1_rows = w1.rearrange("(p j) c -> p j c", j=SLOTS)
 
         def load_w1(part):
-            nc.sync.dma_start(w1_raw[part][:], w1_rows[:, :, SLOTS * W1_PARTS[part] : SLOTS * W1_PARTS[part + 1]])
+            nc.sync.dma_start(w1_raw[part][:], w1_rows[:, :, HALF * part : HALF * (part + 1)])
 
-        load_w1(0)
         nc.sync.dma_start(offsets[:], offs)
+        load_w1(0)
         load_scales(e_scale_win, e_scales, E_PLANE)
-        load_scales(x_scale_win, x_scales, X_PLANE)
+        for r in range(4):
+            nc.sync.dma_start(x_scale_win[X_PLANE + r : P : 32, :].bitcast(I32), x_scales[0][r:16:4, :].bitcast(I32))
         load_w1(1)
         load_words(e_word_win, e_words)
         nc.vector.tensor_copy(e_sc_picked[:], e_scale_win[:].indirect(offsets[:]))
-        nc.vector.tensor_copy(x_sc_picked[:], x_scale_win[:].indirect(offsets[:]))
-        nc.sync.dma_start(w2_raw[:], w2.rearrange("(p j) m -> p j m", j=SLOTS))
-        place_scales(nc.sync, e_sc, e_sc_picked, E_PLANE, range(4))
+        nc.vector.tensor_copy(x_sc[:], x_scale_win[:].indirect(offsets[:]))
+        place_scales(e_sc, e_sc_picked, E_PLANE)
         load_words(x_word_win, x_words)
-        place_scales(nc.sync, x_sc, x_sc_picked, X_PLANE, range(4))
         nc.sync.dma_start(unit_sb[:], unit.rearrange("(p t) o -> p (t o)", t=SLOTS))
-
-        w1_bf = tile("w1_bf", [P, SLOTS, P, SLOTS], BF16)
-        w1_codes = tile("w1_codes", [P, SLOTS, P], U32)
-        w1_sc = tile("w1_sc", [P, SLOTS, P], U8)
-        e_codes = [tile("e_codes%d" % a, [P, HALF], U32) for a in range(2)]
-        h0 = per_half("h0")
-        x_codes = [tile("x_codes%d" % a, [P, HALF], U32) for a in range(2)]
-        sq = [tile("sq0", [P, D - 1, P]), None]
-        h0_turned, dev_sum, dev_sum_sq = (per_half(nm) for nm in ("h0_turned", "dev_sum", "dev_sum_sq"))
-        dev_sum_sq[0] = reuse.tile([P, P], F32, name="dev_sum_sq_first", offset=3 * win_bytes + 1024)
-        neg_sq_sum = [reuse.tile([P, P], F32, name="neg_sq_sum0", offset=3 * win_bytes), tile("neg_sq_sum1", [P, P])]
-        root1, q1, mean_sq, root0, q_diff = (per_half(nm) for nm in ("root1", "q1", "mean_sq", "root0", "q_diff"))
-        q0 = per_half("q0")
-        offset_b = per_half("offset_b")
-        neg_unit = tile("neg_unit", [P, SLOTS])
-        unit8 = tile("unit8", [P, SLOTS])
-        ay = [tile("ay%d" % c, [P, GROUPS, D, SLOTS]) for c in range(4)]
-        z_bf = [tile("z_bf%d" % c, [P, GROUPS, D, SLOTS], BF16) for c in range(4)]
-        z_codes = [tile("z_codes%d" % c, [P, P], U32) for c in range(4)]
-        z_sc = [tile("z_sc%d" % c, [P, P], U8) for c in range(4)]
-        res = [tile("res%d" % c, [P, P]) for c in range(4)]
-        w2_bf = tile("w2_bf", [P, N, SLOTS], BF16)
-        w2_codes = tile("w2_codes", [P, N], U32)
-        w2_sc = tile("w2_sc", [P, N], U8)
+        nc.sync.dma_start(w2_raw[:], w2.rearrange("(p j) m -> p j m", j=SLOTS))
 
         def by_slot(x):
             return x.rearrange("p (v t) -> p v t", t=SLOTS)
@@ -138,199 +105,215 @@ def tile_picked_ywien_wien_p_kernel(tc, x_words, x_scales, e_words, e_scales, w1
         def members(bank):
             return bank[:].rearrange("p (t v d) -> p d v t", t=SLOTS, d=D)
 
-        def over_groups(x, groups):
-            return x[:].unsqueeze(1).to_broadcast([P, groups, SLOTS])
+        def over_groups(x):
+            return x[:].unsqueeze(1).to_broadcast([P, 2 * GROUPS, SLOTS])
 
-        def cast_w1(part):
-            nc.scalar.copy(w1_bf[:].rearrange("p t m j -> p m t j")[:, W1_PARTS[part] : W1_PARTS[part + 1]],
+        def turned_sum(dst, parts):
+            for n, part in enumerate(parts):
+                nc.tensor.matmul(dst, lhsT=part, rhs=ident[:], start=(n == 0), stop=(n == len(parts) - 1), is_transpose=True)
+
+        def rows_of(x):
+            return [x[:, d, :] for d in range(x.shape[1])]
+
+        neg_unit = tile("neg_unit", [P, SLOTS])
+        unit8 = tile("unit8", [P, P])
+        nc.gpsimd.tensor_scalar(by_slot(unit8[:]), over_groups(unit_sb), 1.0 / D, 0.0, ALU.mult, ALU.add)
+        nc.gpsimd.tensor_scalar(neg_unit[:], unit_sb[:], -1.0, 0.0, ALU.mult, ALU.add)
+
+        w1_bf = tile("w1_bf", [P, SLOTS, P, SLOTS], BF16)
+        w1_codes = tile("w1_codes", [P, SLOTS, P], U32)
+        w1_sc = tile("w1_sc", [P, SLOTS, P], U8)
+        w2_codes = tile("w2_codes", [P, N], U32)
+        w2_sc = tile("w2_sc", [P, N], U8)
+        for part in range(2):
+            nc.scalar.copy(w1_bf[:].rearrange("p t m j -> p m t j")[:, 64 * part : 64 * (part + 1)],
                            w1_raw[part][:].rearrange("p j (m t) -> p m t j", t=SLOTS))
-
-        def quantise_w1(t0):
+        for t0 in (0, 2):
             nc.vector.quantize_mx(
                 out=w1_codes[:, t0 : t0 + 2, :].rearrange("p t m -> p (t m)").bitcast(FP8X4),
                 scales=w1_sc[:, t0 : t0 + 2, :].rearrange("p t m -> p (t m)"),
                 in_=w1_bf[:, t0 : t0 + 2].rearrange("p t m j -> p (t m j)"),
             )
+        for n in range(WARM_PASSES):
+            nc.tensor.matmul_mx(out=y_bank[2 + n // 2][:, HALF * (n % 2) : HALF * (n % 2 + 1)], lhsT=w1_codes[:, 0, :].bitcast(FP8X4), lhsT_scale=w1_sc[:, 0, :],
+                                rhs=w1_codes[:, 0:2, :].rearrange("p t m -> p (t m)").bitcast(FP8X4),
+                                rhs_scale=w1_sc[:, 0:2, :].rearrange("p t m -> p (t m)"), start=True, stop=True)
 
-        def gather_words(dst, win, a):
-            cols = HALF // 16
-            nc.vector.tensor_copy(dst[a][:], win[:].bitcast(U32).indirect(offsets[:, cols * a : cols * (a + 1)]))
+        e_codes, x_codes = {}, {}
+
+        def gather_words(codes, picked, win, first):
+            count = picked.shape[1] // P
+            nc.vector.tensor_copy(picked[:], win[:].bitcast(U32).indirect(offsets[:, P // 16 * first : P // 16 * (first + count)]))
+            codes.update({first + n: region(picked, n) for n in range(count)})
 
         def first_product(bank, codes, scales, plane, c):
             for t in range(SLOTS):
                 nc.tensor.matmul_mx(
                     out=region(bank[c], t),
                     lhsT=w1_codes[:, t, :].bitcast(FP8X4), lhsT_scale=w1_sc[:, t, :],
-                    rhs=codes[c // 2][:, P * (c % 2) : P * (c % 2 + 1)].bitcast(FP8X4),
+                    rhs=codes[c].bitcast(FP8X4),
                     rhs_scale=scales[plane:P, P * c : P * (c + 1)],
                     start=True, stop=True,
                 )
 
-        def deviate(dev, c, r0, r1):
+        for first, count in ((0, 1), (1, 1), (2, 2)):
+            gather_words(e_codes, tile("e_codes%d" % first, [P, count * P], U32), e_word_win, first)
+        for c in range(4):
+            first_product(h_bank, e_codes, e_sc, E_PLANE, c)
+
+        pivot = [tile("pivot%d" % a, [P, P]) for a in range(2)]
+        dev = [tile("dev%d" % a, [P, D - 1, P]) for a in range(2)]
+        sq = [tile("sq%d" % a, [P, D - 1, P]) for a in range(2)]
+
+        def deviate(c):
             cols = chunk_cols(c)
             nc.vector.tensor_tensor(
-                dev[:, r0:r1, cols].rearrange("p d (v t) -> p d v t", t=SLOTS),
-                members(h_bank[c])[:, 1 + r0 : 1 + r1],
-                by_slot(h0[c // 2][:, cols]).unsqueeze(1).to_broadcast([P, r1 - r0, GROUPS, SLOTS]),
+                dev[c // 2][:, :, cols].rearrange("p d (v t) -> p d v t", t=SLOTS),
+                members(h_bank[c])[:, 1:D],
+                by_slot(pivot[c // 2][:, cols]).unsqueeze(1).to_broadcast([P, D - 1, GROUPS, SLOTS]),
                 ALU.subtract,
             )
 
-        def square(dev, c, r0, r1):
+        def square(c):
             cols = chunk_cols(c)
-            nc.scalar.activation(sq[c // 2][:, r0:r1, cols], dev[:, r0:r1, cols], ACT.Square)
+            nc.scalar.activation(sq[c // 2][:, :, cols], dev[c // 2][:, :, cols], ACT.Square)
 
-        def turned_sum(dst, parts):
-            for n, part in enumerate(parts):
-                nc.tensor.matmul(dst, lhsT=part, rhs=ident[:], start=(n == 0), stop=(n == len(parts) - 1), is_transpose=True)
+        def group_sum(dst, bank, c):
+            nc.vector.tensor_reduce(by_slot(dst[:, chunk_cols(c)]), bank[c][:].rearrange("p (t v d) -> p v t d", t=SLOTS, d=D), AX.X, ALU.add)
 
-        def rows_of(x, count):
-            return [x[:, d, :] for d in range(count)]
+        def take_pivot(c):
+            nc.scalar.copy(by_slot(pivot[c // 2][:, chunk_cols(c)]), members(h_bank[c])[:, 0])
 
-        def pivot(copy, c):
-            copy(by_slot(h0[c // 2][:, chunk_cols(c)]), members(h_bank[c])[:, 0])
+        for c in range(4):
+            take_pivot(c)
+        for c in range(4):
+            deviate(c)
+        pivot8_turned = tile("pivot8_turned", [P, P])
+        turned_sum(region(y_bank[0], 0), [pivot[0][:]])
+        square(0)
+        square(1)
+        gather_words(x_codes, tile("x_codes2", [P, HALF], U32), x_word_win, 2)
+        gather_words(x_codes, tile("x_codes0", [P, HALF], U32), x_word_win, 0)
+        w2_bf = shared("w2_bf", [P, N, SLOTS], BF16, 16384 + 1024)
+        nc.gpsimd.tensor_copy(w2_bf[:], w2_raw[:].rearrange("p j m -> p m j"))
+        nc.scalar.activation(pivot8_turned[:], region(y_bank[0], 0), ACT.Copy, scale=float(D))
+        square(2)
+        square(3)
 
-        def turn_pivots(a):
-            turned_sum(region(y_bank[2 + a], 0), [h0[a][:]])
-            nc.scalar.activation(h0_turned[a][:], region(y_bank[2 + a], 0), ACT.Copy, scale=float(D))
+        dev_sum, dev_sum_sq = tile("dev_sum", [P, P]), tile("dev_sum_sq", [P, P])
+        turned_sum(region(h_bank[0], 0), rows_of(dev[0]))
+        turned_sum(region(h_bank[1], 0), rows_of(sq[0]))
+        nc.scalar.activation(dev_sum_sq[:], region(h_bank[0], 0), ACT.Square, scale=1.0 / (D * math.sqrt(VAR_NOISE)))
+        nc.scalar.copy(dev_sum[:], region(h_bank[0], 0))
 
-        def sums(a, dev):
-            lo, hi = h_bank[2 * a], h_bank[2 * a + 1]
-            turned_sum(region(lo, 0), dev)
-            turned_sum(region(hi, 0), rows_of(sq[a], D - 1))
-            nc.scalar.activation(dev_sum_sq[a][:], region(lo, 0), ACT.Square, scale=1.0 / (D * math.sqrt(VAR_NOISE)))
-            nc.scalar.copy(dev_sum[a][:], region(lo, 0))
-            nc.scalar.activation(neg_sq_sum[a][:], region(hi, 0), ACT.Copy, scale=neg_scale[a][:])
-
-        def gains(a):
-            mean, spread = region(h_bank[2 * a], 1), region(h_bank[2 * a + 1], 1)
-            turned_sum(mean, [h0_turned[a][:], dev_sum[a][:]])
-            turned_sum(spread, [dev_sum_sq[a][:], neg_sq_sum[a][:]])
-            nc.scalar.activation(mean_sq[a][:], mean, ACT.Square, scale=1.0 / (D * math.sqrt(MEAN_NOISE)))
-            nc.scalar.activation(root1[a][:], spread, ACT.Abs_reciprocal_sqrt, bias=1.0, scale=-1.0)
-            nc.scalar.activation(root0[a][:], mean_sq[a][:], ACT.Abs_reciprocal_sqrt, bias=1.0)
-            nc.scalar.activation(q1[a][:], root1[a][:], ACT.Square)
-            nc.scalar.activation(q0[a][:], root0[a][:], ACT.Square)
-
-        def make_a(a, gain):
-            nc.vector.scalar_tensor_tensor(out=by_slot(gain[:]), in0=by_slot(q1_back if a else q1[a][:]), scalar=-1.0, in1=over_groups(neg_unit, 2 * GROUPS), op0=ALU.add, op1=ALU.mult)
-
-        def per_member(g, c):
-            return by_slot(g[c // 2][:, chunk_cols(c)]).unsqueeze(2).to_broadcast([P, GROUPS, D, SLOTS])
-
-        def times_a(c):
-            nc.vector.tensor_tensor(ay[c][:], y_bank[c][:].rearrange("p (t v d) -> p v d t", t=SLOTS, d=D), per_member(gain_a, c), ALU.mult)
-
-        def plus_b(c):
-            nc.vector.tensor_tensor(z_bf[c][:], ay[c][:], per_member(offset_b, c), ALU.add)
-
-        def second_product(c):
-            nc.vector.quantize_mx(out=z_codes[c][:].bitcast(FP8X4), scales=z_sc[c][:], in_=z_bf[c][:].rearrange("p v d t -> p (v d t)"))
-            acc = region(h_bank[0], c) if c < 2 else region(y_bank[c], 0)
-            nc.tensor.matmul_mx(out=acc, lhsT=w2_codes[:].bitcast(FP8X4), lhsT_scale=w2_sc[:],
-                                rhs=z_codes[c][:].bitcast(FP8X4), rhs_scale=z_sc[c][:], start=True, stop=True)
-            nc.scalar.copy(res[c][:], acc)
-            (nc.scalar if c == 3 else nc.sync).dma_start(out[:, P * c : P * (c + 1)], res[c][:])
-
-        for part in range(2):
-            cast_w1(part)
-        quantise_w1(0)
-        quantise_w1(2)
-        for n in range(4):
-            nc.tensor.matmul_mx(out=y_bank[2 + n // 2][:, HALF * (n % 2) : HALF * (n % 2 + 1)], lhsT=w1_codes[:, 0, :].bitcast(FP8X4), lhsT_scale=w1_sc[:, 0, :],
-                                rhs=w1_codes[:, 0:2, :].rearrange("p t m -> p (t m)").bitcast(FP8X4),
-                                rhs_scale=w1_sc[:, 0:2, :].rearrange("p t m -> p (t m)"), start=True, stop=True)
-        for a in range(2):
-            gather_words(e_codes, e_word_win, a)
-            first_product(h_bank, e_codes, e_sc, E_PLANE, 2 * a)
-            first_product(h_bank, e_codes, e_sc, E_PLANE, 2 * a + 1)
-        nc.gpsimd.tensor_scalar(neg_unit[:], unit_sb[:], -1.0, 0.0, ALU.mult, ALU.add)
-        nc.gpsimd.tensor_scalar(unit8[:], unit_sb[:], 1.0 / D, 0.0, ALU.mult, ALU.add)
-
-        dev0 = tile("dev0", [P, D - 1, P])
-        dev1 = tile("dev1", [P, D - 1, P])
-        y_sum, unit_y_sum, gain_a = per_half("y_sum"), per_half("unit_y_sum"), per_half("gain_a")
-
-        def sum_y(c):
-            nc.vector.tensor_reduce(by_slot(y_sum[c // 2][:, chunk_cols(c)]), y_bank[c][:].rearrange("p (t v d) -> p v t d", t=SLOTS, d=D), AX.X, ALU.add)
-
-        def scale_y_sum(a):
-            nc.gpsimd.tensor_tensor(by_slot(unit_y_sum[a][:]), by_slot(y_sum[a][:]), over_groups(unit8, 2 * GROUPS), ALU.mult)
-
-        def make_b(a):
-            nc.vector.tensor_tensor(q_diff[a][:], q1_back if a else q1[a][:], q0[a][:], ALU.subtract)
-            if a == 0:
-                nc.gpsimd.tensor_tensor(offset_b[a][:], q_diff[a][:], unit_y_sum[a][:], ALU.mult)
-            else:
-                nc.gpsimd.tensor_tensor(by_slot(unit_y_sum[a][:]), by_slot(q_diff[a][:]), over_groups(unit8, 2 * GROUPS), ALU.mult)
-
-        def y_product(c):
+        for c in (2, 3):
+            first_product(y_bank, x_codes, x_sc, X_PLANE, c)
+        neg_sq_sum = shared("neg_sq_sum", [P, P], F32, 16384 + 4096)
+        nc.scalar.activation(neg_sq_sum[:], region(h_bank[1], 0), ACT.Copy, scale=-1.0 / (D * VAR_NOISE))
+        mean0, spread0 = region(h_bank[0], 2), region(h_bank[0], 1)
+        turned_sum(spread0, [dev_sum_sq[:], neg_sq_sum[:]])
+        turned_sum(mean0, [pivot8_turned[:], dev_sum[:]])
+        for c in (0, 1):
             first_product(y_bank, x_codes, x_sc, X_PLANE, c)
 
-        nc.scalar.copy(w2_bf[:].rearrange("p (c i) j -> p c j i", i=SLOTS), w2_raw[:].rearrange("p j (c i) -> p c j i", i=SLOTS))
+        h_sum, dev_sum1, neg_dev_sq = shared("h_sum", [P, P], F32, 16384), tile("dev_sum1", [P, P]), tile("neg_dev_sq", [P, P])
+        group_sum(h_sum, h_bank, 2)
+        group_sum(h_sum, h_bank, 3)
+        nc.vector.scalar_tensor_tensor(out=dev_sum1[:], in0=pivot[1][:], scalar=-float(D), in1=h_sum[:], op0=ALU.mult, op1=ALU.add)
         nc.vector.quantize_mx(out=w2_codes[:].bitcast(FP8X4), scales=w2_sc[:], in_=w2_bf[:].rearrange("p m j -> p (m j)"))
-        pivot(nc.scalar.copy, 0)
-        pivot(nc.scalar.copy, 1)
-        deviate(dev0, 0, 0, D - 1)
-        deviate(dev0, 1, 0, D - 1)
-        square(dev0, 0, 0, D - 1)
-        square(dev0, 1, 0, D - 1)
-        pivot(nc.scalar.copy, 2)
-        pivot(nc.scalar.copy, 3)
-        turn_pivots(0)
-        gather_words(x_codes, x_word_win, 0)
-        deviate(dev1, 2, 0, D - 1)
-        deviate(dev1, 3, 0, D - 1)
-        h_sum = tile("h_sum", [P, P])
-        q1_back = region(h_bank[2], 1)
-        for c in (2, 3):
-            nc.vector.tensor_reduce(by_slot(h_sum[:, chunk_cols(c)]), h_bank[c][:].rearrange("p (t v d) -> p v t d", t=SLOTS, d=D), AX.X, ALU.add)
-        gather_words(x_codes, x_word_win, 1)
-        nc.vector.scalar_tensor_tensor(out=dev_sum[1][:], in0=h0[1][:], scalar=-float(D), in1=h_sum[:], op0=ALU.mult, op1=ALU.add)
-        sums(0, rows_of(dev0, D - 1))
-        y_product(0)
-        y_product(1)
-        gains(0)
-        y_product(2)
-        y_product(3)
-        sq[1] = reuse.tile([P, D - 1, P], F32, name="sq1", offset=2 * win_bytes + 1024)
-        square(dev1, 2, 0, D - 1)
-        square(dev1, 3, 0, D - 1)
-        mean_sq[1] = reuse.tile([P, P], F32, name="mean_sq_last", offset=3 * win_bytes)
-        nc.scalar.activation(mean_sq[1][:], h_sum[:], ACT.Square, scale=1.0 / (D * math.sqrt(MEAN_NOISE)))
-        nc.scalar.activation(root0[1][:], mean_sq[1][:], ACT.Abs_reciprocal_sqrt, bias=1.0)
-        nc.scalar.activation(q0[1][:], root0[1][:], ACT.Square)
-        sum_y(0)
-        sum_y(1)
-        scale_y_sum(0)
-        neg_sq_sum[1] = reuse.tile([P, P], F32, name="neg_sq_sum_last", offset=3 * win_bytes + 1024)
-        nc.vector.scalar_tensor_tensor(out=neg_sq_sum[1][:], in0=dev_sum[1][:], scalar=-1.0 / D, in1=dev_sum[1][:], op0=ALU.mult, op1=ALU.mult)
-        make_a(0, gain_a[0])
-        make_b(0)
-        turned_sum(region(h_bank[3], 0), rows_of(sq[1], D - 1) + [neg_sq_sum[1][:]])
-        nc.scalar.activation(root1[1][:], region(h_bank[3], 0), ACT.Abs_reciprocal_sqrt, bias=1.0, scale=1.0 / (D * VAR_NOISE))
-        nc.scalar.activation(q1[1][:], root1[1][:], ACT.Square)
-        turned_sum(q1_back, [q1[1][:]])
+        nc.vector.scalar_tensor_tensor(out=neg_dev_sq[:], in0=dev_sum1[:], scalar=-1.0 / D, in1=dev_sum1[:], op0=ALU.mult, op1=ALU.mult)
         y_rows = tile("y_rows", [P, D, P])
-        y_sum_turned = reuse.tile([P, P], F32, name="y_sum_turned", offset=3 * win_bytes + 2048)
-        y_sum_back = region(h_bank[0], 3)
         for c in (2, 3):
             nc.scalar.copy(y_rows[:, :, chunk_cols(c)].rearrange("p d (v t) -> p d v t", t=SLOTS), members(y_bank[c]))
-        turned_sum(region(h_bank[1], 2), rows_of(y_rows, D))
-        nc.scalar.copy(y_sum_turned[:], region(h_bank[1], 2))
-        turned_sum(y_sum_back, [y_sum_turned[:]])
-        times_a(0)
-        times_a(1)
-        plus_b(0)
-        plus_b(1)
-        make_a(1, gain_a[1])
-        make_b(1)
-        times_a(2)
-        nc.vector.tensor_tensor(offset_b[1][:], y_sum_back, unit_y_sum[1][:], ALU.mult)
-        second_product(0)
-        second_product(1)
-        ay[3] = reuse.tile([P, GROUPS, D, SLOTS], F32, name="ay_last", offset=3 * win_bytes + 2048)
-        times_a(3)
-        plus_b(2)
-        plus_b(3)
-        second_product(2)
-        second_product(3)
+        y_sum0 = tile("y_sum0", [P, P])
+        group_sum(y_sum0, y_bank, 0)
+        group_sum(y_sum0, y_bank, 1)
+
+        spread_root0, spread_q0 = tile("spread_root0", [P, P]), tile("spread_q0", [P, P])
+        mean_sq = shared("mean_sq", [P, HALF], F32, 16384 + 4096)
+        mean_root, mean_q = tile("mean_root", [P, HALF]), tile("mean_q", [P, HALF])
+        mean_scale = 1.0 / (D * math.sqrt(MEAN_NOISE))
+        nc.scalar.activation(spread_root0[:], spread0, ACT.Abs_reciprocal_sqrt, bias=1.0, scale=-1.0)
+        nc.scalar.activation(mean_sq[:, 0:P], mean0, ACT.Square, scale=mean_scale)
+        nc.scalar.activation(mean_sq[:, P:HALF], h_sum[:], ACT.Square, scale=mean_scale)
+        nc.scalar.activation(spread_q0[:], spread_root0[:], ACT.Square)
+        nc.scalar.activation(mean_root[:], mean_sq[:], ACT.Abs_reciprocal_sqrt, bias=1.0)
+        nc.scalar.activation(mean_q[:], mean_root[:], ACT.Square)
+
+        unit8_turned = tile("unit8_turned", [P, P])
+        turned_sum(region(h_bank[3], 2), [unit8[:]])
+        nc.scalar.copy(unit8_turned[:], region(h_bank[3], 2))
+        spread1, y_sum1_turned = region(h_bank[1], 1), region(h_bank[2], 0)
+        turned_sum(spread1, rows_of(sq[1]) + [neg_dev_sq[:]])
+        turned_sum(y_sum1_turned, rows_of(y_rows))
+        spread_root1 = shared("spread_root1", [P, P], F32, 4096 - 256)
+        spread_q1_turned = tile("spread_q1_turned", [P, P])
+        nc.scalar.activation(spread_root1[:], spread1, ACT.Abs_reciprocal_sqrt, bias=1.0, scale=1.0 / (D * VAR_NOISE))
+        nc.scalar.activation(spread_q1_turned[:], spread_root1[:], ACT.Square)
+        spread_q1, unit_mean1 = region(h_bank[0], 3), region(h_bank[3], 0)
+        turned_sum(spread_q1, [spread_q1_turned[:]])
+
+        gain = [shared("gain0", [P, P], F32, 10240), tile("gain1", [P, P])]
+        bias = [shared("bias0", [P, P], F32, 10752), tile("bias1", [P, P])]
+        q_diff = [tile("q_diff0", [P, P]), shared("q_diff1", [P, P], F32, 8192)]
+        unit_mean0, unit_mean1_turned = tile("unit_mean0", [P, P]), tile("unit_mean1_turned", [P, P])
+        ay = [tile("ay%d" % c, [P, GROUPS, D, SLOTS]) for c in range(4)]
+        z_bf = [tile("z_bf0", [P, GROUPS, D, SLOTS], BF16)[:], tile("z_bf1", [P, OWN_GROUPS, D, SLOTS], BF16)[:], tile("z_bf2", [P, GROUPS, D, SLOTS], BF16)[:], tile("z_bf3", [P, GROUPS, D, SLOTS], BF16)[:]]
+
+        z_share = shared("z_share", [P, GROUPS - OWN_GROUPS, D, SLOTS], BF16, 3584)
+
+        def make_gain(a, q):
+            nc.vector.scalar_tensor_tensor(out=by_slot(gain[a][:]), in0=by_slot(q), scalar=-1.0, in1=over_groups(neg_unit), op0=ALU.add, op1=ALU.mult)
+
+        def per_member(g, c, groups):
+            return by_slot(g[c // 2][:, chunk_cols(c)])[:, 0:groups].unsqueeze(2).to_broadcast([P, groups, D, SLOTS])
+
+        def times_gain(c, groups):
+            nc.vector.tensor_tensor(ay[c][:, 0:groups], y_bank[c][:].rearrange("p (t v d) -> p v d t", t=SLOTS, d=D)[:, 0:groups], per_member(gain, c, groups), ALU.mult)
+
+        def plus_bias(engine, c, groups):
+            engine.tensor_tensor(z_bf[c][:, 0:groups], ay[c][:, 0:groups], per_member(bias, c, groups), ALU.add)
+
+        make_gain(0, spread_q0[:])
+        nc.gpsimd.tensor_tensor(q_diff[0][:], spread_q0[:], mean_q[:, 0:P], ALU.subtract)
+        nc.gpsimd.tensor_tensor(unit_mean0[:], y_sum0[:], unit8[:], ALU.mult)
+        times_gain(0, GROUPS)
+        nc.gpsimd.tensor_tensor(bias[0][:], q_diff[0][:], unit_mean0[:], ALU.mult)
+        times_gain(1, OWN_GROUPS)
+        plus_bias(nc.gpsimd, 0, GROUPS)
+        plus_bias(nc.gpsimd, 1, OWN_GROUPS)
+        for v in range(OWN_GROUPS, GROUPS):
+            for t in range(SLOTS):
+                col = CHUNK_COLS + SLOTS * v + t
+                nc.scalar.activation(z_share[:, v - OWN_GROUPS, :, t], y_bank[1][:, P * t + D * v : P * t + D * (v + 1)], ACT.Identity,
+                                     bias=bias[0][:, col : col + 1], scale=gain[0][:, col : col + 1])
+        nc.vector.tensor_tensor(unit_mean1_turned[:], y_sum1_turned, unit8_turned[:], ALU.mult)
+        turned_sum(unit_mean1, [unit_mean1_turned[:]])
+        make_gain(1, spread_q1)
+        nc.vector.tensor_tensor(q_diff[1][:], spread_q1, mean_q[:, P:HALF], ALU.subtract)
+        times_gain(2, GROUPS)
+        nc.vector.tensor_tensor(bias[1][:], unit_mean1, q_diff[1][:], ALU.mult)
+        times_gain(3, GROUPS)
+        plus_bias(nc.vector, 2, GROUPS)
+
+        def second_product(name, codes, z, cols, acc, queue, res):
+            width = cols.stop - cols.start
+            scales = tile(name + "_sc", [P, width], U8)
+            part = width // len(z)
+            for n, piece in enumerate(z):
+                nc.vector.quantize_mx(out=codes[:, part * n : part * (n + 1)].bitcast(FP8X4), scales=scales[:, part * n : part * (n + 1)],
+                                      in_=piece.rearrange("p v d t -> p (v d t)"))
+            nc.tensor.matmul_mx(out=acc, lhsT=w2_codes[:].bitcast(FP8X4), lhsT_scale=w2_sc[:],
+                                rhs=codes[:].bitcast(FP8X4), rhs_scale=scales[:], start=True, stop=True)
+            nc.scalar.copy(res[:], acc)
+            queue.dma_start(out[:, cols], res[:])
+
+        second_product("first", shared("first_codes", [P, P], U32, 8192 - 256), [z_bf[0]],
+                       slice(0, P), region(h_bank[3], 1), nc.sync, tile("res0", [P, P]))
+        plus_bias(nc.vector, 3, GROUPS)
+        second_product("third", tile("third_codes", [P, P], U32), [z_bf[2]],
+                       slice(2 * P, 3 * P), region(h_bank[2], 1), nc.sync, shared("res2", [P, P], F32, 10240))
+        second_product("second", shared("second_codes", [P, P], U32, 8192 + 256), [z_bf[1], z_share[:]],
+                       slice(P, 2 * P), region(h_bank[1], 3), nc.sync, tile("res1", [P, P]))
+        second_product("fourth", tile("fourth_codes", [P, P], U32), [z_bf[3]],
+                       slice(3 * P, 4 * P), region(h_bank[0], 0), nc.scalar, shared("res3", [P, P], F32, 10752))

@@ -26,7 +26,7 @@ HALF = 2 * P
 MEAN_NOISE, VAR_NOISE = 0.2, 0.3
 E_PLANE, X_PLANE = 0, 4
 WARM_PASSES = 4
-OWN_GROUPS = 8
+OWN_GROUPS = 10
 
 
 def tile_picked_ywien_wien_p_kernel(tc, x_words, x_scales, e_words, e_scales, w1, unit, w2, offs, out):
@@ -48,7 +48,7 @@ def tile_picked_ywien_wien_p_kernel(tc, x_words, x_scales, e_words, e_scales, w1
 
         e_scale_win = tile("e_scale_win", [P, T], U8)
         x_scale_win = tile("x_scale_win", [P, T], U8)
-        e_word_win = tile("e_word_win", [P, T], I32)
+        e_word_win = shared("e_word_win", [P, T], I32, 24576)
         x_word_win = shared("x_word_win", [P, T], I32, 16384)
         w1_raw = [tile("w1_raw%d" % part, [P, SLOTS, HALF]) for part in range(2)]
         w2_raw = tile("w2_raw", [P, SLOTS, N])
@@ -89,9 +89,9 @@ def tile_picked_ywien_wien_p_kernel(tc, x_words, x_scales, e_words, e_scales, w1
         nc.vector.tensor_copy(e_sc_picked[:], e_scale_win[:].indirect(offsets[:]))
         nc.vector.tensor_copy(x_sc[:], x_scale_win[:].indirect(offsets[:]))
         place_scales(e_sc, e_sc_picked, E_PLANE)
+        nc.sync.dma_start(w2_raw[:], w2.rearrange("(p j) m -> p j m", j=SLOTS))
         load_words(x_word_win, x_words)
         nc.sync.dma_start(unit_sb[:], unit.rearrange("(p t) o -> p (t o)", t=SLOTS))
-        nc.sync.dma_start(w2_raw[:], w2.rearrange("(p j) m -> p j m", j=SLOTS))
 
         def by_slot(x):
             return x.rearrange("p (v t) -> p v t", t=SLOTS)
@@ -123,11 +123,11 @@ def tile_picked_ywien_wien_p_kernel(tc, x_words, x_scales, e_words, e_scales, w1
         w1_bf = tile("w1_bf", [P, SLOTS, P, SLOTS], BF16)
         w1_codes = tile("w1_codes", [P, SLOTS, P], U32)
         w1_sc = tile("w1_sc", [P, SLOTS, P], U8)
-        w2_codes = tile("w2_codes", [P, N], U32)
+        w2_codes = shared("w2_codes", [P, N], U32, 16384)
         w2_sc = tile("w2_sc", [P, N], U8)
         for part in range(2):
-            nc.scalar.copy(w1_bf[:].rearrange("p t m j -> p m t j")[:, 64 * part : 64 * (part + 1)],
-                           w1_raw[part][:].rearrange("p j (m t) -> p m t j", t=SLOTS))
+            nc.scalar.copy(w1_bf[:].rearrange("p t m j -> p m j t")[:, 64 * part : 64 * (part + 1)],
+                           w1_raw[part][:].rearrange("p j (m t) -> p m j t", t=SLOTS))
         for t0 in (0, 2):
             nc.vector.quantize_mx(
                 out=w1_codes[:, t0 : t0 + 2, :].rearrange("p t m -> p (t m)").bitcast(FP8X4),
@@ -194,7 +194,7 @@ def tile_picked_ywien_wien_p_kernel(tc, x_words, x_scales, e_words, e_scales, w1
         square(1)
         gather_words(x_codes, tile("x_codes2", [P, HALF], U32), x_word_win, 2)
         gather_words(x_codes, tile("x_codes0", [P, HALF], U32), x_word_win, 0)
-        w2_bf = shared("w2_bf", [P, N, SLOTS], BF16, 16384 + 1024)
+        w2_bf = shared("w2_bf", [P, N, SLOTS], BF16, 24576)
         nc.gpsimd.tensor_copy(w2_bf[:], w2_raw[:].rearrange("p j m -> p m j"))
         nc.scalar.activation(pivot8_turned[:], region(y_bank[0], 0), ACT.Copy, scale=float(D))
         square(2)
@@ -216,7 +216,7 @@ def tile_picked_ywien_wien_p_kernel(tc, x_words, x_scales, e_words, e_scales, w1
         for c in (0, 1):
             first_product(y_bank, x_codes, x_sc, X_PLANE, c)
 
-        h_sum, dev_sum1, neg_dev_sq = shared("h_sum", [P, P], F32, 16384), tile("dev_sum1", [P, P]), tile("neg_dev_sq", [P, P])
+        h_sum, dev_sum1, neg_dev_sq = shared("h_sum", [P, P], F32, 16384 + 2048), tile("dev_sum1", [P, P]), tile("neg_dev_sq", [P, P])
         group_sum(h_sum, h_bank, 2)
         group_sum(h_sum, h_bank, 3)
         nc.vector.scalar_tensor_tensor(out=dev_sum1[:], in0=pivot[1][:], scalar=-float(D), in1=h_sum[:], op0=ALU.mult, op1=ALU.add)
@@ -240,27 +240,25 @@ def tile_picked_ywien_wien_p_kernel(tc, x_words, x_scales, e_words, e_scales, w1
         nc.scalar.activation(mean_root[:], mean_sq[:], ACT.Abs_reciprocal_sqrt, bias=1.0)
         nc.scalar.activation(mean_q[:], mean_root[:], ACT.Square)
 
-        unit8_turned = tile("unit8_turned", [P, P])
-        turned_sum(region(h_bank[3], 2), [unit8[:]])
-        nc.scalar.copy(unit8_turned[:], region(h_bank[3], 2))
         spread1, y_sum1_turned = region(h_bank[1], 1), region(h_bank[2], 0)
         turned_sum(spread1, rows_of(sq[1]) + [neg_dev_sq[:]])
         turned_sum(y_sum1_turned, rows_of(y_rows))
+        unit8_turned, mean_q1_turned = region(h_bank[3], 2), region(h_bank[3], 3)
+        turned_sum(unit8_turned, [unit8[:]])
+        turned_sum(mean_q1_turned, [mean_q[:, P:HALF]])
         spread_root1 = shared("spread_root1", [P, P], F32, 4096 - 256)
         spread_q1_turned = tile("spread_q1_turned", [P, P])
         nc.scalar.activation(spread_root1[:], spread1, ACT.Abs_reciprocal_sqrt, bias=1.0, scale=1.0 / (D * VAR_NOISE))
         nc.scalar.activation(spread_q1_turned[:], spread_root1[:], ACT.Square)
-        spread_q1, unit_mean1 = region(h_bank[0], 3), region(h_bank[3], 0)
+        spread_q1, bias1 = region(h_bank[0], 3), region(h_bank[0], 0)
         turned_sum(spread_q1, [spread_q1_turned[:]])
 
         gain = [shared("gain0", [P, P], F32, 10240), tile("gain1", [P, P])]
-        bias = [shared("bias0", [P, P], F32, 10752), tile("bias1", [P, P])]
-        q_diff = [tile("q_diff0", [P, P]), shared("q_diff1", [P, P], F32, 8192)]
-        unit_mean0, unit_mean1_turned = tile("unit_mean0", [P, P]), tile("unit_mean1_turned", [P, P])
-        ay = [tile("ay%d" % c, [P, GROUPS, D, SLOTS]) for c in range(4)]
-        z_bf = [tile("z_bf0", [P, GROUPS, D, SLOTS], BF16)[:], tile("z_bf1", [P, OWN_GROUPS, D, SLOTS], BF16)[:], tile("z_bf2", [P, GROUPS, D, SLOTS], BF16)[:], tile("z_bf3", [P, GROUPS, D, SLOTS], BF16)[:]]
-
-        z_share = shared("z_share", [P, GROUPS - OWN_GROUPS, D, SLOTS], BF16, 3584)
+        bias = [shared("bias0", [P, P], F32, 10752), bias1]
+        q_diff = [tile("q_diff0", [P, P]), tile("q_diff1", [P, P])]
+        unit_mean0, unit_diff1, bias1_turned = tile("unit_mean0", [P, P]), tile("unit_diff1", [P, P]), tile("bias1_turned", [P, P])
+        ay = [shared("ay2", [P, GROUPS, D, SLOTS], F32, 12288) if c == 2 else tile("ay%d" % c, [P, GROUPS, D, SLOTS]) for c in range(4)]
+        z_bf = [tile("z_bf0", [P, GROUPS, D, SLOTS], BF16)[:], shared("z_bf1", [P, GROUPS * D * SLOTS], BF16, 3072)[:].rearrange("p (v d t) -> p v d t", d=D, t=SLOTS), tile("z_bf2", [P, GROUPS, D, SLOTS], BF16)[:], tile("z_bf3", [P, GROUPS, D, SLOTS], BF16)[:]]
 
         def make_gain(a, q):
             nc.vector.scalar_tensor_tensor(out=by_slot(gain[a][:]), in0=by_slot(q), scalar=-1.0, in1=over_groups(neg_unit), op0=ALU.add, op1=ALU.mult)
@@ -285,14 +283,14 @@ def tile_picked_ywien_wien_p_kernel(tc, x_words, x_scales, e_words, e_scales, w1
         for v in range(OWN_GROUPS, GROUPS):
             for t in range(SLOTS):
                 col = CHUNK_COLS + SLOTS * v + t
-                nc.scalar.activation(z_share[:, v - OWN_GROUPS, :, t], y_bank[1][:, P * t + D * v : P * t + D * (v + 1)], ACT.Identity,
+                nc.scalar.activation(z_bf[1][:, v, :, t], y_bank[1][:, P * t + D * v : P * t + D * (v + 1)], ACT.Identity,
                                      bias=bias[0][:, col : col + 1], scale=gain[0][:, col : col + 1])
-        nc.vector.tensor_tensor(unit_mean1_turned[:], y_sum1_turned, unit8_turned[:], ALU.mult)
-        turned_sum(unit_mean1, [unit_mean1_turned[:]])
+        nc.vector.tensor_tensor(q_diff[1][:], spread_q1_turned[:], mean_q1_turned, ALU.subtract)
         make_gain(1, spread_q1)
-        nc.vector.tensor_tensor(q_diff[1][:], spread_q1, mean_q[:, P:HALF], ALU.subtract)
+        nc.vector.tensor_tensor(unit_diff1[:], unit8_turned, q_diff[1][:], ALU.mult)
         times_gain(2, GROUPS)
-        nc.vector.tensor_tensor(bias[1][:], unit_mean1, q_diff[1][:], ALU.mult)
+        nc.vector.tensor_tensor(bias1_turned[:], y_sum1_turned, unit_diff1[:], ALU.mult)
+        turned_sum(bias1, [bias1_turned[:]])
         times_gain(3, GROUPS)
         plus_bias(nc.vector, 2, GROUPS)
 
@@ -308,12 +306,12 @@ def tile_picked_ywien_wien_p_kernel(tc, x_words, x_scales, e_words, e_scales, w1
             nc.scalar.copy(res[:], acc)
             queue.dma_start(out[:, cols], res[:])
 
-        second_product("first", shared("first_codes", [P, P], U32, 8192 - 256), [z_bf[0]],
-                       slice(0, P), region(h_bank[3], 1), nc.sync, tile("res0", [P, P]))
         plus_bias(nc.vector, 3, GROUPS)
         second_product("third", tile("third_codes", [P, P], U32), [z_bf[2]],
                        slice(2 * P, 3 * P), region(h_bank[2], 1), nc.sync, shared("res2", [P, P], F32, 10240))
-        second_product("second", shared("second_codes", [P, P], U32, 8192 + 256), [z_bf[1], z_share[:]],
+        second_product("first", shared("first_codes", [P, P], U32, 12288), [z_bf[0]],
+                       slice(0, P), region(h_bank[3], 1), nc.sync, tile("res0", [P, P]))
+        second_product("second", shared("second_codes", [P, P], U32, 12288 + 512), [z_bf[1]],
                        slice(P, 2 * P), region(h_bank[1], 3), nc.sync, tile("res1", [P, P]))
         second_product("fourth", tile("fourth_codes", [P, P], U32), [z_bf[3]],
-                       slice(3 * P, 4 * P), region(h_bank[0], 0), nc.scalar, shared("res3", [P, P], F32, 10752))
+                       slice(3 * P, 4 * P), region(h_bank[0], 1), nc.scalar, shared("res3", [P, P], F32, 10752))

@@ -25,7 +25,7 @@ CHUNK_COLS = GROUPS * SLOTS
 HALF = 2 * P
 MEAN_NOISE, VAR_NOISE = 0.2, 0.3
 E_PLANE, X_PLANE = 0, 4
-WARM_PASSES = 4
+WARM_PASSES = 2
 OWN_GROUPS = 10
 
 
@@ -48,7 +48,7 @@ def tile_picked_ywien_wien_p_kernel(tc, x_words, x_scales, e_words, e_scales, w1
 
         e_scale_win = tile("e_scale_win", [P, T], U8)
         x_scale_win = tile("x_scale_win", [P, T], U8)
-        e_word_win = shared("e_word_win", [P, T], I32, 24576)
+        e_word_win = tile("e_word_win", [P, T], I32)
         x_word_win = shared("x_word_win", [P, T], I32, 16384)
         w1_raw = [tile("w1_raw%d" % part, [P, SLOTS, HALF]) for part in range(2)]
         w2_raw = tile("w2_raw", [P, SLOTS, N])
@@ -86,12 +86,12 @@ def tile_picked_ywien_wien_p_kernel(tc, x_words, x_scales, e_words, e_scales, w1
             nc.sync.dma_start(x_scale_win[X_PLANE + r : P : 32, :].bitcast(I32), x_scales[0][r:16:4, :].bitcast(I32))
         load_w1(1)
         load_words(e_word_win, e_words)
+        nc.sync.dma_start(unit_sb[:], unit.rearrange("(p t) o -> p (t o)", t=SLOTS))
         nc.vector.tensor_copy(e_sc_picked[:], e_scale_win[:].indirect(offsets[:]))
         nc.vector.tensor_copy(x_sc[:], x_scale_win[:].indirect(offsets[:]))
         place_scales(e_sc, e_sc_picked, E_PLANE)
-        nc.sync.dma_start(w2_raw[:], w2.rearrange("(p j) m -> p j m", j=SLOTS))
         load_words(x_word_win, x_words)
-        nc.sync.dma_start(unit_sb[:], unit.rearrange("(p t) o -> p (t o)", t=SLOTS))
+        nc.sync.dma_start(w2_raw[:], w2.rearrange("(p j) m -> p j m", j=SLOTS))
 
         def by_slot(x):
             return x.rearrange("p (v t) -> p v t", t=SLOTS)
@@ -134,10 +134,6 @@ def tile_picked_ywien_wien_p_kernel(tc, x_words, x_scales, e_words, e_scales, w1
                 scales=w1_sc[:, t0 : t0 + 2, :].rearrange("p t m -> p (t m)"),
                 in_=w1_bf[:, t0 : t0 + 2].rearrange("p t m j -> p (t m j)"),
             )
-        for n in range(WARM_PASSES):
-            nc.tensor.matmul_mx(out=y_bank[2 + n // 2][:, HALF * (n % 2) : HALF * (n % 2 + 1)], lhsT=w1_codes[:, 0, :].bitcast(FP8X4), lhsT_scale=w1_sc[:, 0, :],
-                                rhs=w1_codes[:, 0:2, :].rearrange("p t m -> p (t m)").bitcast(FP8X4),
-                                rhs_scale=w1_sc[:, 0:2, :].rearrange("p t m -> p (t m)"), start=True, stop=True)
 
         e_codes, x_codes = {}, {}
 
@@ -194,15 +190,21 @@ def tile_picked_ywien_wien_p_kernel(tc, x_words, x_scales, e_words, e_scales, w1
         square(1)
         gather_words(x_codes, tile("x_codes2", [P, HALF], U32), x_word_win, 2)
         gather_words(x_codes, tile("x_codes0", [P, HALF], U32), x_word_win, 0)
-        w2_bf = shared("w2_bf", [P, N, SLOTS], BF16, 24576)
+        w2_bf = tile("w2_bf", [P, N, SLOTS], BF16)
         nc.gpsimd.tensor_copy(w2_bf[:], w2_raw[:].rearrange("p j m -> p m j"))
         nc.scalar.activation(pivot8_turned[:], region(y_bank[0], 0), ACT.Copy, scale=float(D))
         square(2)
         square(3)
 
         dev_sum, dev_sum_sq = tile("dev_sum", [P, P]), tile("dev_sum_sq", [P, P])
+        for n in range(WARM_PASSES):
+            nc.tensor.matmul_mx(out=h_bank[0][:], lhsT=w1_codes[:, 0, :].bitcast(FP8X4), lhsT_scale=w1_sc[:, 0, :],
+                                rhs=w1_codes[:].rearrange("p t m -> p (t m)").bitcast(FP8X4),
+                                rhs_scale=w1_sc[:].rearrange("p t m -> p (t m)"), start=True, stop=True)
         turned_sum(region(h_bank[0], 0), rows_of(dev[0]))
         turned_sum(region(h_bank[1], 0), rows_of(sq[0]))
+        unit8_turned = region(h_bank[1], 2)
+        turned_sum(unit8_turned, [unit8[:]])
         nc.scalar.activation(dev_sum_sq[:], region(h_bank[0], 0), ACT.Square, scale=1.0 / (D * math.sqrt(VAR_NOISE)))
         nc.scalar.copy(dev_sum[:], region(h_bank[0], 0))
 
@@ -216,16 +218,16 @@ def tile_picked_ywien_wien_p_kernel(tc, x_words, x_scales, e_words, e_scales, w1
         for c in (0, 1):
             first_product(y_bank, x_codes, x_sc, X_PLANE, c)
 
-        h_sum, dev_sum1, neg_dev_sq = shared("h_sum", [P, P], F32, 16384 + 2048), tile("dev_sum1", [P, P]), tile("neg_dev_sq", [P, P])
+        h_sum, dev_sum1, neg_dev_sq = tile("h_sum", [P, P]), tile("dev_sum1", [P, P]), tile("neg_dev_sq", [P, P])
         group_sum(h_sum, h_bank, 2)
         group_sum(h_sum, h_bank, 3)
-        nc.vector.scalar_tensor_tensor(out=dev_sum1[:], in0=pivot[1][:], scalar=-float(D), in1=h_sum[:], op0=ALU.mult, op1=ALU.add)
         nc.vector.quantize_mx(out=w2_codes[:].bitcast(FP8X4), scales=w2_sc[:], in_=w2_bf[:].rearrange("p m j -> p (m j)"))
-        nc.vector.scalar_tensor_tensor(out=neg_dev_sq[:], in0=dev_sum1[:], scalar=-1.0 / D, in1=dev_sum1[:], op0=ALU.mult, op1=ALU.mult)
+        nc.vector.scalar_tensor_tensor(out=dev_sum1[:], in0=pivot[1][:], scalar=-float(D), in1=h_sum[:], op0=ALU.mult, op1=ALU.add)
         y_rows = tile("y_rows", [P, D, P])
         for c in (2, 3):
             nc.scalar.copy(y_rows[:, :, chunk_cols(c)].rearrange("p d (v t) -> p d v t", t=SLOTS), members(y_bank[c]))
         y_sum0 = tile("y_sum0", [P, P])
+        nc.vector.scalar_tensor_tensor(out=neg_dev_sq[:], in0=dev_sum1[:], scalar=-1.0 / D, in1=dev_sum1[:], op0=ALU.mult, op1=ALU.mult)
         group_sum(y_sum0, y_bank, 0)
         group_sum(y_sum0, y_bank, 1)
 
@@ -243,8 +245,7 @@ def tile_picked_ywien_wien_p_kernel(tc, x_words, x_scales, e_words, e_scales, w1
         spread1, y_sum1_turned = region(h_bank[1], 1), region(h_bank[2], 0)
         turned_sum(spread1, rows_of(sq[1]) + [neg_dev_sq[:]])
         turned_sum(y_sum1_turned, rows_of(y_rows))
-        unit8_turned, mean_q1_turned = region(h_bank[3], 2), region(h_bank[3], 3)
-        turned_sum(unit8_turned, [unit8[:]])
+        mean_q1_turned = region(h_bank[3], 3)
         turned_sum(mean_q1_turned, [mean_q[:, P:HALF]])
         spread_root1 = shared("spread_root1", [P, P], F32, 4096 - 256)
         spread_q1_turned = tile("spread_q1_turned", [P, P])
@@ -257,7 +258,7 @@ def tile_picked_ywien_wien_p_kernel(tc, x_words, x_scales, e_words, e_scales, w1
         bias = [shared("bias0", [P, P], F32, 10752), bias1]
         q_diff = [tile("q_diff0", [P, P]), tile("q_diff1", [P, P])]
         unit_mean0, unit_diff1, bias1_turned = tile("unit_mean0", [P, P]), tile("unit_diff1", [P, P]), tile("bias1_turned", [P, P])
-        ay = [shared("ay2", [P, GROUPS, D, SLOTS], F32, 12288) if c == 2 else tile("ay%d" % c, [P, GROUPS, D, SLOTS]) for c in range(4)]
+        ay = [tile("ay0", [P, GROUPS, D, SLOTS]), shared("ay1", [P, GROUPS, D, SLOTS], F32, 4096), shared("ay2", [P, GROUPS, D, SLOTS], F32, 12288), tile("ay3", [P, GROUPS, D, SLOTS])]
         z_bf = [tile("z_bf0", [P, GROUPS, D, SLOTS], BF16)[:], shared("z_bf1", [P, GROUPS * D * SLOTS], BF16, 3072)[:].rearrange("p (v d t) -> p v d t", d=D, t=SLOTS), tile("z_bf2", [P, GROUPS, D, SLOTS], BF16)[:], tile("z_bf3", [P, GROUPS, D, SLOTS], BF16)[:]]
 
         def make_gain(a, q):
@@ -277,6 +278,7 @@ def tile_picked_ywien_wien_p_kernel(tc, x_words, x_scales, e_words, e_scales, w1
         nc.gpsimd.tensor_tensor(unit_mean0[:], y_sum0[:], unit8[:], ALU.mult)
         times_gain(0, GROUPS)
         nc.gpsimd.tensor_tensor(bias[0][:], q_diff[0][:], unit_mean0[:], ALU.mult)
+        nc.vector.tensor_tensor(q_diff[1][:], spread_q1_turned[:], mean_q1_turned, ALU.subtract)
         times_gain(1, OWN_GROUPS)
         plus_bias(nc.gpsimd, 0, GROUPS)
         plus_bias(nc.gpsimd, 1, OWN_GROUPS)
@@ -285,12 +287,11 @@ def tile_picked_ywien_wien_p_kernel(tc, x_words, x_scales, e_words, e_scales, w1
                 col = CHUNK_COLS + SLOTS * v + t
                 nc.scalar.activation(z_bf[1][:, v, :, t], y_bank[1][:, P * t + D * v : P * t + D * (v + 1)], ACT.Identity,
                                      bias=bias[0][:, col : col + 1], scale=gain[0][:, col : col + 1])
-        nc.vector.tensor_tensor(q_diff[1][:], spread_q1_turned[:], mean_q1_turned, ALU.subtract)
-        make_gain(1, spread_q1)
         nc.vector.tensor_tensor(unit_diff1[:], unit8_turned, q_diff[1][:], ALU.mult)
-        times_gain(2, GROUPS)
+        make_gain(1, spread_q1)
         nc.vector.tensor_tensor(bias1_turned[:], y_sum1_turned, unit_diff1[:], ALU.mult)
         turned_sum(bias1, [bias1_turned[:]])
+        times_gain(2, GROUPS)
         times_gain(3, GROUPS)
         plus_bias(nc.vector, 2, GROUPS)
 

@@ -25,7 +25,7 @@ CHUNK_COLS = GROUPS * SLOTS
 HALF = 2 * P
 MEAN_NOISE, VAR_NOISE = 0.2, 0.3
 E_PLANE, X_PLANE = 0, 4
-WARM_PASSES = 2
+WARM_PASSES = 4
 OWN_GROUPS = 10
 
 
@@ -50,17 +50,16 @@ def tile_picked_ywien_wien_p_kernel(tc, x_words, x_scales, e_words, e_scales, w1
         x_scale_win = tile("x_scale_win", [P, T], U8)
         e_word_win = tile("e_word_win", [P, T], I32)
         x_word_win = shared("x_word_win", [P, T], I32, 16384)
-        w1_raw = [tile("w1_raw%d" % part, [P, SLOTS, HALF]) for part in range(2)]
+        w1_raw = [tile("w1_raw0", [P, SLOTS, HALF]), shared("w1_raw1", [P, SLOTS, HALF], F32, 24576)]
         w2_raw = tile("w2_raw", [P, SLOTS, N])
         unit_sb = tile("unit_sb", [P, SLOTS])
         ident = tile("ident", [P, P])
         warm = tile("warm", [P, 1])
-        e_sc, e_sc_picked, x_sc = (tile(nm, [P, S], U8) for nm in ("e_sc", "e_sc_picked", "x_sc"))
+        e_sc, x_sc_picked = (tile(nm, [P, S], U8) for nm in ("e_sc", "x_sc_picked"))
 
-        nc.gpsimd.memset(e_scale_win[:].bitcast(I32), 0)
+        nc.gpsimd.memset(x_scale_win[:].bitcast(I32), 0)
         nc.vector.memset(warm[:], 1.0)
-        nc.vector.memset(x_scale_win[:].bitcast(I32), 0)
-        nc.gpsimd.memset(e_sc[:].bitcast(I32), 0)
+        nc.vector.memset(e_scale_win[:].bitcast(I32), 0)
         nc.scalar.activation(warm[:], warm[:], ACT.Abs_reciprocal_sqrt)
         make_identity(nc, ident[:])
 
@@ -69,7 +68,7 @@ def tile_picked_ywien_wien_p_kernel(tc, x_words, x_scales, e_words, e_scales, w1
 
         def place_scales(dst, picked, plane):
             for r in range(4):
-                nc.sync.dma_start(dst[plane + r : P : 32, :].bitcast(I32), picked[plane + 8 * r : P : 32, :].bitcast(I32))
+                nc.scalar.dma_start(dst[plane + r : P : 32, :].bitcast(I32), picked[plane + 8 * r : P : 32, :].bitcast(I32))
 
         def load_words(win, src):
             nc.sync.dma_start(win[:], src[0].rearrange("p n t -> p (n t)").bitcast(I32))
@@ -81,17 +80,16 @@ def tile_picked_ywien_wien_p_kernel(tc, x_words, x_scales, e_words, e_scales, w1
 
         nc.sync.dma_start(offsets[:], offs)
         load_w1(0)
-        load_scales(e_scale_win, e_scales, E_PLANE)
+        load_scales(x_scale_win, x_scales, X_PLANE)
         for r in range(4):
-            nc.sync.dma_start(x_scale_win[X_PLANE + r : P : 32, :].bitcast(I32), x_scales[0][r:16:4, :].bitcast(I32))
+            nc.sync.dma_start(e_scale_win[E_PLANE + r : P : 32, :].bitcast(I32), e_scales[0][r:16:4, :].bitcast(I32))
         load_w1(1)
         load_words(e_word_win, e_words)
-        nc.sync.dma_start(unit_sb[:], unit.rearrange("(p t) o -> p (t o)", t=SLOTS))
-        nc.vector.tensor_copy(e_sc_picked[:], e_scale_win[:].indirect(offsets[:]))
-        nc.vector.tensor_copy(x_sc[:], x_scale_win[:].indirect(offsets[:]))
-        place_scales(e_sc, e_sc_picked, E_PLANE)
+        nc.vector.tensor_copy(x_sc_picked[:], x_scale_win[:].indirect(offsets[:]))
+        nc.vector.tensor_copy(e_sc[:], e_scale_win[:].indirect(offsets[:]))
         load_words(x_word_win, x_words)
         nc.sync.dma_start(w2_raw[:], w2.rearrange("(p j) m -> p j m", j=SLOTS))
+        nc.sync.dma_start(unit_sb[:], unit.rearrange("(p t) o -> p (t o)", t=SLOTS))
 
         def by_slot(x):
             return x.rearrange("p (v t) -> p v t", t=SLOTS)
@@ -128,12 +126,20 @@ def tile_picked_ywien_wien_p_kernel(tc, x_words, x_scales, e_words, e_scales, w1
         for part in range(2):
             nc.scalar.copy(w1_bf[:].rearrange("p t m j -> p m j t")[:, 64 * part : 64 * (part + 1)],
                            w1_raw[part][:].rearrange("p j (m t) -> p m j t", t=SLOTS))
+        x_sc = shared("x_sc", [P, S], U8, 24576)
+        nc.gpsimd.memset(x_sc[:].bitcast(I32), 0)
+        place_scales(x_sc, x_sc_picked, X_PLANE)
         for t0 in (0, 2):
             nc.vector.quantize_mx(
                 out=w1_codes[:, t0 : t0 + 2, :].rearrange("p t m -> p (t m)").bitcast(FP8X4),
                 scales=w1_sc[:, t0 : t0 + 2, :].rearrange("p t m -> p (t m)"),
                 in_=w1_bf[:, t0 : t0 + 2].rearrange("p t m j -> p (t m j)"),
             )
+
+        for n in range(WARM_PASSES):
+            nc.tensor.matmul_mx(out=y_bank[2 + n // 2][:, HALF * (n % 2) : HALF * (n % 2 + 1)], lhsT=w1_codes[:, 0, :].bitcast(FP8X4), lhsT_scale=w1_sc[:, 0, :],
+                                rhs=w1_codes[:, 0:2, :].rearrange("p t m -> p (t m)").bitcast(FP8X4),
+                                rhs_scale=w1_sc[:, 0:2, :].rearrange("p t m -> p (t m)"), start=True, stop=True)
 
         e_codes, x_codes = {}, {}
 
@@ -197,14 +203,8 @@ def tile_picked_ywien_wien_p_kernel(tc, x_words, x_scales, e_words, e_scales, w1
         square(3)
 
         dev_sum, dev_sum_sq = tile("dev_sum", [P, P]), tile("dev_sum_sq", [P, P])
-        for n in range(WARM_PASSES):
-            nc.tensor.matmul_mx(out=h_bank[0][:], lhsT=w1_codes[:, 0, :].bitcast(FP8X4), lhsT_scale=w1_sc[:, 0, :],
-                                rhs=w1_codes[:].rearrange("p t m -> p (t m)").bitcast(FP8X4),
-                                rhs_scale=w1_sc[:].rearrange("p t m -> p (t m)"), start=True, stop=True)
         turned_sum(region(h_bank[0], 0), rows_of(dev[0]))
         turned_sum(region(h_bank[1], 0), rows_of(sq[0]))
-        unit8_turned = region(h_bank[1], 2)
-        turned_sum(unit8_turned, [unit8[:]])
         nc.scalar.activation(dev_sum_sq[:], region(h_bank[0], 0), ACT.Square, scale=1.0 / (D * math.sqrt(VAR_NOISE)))
         nc.scalar.copy(dev_sum[:], region(h_bank[0], 0))
 
@@ -226,12 +226,11 @@ def tile_picked_ywien_wien_p_kernel(tc, x_words, x_scales, e_words, e_scales, w1
         y_rows = tile("y_rows", [P, D, P])
         for c in (2, 3):
             nc.scalar.copy(y_rows[:, :, chunk_cols(c)].rearrange("p d (v t) -> p d v t", t=SLOTS), members(y_bank[c]))
-        y_sum0 = tile("y_sum0", [P, P])
+        y_sum = [tile("y_sum0", [P, P])]
         nc.vector.scalar_tensor_tensor(out=neg_dev_sq[:], in0=dev_sum1[:], scalar=-1.0 / D, in1=dev_sum1[:], op0=ALU.mult, op1=ALU.mult)
-        group_sum(y_sum0, y_bank, 0)
-        group_sum(y_sum0, y_bank, 1)
+        group_sum(y_sum[0], y_bank, 0)
 
-        spread_root0, spread_q0 = tile("spread_root0", [P, P]), tile("spread_q0", [P, P])
+        spread_root0, spread_q0 = shared("spread_root0", [P, P], F32, 0), tile("spread_q0", [P, P])
         mean_sq = shared("mean_sq", [P, HALF], F32, 16384 + 4096)
         mean_root, mean_q = tile("mean_root", [P, HALF]), tile("mean_q", [P, HALF])
         mean_scale = 1.0 / (D * math.sqrt(MEAN_NOISE))
@@ -245,7 +244,8 @@ def tile_picked_ywien_wien_p_kernel(tc, x_words, x_scales, e_words, e_scales, w1
         spread1, y_sum1_turned = region(h_bank[1], 1), region(h_bank[2], 0)
         turned_sum(spread1, rows_of(sq[1]) + [neg_dev_sq[:]])
         turned_sum(y_sum1_turned, rows_of(y_rows))
-        mean_q1_turned = region(h_bank[3], 3)
+        unit8_turned, mean_q1_turned = region(h_bank[3], 2), region(h_bank[3], 3)
+        turned_sum(unit8_turned, [unit8[:]])
         turned_sum(mean_q1_turned, [mean_q[:, P:HALF]])
         spread_root1 = shared("spread_root1", [P, P], F32, 4096 - 256)
         spread_q1_turned = tile("spread_q1_turned", [P, P])
@@ -274,8 +274,11 @@ def tile_picked_ywien_wien_p_kernel(tc, x_words, x_scales, e_words, e_scales, w1
             engine.tensor_tensor(z_bf[c][:, 0:groups], ay[c][:, 0:groups], per_member(bias, c, groups), ALU.add)
 
         make_gain(0, spread_q0[:])
+        y_sum.append(shared("y_sum1", [P, P], F32, 0))
+        group_sum(y_sum[1], y_bank, 1)
+        nc.gpsimd.tensor_tensor(unit_mean0[:, chunk_cols(0)], y_sum[0][:, chunk_cols(0)], unit8[:, chunk_cols(0)], ALU.mult)
         nc.gpsimd.tensor_tensor(q_diff[0][:], spread_q0[:], mean_q[:, 0:P], ALU.subtract)
-        nc.gpsimd.tensor_tensor(unit_mean0[:], y_sum0[:], unit8[:], ALU.mult)
+        nc.gpsimd.tensor_tensor(unit_mean0[:, chunk_cols(1)], y_sum[1][:, chunk_cols(1)], unit8[:, chunk_cols(1)], ALU.mult)
         times_gain(0, GROUPS)
         nc.gpsimd.tensor_tensor(bias[0][:], q_diff[0][:], unit_mean0[:], ALU.mult)
         nc.vector.tensor_tensor(q_diff[1][:], spread_q1_turned[:], mean_q1_turned, ALU.subtract)

@@ -25,8 +25,8 @@ CHUNK_COLS = GROUPS * SLOTS
 HALF = 2 * P
 MEAN_NOISE, VAR_NOISE = 0.2, 0.3
 E_PLANE, X_PLANE = 0, 4
-WARM_PASSES = 4
-OWN_GROUPS = 10
+WARM_PASSES = 2
+OWN_GROUPS = 9
 
 
 def tile_picked_ywien_wien_p_kernel(tc, x_words, x_scales, e_words, e_scales, w1, unit, w2, offs, out):
@@ -203,6 +203,9 @@ def tile_picked_ywien_wien_p_kernel(tc, x_words, x_scales, e_words, e_scales, w1
         square(3)
 
         dev_sum, dev_sum_sq = tile("dev_sum", [P, P]), tile("dev_sum_sq", [P, P])
+        nc.tensor.matmul_mx(out=h_bank[0][:], lhsT=w1_codes[:, 0, :].bitcast(FP8X4), lhsT_scale=w1_sc[:, 0, :],
+                            rhs=w1_codes[:].rearrange("p t m -> p (t m)").bitcast(FP8X4),
+                            rhs_scale=w1_sc[:].rearrange("p t m -> p (t m)"), start=True, stop=True)
         turned_sum(region(h_bank[0], 0), rows_of(dev[0]))
         turned_sum(region(h_bank[1], 0), rows_of(sq[0]))
         nc.scalar.activation(dev_sum_sq[:], region(h_bank[0], 0), ACT.Square, scale=1.0 / (D * math.sqrt(VAR_NOISE)))

@@ -87,8 +87,8 @@ def tile_picked_ywien_wien_p_kernel(tc, x_words, x_scales, e_words, e_scales, w1
         load_words(e_word_win, e_words)
         nc.vector.tensor_copy(x_sc_picked[:], x_scale_win[:].indirect(offsets[:]))
         nc.vector.tensor_copy(e_sc[:], e_scale_win[:].indirect(offsets[:]))
-        load_words(x_word_win, x_words)
         nc.sync.dma_start(w2_raw[:], w2.rearrange("(p j) m -> p j m", j=SLOTS))
+        load_words(x_word_win, x_words)
         nc.sync.dma_start(unit_sb[:], unit.rearrange("(p t) o -> p (t o)", t=SLOTS))
 
         def by_slot(x):
@@ -121,7 +121,7 @@ def tile_picked_ywien_wien_p_kernel(tc, x_words, x_scales, e_words, e_scales, w1
         w1_bf = tile("w1_bf", [P, SLOTS, P, SLOTS], BF16)
         w1_codes = tile("w1_codes", [P, SLOTS, P], U32)
         w1_sc = tile("w1_sc", [P, SLOTS, P], U8)
-        w2_codes = shared("w2_codes", [P, N], U32, 16384)
+        w2_codes = tile("w2_codes", [P, N], U32)
         w2_sc = tile("w2_sc", [P, N], U8)
         for part in range(2):
             nc.scalar.copy(w1_bf[:].rearrange("p t m j -> p m j t")[:, 64 * part : 64 * (part + 1)],
@@ -162,9 +162,12 @@ def tile_picked_ywien_wien_p_kernel(tc, x_words, x_scales, e_words, e_scales, w1
             gather_words(e_codes, tile("e_codes%d" % first, [P, count * P], U32), e_word_win, first)
         for c in range(4):
             first_product(h_bank, e_codes, e_sc, E_PLANE, c)
+        w2_bf = tile("w2_bf", [P, N, SLOTS], BF16)
+        nc.scalar.copy(w2_bf[:].rearrange("p (c i) j -> p c j i", i=SLOTS), w2_raw[:].rearrange("p j (c i) -> p c j i", i=SLOTS))
+        nc.vector.quantize_mx(out=w2_codes[:].bitcast(FP8X4), scales=w2_sc[:], in_=w2_bf[:].rearrange("p m j -> p (m j)"))
 
         pivot = [tile("pivot%d" % a, [P, P]) for a in range(2)]
-        dev = [tile("dev%d" % a, [P, D - 1, P]) for a in range(2)]
+        dev = [shared("dev0", [P, D - 1, P], F32, 28672), tile("dev1", [P, D - 1, P])]
         sq = [tile("sq%d" % a, [P, D - 1, P]) for a in range(2)]
 
         def deviate(c):
@@ -196,8 +199,6 @@ def tile_picked_ywien_wien_p_kernel(tc, x_words, x_scales, e_words, e_scales, w1
         square(1)
         gather_words(x_codes, tile("x_codes2", [P, HALF], U32), x_word_win, 2)
         gather_words(x_codes, tile("x_codes0", [P, HALF], U32), x_word_win, 0)
-        w2_bf = tile("w2_bf", [P, N, SLOTS], BF16)
-        nc.gpsimd.tensor_copy(w2_bf[:], w2_raw[:].rearrange("p j m -> p m j"))
         nc.scalar.activation(pivot8_turned[:], region(y_bank[0], 0), ACT.Copy, scale=float(D))
         square(2)
         square(3)
@@ -206,26 +207,27 @@ def tile_picked_ywien_wien_p_kernel(tc, x_words, x_scales, e_words, e_scales, w1
         nc.tensor.matmul_mx(out=h_bank[0][:], lhsT=w1_codes[:, 0, :].bitcast(FP8X4), lhsT_scale=w1_sc[:, 0, :],
                             rhs=w1_codes[:].rearrange("p t m -> p (t m)").bitcast(FP8X4),
                             rhs_scale=w1_sc[:].rearrange("p t m -> p (t m)"), start=True, stop=True)
-        turned_sum(region(h_bank[0], 0), rows_of(dev[0]))
-        turned_sum(region(h_bank[1], 0), rows_of(sq[0]))
-        nc.scalar.activation(dev_sum_sq[:], region(h_bank[0], 0), ACT.Square, scale=1.0 / (D * math.sqrt(VAR_NOISE)))
-        nc.scalar.copy(dev_sum[:], region(h_bank[0], 0))
+        turned_sum(region(h_bank[1], 0), rows_of(dev[0]))
+        turned_sum(region(h_bank[0], 0), rows_of(sq[0]))
+        nc.scalar.activation(dev_sum_sq[:], region(h_bank[1], 0), ACT.Square, scale=1.0 / (D * math.sqrt(VAR_NOISE)))
+        nc.scalar.copy(dev_sum[:], region(h_bank[1], 0))
 
         for c in (2, 3):
             first_product(y_bank, x_codes, x_sc, X_PLANE, c)
         neg_sq_sum = shared("neg_sq_sum", [P, P], F32, 16384 + 4096)
-        nc.scalar.activation(neg_sq_sum[:], region(h_bank[1], 0), ACT.Copy, scale=-1.0 / (D * VAR_NOISE))
-        mean0, spread0 = region(h_bank[0], 2), region(h_bank[0], 1)
+        nc.scalar.activation(neg_sq_sum[:], region(h_bank[0], 0), ACT.Copy, scale=-1.0 / (D * VAR_NOISE))
+        mean0, spread0 = region(h_bank[1], 2), region(h_bank[1], 1)
         turned_sum(spread0, [dev_sum_sq[:], neg_sq_sum[:]])
         turned_sum(mean0, [pivot8_turned[:], dev_sum[:]])
         for c in (0, 1):
             first_product(y_bank, x_codes, x_sc, X_PLANE, c)
 
-        h_sum, dev_sum1, neg_dev_sq = tile("h_sum", [P, P]), tile("dev_sum1", [P, P]), tile("neg_dev_sq", [P, P])
+        h_sum, dev_sum1, neg_dev_sq = shared("h_sum", [P, P], F32, 28672), tile("dev_sum1", [P, P]), tile("neg_dev_sq", [P, P])
         group_sum(h_sum, h_bank, 2)
         group_sum(h_sum, h_bank, 3)
-        nc.vector.quantize_mx(out=w2_codes[:].bitcast(FP8X4), scales=w2_sc[:], in_=w2_bf[:].rearrange("p m j -> p (m j)"))
-        nc.vector.scalar_tensor_tensor(out=dev_sum1[:], in0=pivot[1][:], scalar=-float(D), in1=h_sum[:], op0=ALU.mult, op1=ALU.add)
+        for c in (2, 3):
+            cols = chunk_cols(c)
+            nc.vector.scalar_tensor_tensor(out=dev_sum1[:, cols], in0=pivot[1][:, cols], scalar=-float(D), in1=h_sum[:, cols], op0=ALU.mult, op1=ALU.add)
         y_rows = tile("y_rows", [P, D, P])
         for c in (2, 3):
             nc.scalar.copy(y_rows[:, :, chunk_cols(c)].rearrange("p d (v t) -> p d v t", t=SLOTS), members(y_bank[c]))
@@ -244,7 +246,7 @@ def tile_picked_ywien_wien_p_kernel(tc, x_words, x_scales, e_words, e_scales, w1
         nc.scalar.activation(mean_root[:], mean_sq[:], ACT.Abs_reciprocal_sqrt, bias=1.0)
         nc.scalar.activation(mean_q[:], mean_root[:], ACT.Square)
 
-        spread1, y_sum1_turned = region(h_bank[1], 1), region(h_bank[2], 0)
+        spread1, y_sum1_turned = region(h_bank[0], 1), region(h_bank[2], 0)
         turned_sum(spread1, rows_of(sq[1]) + [neg_dev_sq[:]])
         turned_sum(y_sum1_turned, rows_of(y_rows))
         unit8_turned, mean_q1_turned = region(h_bank[3], 2), region(h_bank[3], 3)
@@ -254,7 +256,7 @@ def tile_picked_ywien_wien_p_kernel(tc, x_words, x_scales, e_words, e_scales, w1
         spread_q1_turned = tile("spread_q1_turned", [P, P])
         nc.scalar.activation(spread_root1[:], spread1, ACT.Abs_reciprocal_sqrt, bias=1.0, scale=1.0 / (D * VAR_NOISE))
         nc.scalar.activation(spread_q1_turned[:], spread_root1[:], ACT.Square)
-        spread_q1, bias1 = region(h_bank[0], 3), region(h_bank[0], 0)
+        spread_q1, bias1 = region(h_bank[1], 3), region(h_bank[1], 0)
         turned_sum(spread_q1, [spread_q1_turned[:]])
 
         gain = [shared("gain0", [P, P], F32, 10240), tile("gain1", [P, P])]
@@ -319,6 +321,6 @@ def tile_picked_ywien_wien_p_kernel(tc, x_words, x_scales, e_words, e_scales, w1
         second_product("first", shared("first_codes", [P, P], U32, 12288), [z_bf[0]],
                        slice(0, P), region(h_bank[3], 1), nc.sync, tile("res0", [P, P]))
         second_product("second", shared("second_codes", [P, P], U32, 12288 + 512), [z_bf[1]],
-                       slice(P, 2 * P), region(h_bank[1], 3), nc.sync, tile("res1", [P, P]))
+                       slice(P, 2 * P), region(h_bank[0], 3), nc.sync, tile("res1", [P, P]))
         second_product("fourth", tile("fourth_codes", [P, P], U32), [z_bf[3]],
-                       slice(3 * P, 4 * P), region(h_bank[0], 1), nc.scalar, shared("res3", [P, P], F32, 10752))
+                       slice(3 * P, 4 * P), region(h_bank[1], 1), nc.scalar, shared("res3", [P, P], F32, 10752))

@@ -25,8 +25,7 @@ CHUNK_COLS = GROUPS * SLOTS
 HALF = 2 * P
 MEAN_NOISE, VAR_NOISE = 0.2, 0.3
 E_PLANE, X_PLANE = 0, 4
-WARM_PASSES = 2
-OWN_GROUPS = 9
+OWN_GROUPS = 8
 
 
 def tile_picked_ywien_wien_p_kernel(tc, x_words, x_scales, e_words, e_scales, w1, unit, w2, offs, out):
@@ -135,11 +134,6 @@ def tile_picked_ywien_wien_p_kernel(tc, x_words, x_scales, e_words, e_scales, w1
                 scales=w1_sc[:, t0 : t0 + 2, :].rearrange("p t m -> p (t m)"),
                 in_=w1_bf[:, t0 : t0 + 2].rearrange("p t m j -> p (t m j)"),
             )
-
-        for n in range(WARM_PASSES):
-            nc.tensor.matmul_mx(out=y_bank[2 + n // 2][:, HALF * (n % 2) : HALF * (n % 2 + 1)], lhsT=w1_codes[:, 0, :].bitcast(FP8X4), lhsT_scale=w1_sc[:, 0, :],
-                                rhs=w1_codes[:, 0:2, :].rearrange("p t m -> p (t m)").bitcast(FP8X4),
-                                rhs_scale=w1_sc[:, 0:2, :].rearrange("p t m -> p (t m)"), start=True, stop=True)
 
         e_codes, x_codes = {}, {}
 

@@ -192,7 +192,7 @@ def tile_picked_ywien_wien_p_kernel(tc, x_words, x_scales, e_words, e_scales, w1
         square(0)
         square(1)
         gather_words(x_codes, tile("x_codes2", [P, HALF], U32), x_word_win, 2)
-        gather_words(x_codes, tile("x_codes0", [P, HALF], U32), x_word_win, 0)
+        gather_words(x_codes, shared("x_codes0", [P, HALF], U32, 32768), x_word_win, 0)
         nc.scalar.activation(pivot8_turned[:], region(y_bank[0], 0), ACT.Copy, scale=float(D))
         square(2)
         square(3)
@@ -208,15 +208,15 @@ def tile_picked_ywien_wien_p_kernel(tc, x_words, x_scales, e_words, e_scales, w1
 
         for c in (2, 3):
             first_product(y_bank, x_codes, x_sc, X_PLANE, c)
+        for c in (0, 1):
+            first_product(y_bank, x_codes, x_sc, X_PLANE, c)
         neg_sq_sum = shared("neg_sq_sum", [P, P], F32, 16384 + 4096)
         nc.scalar.activation(neg_sq_sum[:], region(h_bank[0], 0), ACT.Copy, scale=-1.0 / (D * VAR_NOISE))
         mean0, spread0 = region(h_bank[1], 2), region(h_bank[1], 1)
-        turned_sum(spread0, [dev_sum_sq[:], neg_sq_sum[:]])
         turned_sum(mean0, [pivot8_turned[:], dev_sum[:]])
-        for c in (0, 1):
-            first_product(y_bank, x_codes, x_sc, X_PLANE, c)
+        turned_sum(spread0, [dev_sum_sq[:], neg_sq_sum[:]])
 
-        h_sum, dev_sum1, neg_dev_sq = shared("h_sum", [P, P], F32, 28672), tile("dev_sum1", [P, P]), tile("neg_dev_sq", [P, P])
+        h_sum, dev_sum1, neg_dev_sq = shared("h_sum", [P, P], F32, 28672), tile("dev_sum1", [P, P]), shared("neg_dev_sq", [P, P], F32, 32768)
         group_sum(h_sum, h_bank, 2)
         group_sum(h_sum, h_bank, 3)
         for c in (2, 3):
@@ -225,27 +225,30 @@ def tile_picked_ywien_wien_p_kernel(tc, x_words, x_scales, e_words, e_scales, w1
         y_rows = tile("y_rows", [P, D, P])
         for c in (2, 3):
             nc.scalar.copy(y_rows[:, :, chunk_cols(c)].rearrange("p d (v t) -> p d v t", t=SLOTS), members(y_bank[c]))
-        y_sum = [tile("y_sum0", [P, P])]
-        nc.vector.scalar_tensor_tensor(out=neg_dev_sq[:], in0=dev_sum1[:], scalar=-1.0 / D, in1=dev_sum1[:], op0=ALU.mult, op1=ALU.mult)
+        y_sum = [tile("y_sum0", [P, P]), tile("y_sum1", [P, P])]
         group_sum(y_sum[0], y_bank, 0)
+        nc.vector.scalar_tensor_tensor(out=neg_dev_sq[:], in0=dev_sum1[:], scalar=-1.0 / D, in1=dev_sum1[:], op0=ALU.mult, op1=ALU.mult)
+        group_sum(y_sum[1], y_bank, 1)
 
         spread_root0, spread_q0 = shared("spread_root0", [P, P], F32, 0), tile("spread_q0", [P, P])
-        mean_sq = shared("mean_sq", [P, HALF], F32, 16384 + 4096)
-        mean_root, mean_q = tile("mean_root", [P, HALF]), tile("mean_q", [P, HALF])
+        mean_sq = [tile("mean_sq0", [P, P]), tile("mean_sq1", [P, P])]
+        mean_root, mean_q = [tile("mean_root%d" % a, [P, P]) for a in range(2)], [tile("mean_q%d" % a, [P, P]) for a in range(2)]
         mean_scale = 1.0 / (D * math.sqrt(MEAN_NOISE))
+        nc.gpsimd.tensor_tensor(mean_sq[1][:], h_sum[:], h_sum[:], ALU.mult)
+        nc.scalar.activation(mean_root[1][:], mean_sq[1][:], ACT.Abs_reciprocal_sqrt, bias=1.0, scale=mean_scale * mean_scale)
+        nc.gpsimd.tensor_tensor(mean_q[1][:], mean_root[1][:], mean_root[1][:], ALU.mult)
+        nc.scalar.activation(mean_sq[0][:], mean0, ACT.Square, scale=mean_scale)
         nc.scalar.activation(spread_root0[:], spread0, ACT.Abs_reciprocal_sqrt, bias=1.0, scale=-1.0)
-        nc.scalar.activation(mean_sq[:, 0:P], mean0, ACT.Square, scale=mean_scale)
-        nc.scalar.activation(mean_sq[:, P:HALF], h_sum[:], ACT.Square, scale=mean_scale)
+        nc.scalar.activation(mean_root[0][:], mean_sq[0][:], ACT.Abs_reciprocal_sqrt, bias=1.0)
         nc.scalar.activation(spread_q0[:], spread_root0[:], ACT.Square)
-        nc.scalar.activation(mean_root[:], mean_sq[:], ACT.Abs_reciprocal_sqrt, bias=1.0)
-        nc.scalar.activation(mean_q[:], mean_root[:], ACT.Square)
+        nc.scalar.activation(mean_q[0][:], mean_root[0][:], ACT.Square)
 
         spread1, y_sum1_turned = region(h_bank[0], 1), region(h_bank[2], 0)
         turned_sum(spread1, rows_of(sq[1]) + [neg_dev_sq[:]])
-        turned_sum(y_sum1_turned, rows_of(y_rows))
         unit8_turned, mean_q1_turned = region(h_bank[3], 2), region(h_bank[3], 3)
         turned_sum(unit8_turned, [unit8[:]])
-        turned_sum(mean_q1_turned, [mean_q[:, P:HALF]])
+        turned_sum(mean_q1_turned, [mean_q[1][:]])
+        turned_sum(y_sum1_turned, rows_of(y_rows))
         spread_root1 = shared("spread_root1", [P, P], F32, 4096 - 256)
         spread_q1_turned = tile("spread_q1_turned", [P, P])
         nc.scalar.activation(spread_root1[:], spread1, ACT.Abs_reciprocal_sqrt, bias=1.0, scale=1.0 / (D * VAR_NOISE))
@@ -273,11 +276,9 @@ def tile_picked_ywien_wien_p_kernel(tc, x_words, x_scales, e_words, e_scales, w1
             engine.tensor_tensor(z_bf[c][:, 0:groups], ay[c][:, 0:groups], per_member(bias, c, groups), ALU.add)
 
         make_gain(0, spread_q0[:])
-        y_sum.append(shared("y_sum1", [P, P], F32, 0))
-        group_sum(y_sum[1], y_bank, 1)
         nc.gpsimd.tensor_tensor(unit_mean0[:, chunk_cols(0)], y_sum[0][:, chunk_cols(0)], unit8[:, chunk_cols(0)], ALU.mult)
-        nc.gpsimd.tensor_tensor(q_diff[0][:], spread_q0[:], mean_q[:, 0:P], ALU.subtract)
         nc.gpsimd.tensor_tensor(unit_mean0[:, chunk_cols(1)], y_sum[1][:, chunk_cols(1)], unit8[:, chunk_cols(1)], ALU.mult)
+        nc.gpsimd.tensor_tensor(q_diff[0][:], spread_q0[:], mean_q[0][:], ALU.subtract)
         times_gain(0, GROUPS)
         nc.gpsimd.tensor_tensor(bias[0][:], q_diff[0][:], unit_mean0[:], ALU.mult)
         nc.vector.tensor_tensor(q_diff[1][:], spread_q1_turned[:], mean_q1_turned, ALU.subtract)
@@ -317,4 +318,4 @@ def tile_picked_ywien_wien_p_kernel(tc, x_words, x_scales, e_words, e_scales, w1
         second_product("second", shared("second_codes", [P, P], U32, 12288 + 512), [z_bf[1]],
                        slice(P, 2 * P), region(h_bank[0], 3), nc.sync, tile("res1", [P, P]))
         second_product("fourth", tile("fourth_codes", [P, P], U32), [z_bf[3]],
-                       slice(3 * P, 4 * P), region(h_bank[1], 1), nc.scalar, shared("res3", [P, P], F32, 10752))
+                       slice(3 * P, 4 * P), region(y_bank[0], 0), nc.scalar, tile("res3", [P, P]))

@@ -25,6 +25,8 @@ CHUNK_COLS = GROUPS * SLOTS
 HALF = 2 * P
 MEAN_NOISE, VAR_NOISE = 0.2, 0.3
 E_PLANE, X_PLANE = 0, 4
+QUAD = D // 2
+MX_SUM_SLOTS = 2
 OWN_GROUPS = 8
 
 
@@ -152,17 +154,24 @@ def tile_picked_ywien_wien_p_kernel(tc, x_words, x_scales, e_words, e_scales, w1
                     start=True, stop=True,
                 )
 
-        for first, count in ((0, 1), (1, 1), (2, 2)):
-            gather_words(e_codes, tile("e_codes%d" % first, [P, count * P], U32), e_word_win, first)
+        e_quads, e_sc_quads = tile("e_quads", [P, HALF], U32), tile("e_sc_quads", [P, HALF], U8)
+        nc.vector.tensor_copy(e_sc_quads[:].bitcast(I32).rearrange("p (q v) -> p q v", q=2), e_sc[:, HALF:S].bitcast(I32).rearrange("p (v q) -> p q v", q=2))
+        nc.tensor.matmul_mx(out=y_bank[3][:], lhsT=w1_codes[:, 0, :].bitcast(FP8X4), lhsT_scale=w1_sc[:, 0, :],
+                            rhs=w1_codes[:].rearrange("p t m -> p (t m)").bitcast(FP8X4),
+                            rhs_scale=w1_sc[:].rearrange("p t m -> p (t m)"), start=True, stop=True)
+        e_picked = [tile("e_codes%d" % first, [P, count * P], U32) for first, count in ((0, 1), (1, 1), (2, 2))]
+        for first in range(3):
+            gather_words(e_codes, e_picked[first], e_word_win, first)
         for c in range(4):
             first_product(h_bank, e_codes, e_sc, E_PLANE, c)
         w2_bf = tile("w2_bf", [P, N, SLOTS], BF16)
         nc.scalar.copy(w2_bf[:].rearrange("p (c i) j -> p c j i", i=SLOTS), w2_raw[:].rearrange("p j (c i) -> p c j i", i=SLOTS))
         nc.vector.quantize_mx(out=w2_codes[:].bitcast(FP8X4), scales=w2_sc[:], in_=w2_bf[:].rearrange("p m j -> p (m j)"))
 
+        nc.vector.tensor_copy(e_quads[:].bitcast(I32).rearrange("p (q v d) -> p q v d", q=2, d=QUAD), e_picked[2][:].bitcast(I32).rearrange("p (v q d) -> p q v d", q=2, d=QUAD))
         pivot = [tile("pivot%d" % a, [P, P]) for a in range(2)]
         dev = [shared("dev0", [P, D - 1, P], F32, 28672), tile("dev1", [P, D - 1, P])]
-        sq = [tile("sq%d" % a, [P, D - 1, P]) for a in range(2)]
+        sq = [tile("sq0", [P, D - 1, P]), tile("sq1", [P, D - 1, P])]
 
         def deviate(c):
             cols = chunk_cols(c)
@@ -191,34 +200,35 @@ def tile_picked_ywien_wien_p_kernel(tc, x_words, x_scales, e_words, e_scales, w1
         turned_sum(region(y_bank[0], 0), [pivot[0][:]])
         square(0)
         square(1)
-        gather_words(x_codes, tile("x_codes2", [P, HALF], U32), x_word_win, 2)
+        gather_words(x_codes, shared("x_codes2", [P, HALF], U32, 40960), x_word_win, 2)
         gather_words(x_codes, shared("x_codes0", [P, HALF], U32, 32768), x_word_win, 0)
         nc.scalar.activation(pivot8_turned[:], region(y_bank[0], 0), ACT.Copy, scale=float(D))
         square(2)
         square(3)
 
         dev_sum, dev_sum_sq = tile("dev_sum", [P, P]), tile("dev_sum_sq", [P, P])
-        nc.tensor.matmul_mx(out=h_bank[0][:], lhsT=w1_codes[:, 0, :].bitcast(FP8X4), lhsT_scale=w1_sc[:, 0, :],
-                            rhs=w1_codes[:].rearrange("p t m -> p (t m)").bitcast(FP8X4),
-                            rhs_scale=w1_sc[:].rearrange("p t m -> p (t m)"), start=True, stop=True)
-        turned_sum(region(h_bank[1], 0), rows_of(dev[0]))
-        turned_sum(region(h_bank[0], 0), rows_of(sq[0]))
-        nc.scalar.activation(dev_sum_sq[:], region(h_bank[1], 0), ACT.Square, scale=1.0 / (D * math.sqrt(VAR_NOISE)))
-        nc.scalar.copy(dev_sum[:], region(h_bank[1], 0))
+        for t in range(MX_SUM_SLOTS):
+            for q in range(2):
+                nc.tensor.matmul_mx(out=region(h_bank[0], t), lhsT=w1_codes[:, t, :].bitcast(FP8X4), lhsT_scale=w1_sc[:, t, :],
+                                    rhs=region(e_quads, q).bitcast(FP8X4), rhs_scale=region(e_sc_quads, q), start=(q == 0), stop=(q == 1))
+        turned_sum(region(y_bank[1], 0), rows_of(dev[0]))
+        turned_sum(region(h_bank[1], 0), rows_of(sq[0]))
+        nc.scalar.activation(dev_sum_sq[:], region(y_bank[1], 0), ACT.Square, scale=1.0 / (D * math.sqrt(VAR_NOISE)))
+        nc.scalar.copy(dev_sum[:], region(y_bank[1], 0))
 
-        for c in (2, 3):
-            first_product(y_bank, x_codes, x_sc, X_PLANE, c)
-        for c in (0, 1):
+        for c in (2, 3, 0, 1):
             first_product(y_bank, x_codes, x_sc, X_PLANE, c)
         neg_sq_sum = shared("neg_sq_sum", [P, P], F32, 16384 + 4096)
-        nc.scalar.activation(neg_sq_sum[:], region(h_bank[0], 0), ACT.Copy, scale=-1.0 / (D * VAR_NOISE))
+        nc.scalar.activation(neg_sq_sum[:], region(h_bank[1], 0), ACT.Copy, scale=-1.0 / (D * VAR_NOISE))
         mean0, spread0 = region(h_bank[1], 2), region(h_bank[1], 1)
         turned_sum(mean0, [pivot8_turned[:], dev_sum[:]])
         turned_sum(spread0, [dev_sum_sq[:], neg_sq_sum[:]])
 
         h_sum, dev_sum1, neg_dev_sq = shared("h_sum", [P, P], F32, 28672), tile("dev_sum1", [P, P]), shared("neg_dev_sq", [P, P], F32, 32768)
-        group_sum(h_sum, h_bank, 2)
-        group_sum(h_sum, h_bank, 3)
+        nc.vector.tensor_reduce(by_slot(h_sum[:])[:, :, 0:MX_SUM_SLOTS], h_bank[0][:].rearrange("p (t v d) -> p v t d", t=SLOTS, d=QUAD)[:, :, 0:MX_SUM_SLOTS], AX.X, ALU.add)
+        for c in (2, 3):
+            nc.vector.tensor_reduce(by_slot(h_sum[:, chunk_cols(c)])[:, :, MX_SUM_SLOTS:SLOTS],
+                                    h_bank[c][:].rearrange("p (t v d) -> p v t d", t=SLOTS, d=D)[:, :, MX_SUM_SLOTS:SLOTS], AX.X, ALU.add)
         for c in (2, 3):
             cols = chunk_cols(c)
             nc.vector.scalar_tensor_tensor(out=dev_sum1[:, cols], in0=pivot[1][:, cols], scalar=-float(D), in1=h_sum[:, cols], op0=ALU.mult, op1=ALU.add)
@@ -232,7 +242,7 @@ def tile_picked_ywien_wien_p_kernel(tc, x_words, x_scales, e_words, e_scales, w1
 
         spread_root0, spread_q0 = shared("spread_root0", [P, P], F32, 0), tile("spread_q0", [P, P])
         mean_sq = [tile("mean_sq0", [P, P]), tile("mean_sq1", [P, P])]
-        mean_root, mean_q = [tile("mean_root%d" % a, [P, P]) for a in range(2)], [tile("mean_q%d" % a, [P, P]) for a in range(2)]
+        mean_root, mean_q = [tile("mean_root0", [P, P]), shared("mean_root1", [P, P], F32, 40960)], [tile("mean_q%d" % a, [P, P]) for a in range(2)]
         mean_scale = 1.0 / (D * math.sqrt(MEAN_NOISE))
         nc.gpsimd.tensor_tensor(mean_sq[1][:], h_sum[:], h_sum[:], ALU.mult)
         nc.scalar.activation(mean_root[1][:], mean_sq[1][:], ACT.Abs_reciprocal_sqrt, bias=1.0, scale=mean_scale * mean_scale)
@@ -243,7 +253,7 @@ def tile_picked_ywien_wien_p_kernel(tc, x_words, x_scales, e_words, e_scales, w1
         nc.scalar.activation(spread_q0[:], spread_root0[:], ACT.Square)
         nc.scalar.activation(mean_q[0][:], mean_root[0][:], ACT.Square)
 
-        spread1, y_sum1_turned = region(h_bank[0], 1), region(h_bank[2], 0)
+        spread1, y_sum1_turned = region(h_bank[0], 2), region(h_bank[2], 0)
         turned_sum(spread1, rows_of(sq[1]) + [neg_dev_sq[:]])
         unit8_turned, mean_q1_turned = region(h_bank[3], 2), region(h_bank[3], 3)
         turned_sum(unit8_turned, [unit8[:]])
@@ -312,7 +322,7 @@ def tile_picked_ywien_wien_p_kernel(tc, x_words, x_scales, e_words, e_scales, w1
 
         plus_bias(nc.vector, 3, GROUPS)
         second_product("third", tile("third_codes", [P, P], U32), [z_bf[2]],
-                       slice(2 * P, 3 * P), region(h_bank[2], 1), nc.sync, shared("res2", [P, P], F32, 10240))
+                       slice(2 * P, 3 * P), region(h_bank[2], 3), nc.sync, shared("res2", [P, P], F32, 10240))
         second_product("first", shared("first_codes", [P, P], U32, 12288), [z_bf[0]],
                        slice(0, P), region(h_bank[3], 1), nc.sync, tile("res0", [P, P]))
         second_product("second", shared("second_codes", [P, P], U32, 12288 + 512), [z_bf[1]],

@@ -88,8 +88,8 @@ def tile_picked_ywien_wien_p_kernel(tc, x_words, x_scales, e_words, e_scales, w1
         load_words(e_word_win, e_words)
         nc.vector.tensor_copy(x_sc_picked[:], x_scale_win[:].indirect(offsets[:]))
         nc.vector.tensor_copy(e_sc[:], e_scale_win[:].indirect(offsets[:]))
-        nc.sync.dma_start(w2_raw[:], w2.rearrange("(p j) m -> p j m", j=SLOTS))
         load_words(x_word_win, x_words)
+        nc.sync.dma_start(w2_raw[:], w2.rearrange("(p j) m -> p j m", j=SLOTS))
         nc.sync.dma_start(unit_sb[:], unit.rearrange("(p t) o -> p (t o)", t=SLOTS))
 
         def by_slot(x):
@@ -122,7 +122,7 @@ def tile_picked_ywien_wien_p_kernel(tc, x_words, x_scales, e_words, e_scales, w1
         w1_bf = tile("w1_bf", [P, SLOTS, P, SLOTS], BF16)
         w1_codes = tile("w1_codes", [P, SLOTS, P], U32)
         w1_sc = tile("w1_sc", [P, SLOTS, P], U8)
-        w2_codes = tile("w2_codes", [P, N], U32)
+        w2_codes = shared("w2_codes", [P, N], U32, 32768 + 512)
         w2_sc = tile("w2_sc", [P, N], U8)
         for part in range(2):
             nc.scalar.copy(w1_bf[:].rearrange("p t m j -> p m j t")[:, 64 * part : 64 * (part + 1)],
@@ -164,9 +164,6 @@ def tile_picked_ywien_wien_p_kernel(tc, x_words, x_scales, e_words, e_scales, w1
             gather_words(e_codes, e_picked[first], e_word_win, first)
         for c in range(4):
             first_product(h_bank, e_codes, e_sc, E_PLANE, c)
-        w2_bf = tile("w2_bf", [P, N, SLOTS], BF16)
-        nc.scalar.copy(w2_bf[:].rearrange("p (c i) j -> p c j i", i=SLOTS), w2_raw[:].rearrange("p j (c i) -> p c j i", i=SLOTS))
-        nc.vector.quantize_mx(out=w2_codes[:].bitcast(FP8X4), scales=w2_sc[:], in_=w2_bf[:].rearrange("p m j -> p (m j)"))
 
         nc.vector.tensor_copy(e_quads[:].bitcast(I32).rearrange("p (q v d) -> p q v d", q=2, d=QUAD), e_picked[2][:].bitcast(I32).rearrange("p (v q d) -> p q v d", q=2, d=QUAD))
         pivot = [tile("pivot%d" % a, [P, P]) for a in range(2)]
@@ -203,6 +200,8 @@ def tile_picked_ywien_wien_p_kernel(tc, x_words, x_scales, e_words, e_scales, w1
         gather_words(x_codes, shared("x_codes2", [P, HALF], U32, 40960), x_word_win, 2)
         gather_words(x_codes, shared("x_codes0", [P, HALF], U32, 32768), x_word_win, 0)
         nc.scalar.activation(pivot8_turned[:], region(y_bank[0], 0), ACT.Copy, scale=float(D))
+        w2_bf = shared("w2_bf", [P, N, SLOTS], BF16, 16384)
+        nc.gpsimd.tensor_copy(w2_bf[:].rearrange("p (c i) j -> p c j i", i=SLOTS), w2_raw[:].rearrange("p j (c i) -> p c j i", i=SLOTS))
         square(2)
         square(3)
 
@@ -285,6 +284,7 @@ def tile_picked_ywien_wien_p_kernel(tc, x_words, x_scales, e_words, e_scales, w1
         def plus_bias(engine, c, groups):
             engine.tensor_tensor(z_bf[c][:, 0:groups], ay[c][:, 0:groups], per_member(bias, c, groups), ALU.add)
 
+        nc.vector.quantize_mx(out=w2_codes[:].bitcast(FP8X4), scales=w2_sc[:], in_=w2_bf[:].rearrange("p m j -> p (m j)"))
         make_gain(0, spread_q0[:])
         nc.gpsimd.tensor_tensor(unit_mean0[:, chunk_cols(0)], y_sum[0][:, chunk_cols(0)], unit8[:, chunk_cols(0)], ALU.mult)
         nc.gpsimd.tensor_tensor(unit_mean0[:, chunk_cols(1)], y_sum[1][:, chunk_cols(1)], unit8[:, chunk_cols(1)], ALU.mult)

import math
from contextlib import ExitStack

import concourse.mybir as mybir
from concourse.masks import make_identity

K, T, S, D, H, N = 512, 2048, 512, 8, 512, 128
FLOPS = 2 * K * H * S * 2 + 2 * H * N * S

F32 = mybir.dt.float32
BF16 = mybir.dt.bfloat16
I32 = mybir.dt.int32
U32 = mybir.dt.uint32
U16 = mybir.dt.uint16
U8 = mybir.dt.uint8
FP8X4 = mybir.dt.float8_e4m3fn_x4
ALU = mybir.AluOpType
ACT = mybir.ActivationFunctionType
AX = mybir.AxisListType

P = 128
SLOTS = 4
GROUPS = P // D
CHUNK_COLS = GROUPS * SLOTS
HALF = 2 * P
MEAN_NOISE, VAR_NOISE = 0.2, 0.3
E_PLANE, X_PLANE = 0, 4
QUAD = D // 2
MX_SUM_SLOTS = 2
OWN_GROUPS = 8


def tile_picked_ywien_wien_p_kernel(tc, x_words, x_scales, e_words, e_scales, w1, unit, w2, offs, out):
    nc = tc.nc
    with ExitStack() as ctx:
        sb = ctx.enter_context(tc.tile_pool(name="sb", bufs=1))
        reuse = ctx.enter_context(tc.tile_pool(name="reuse", bufs=1))
        ps = ctx.enter_context(tc.psum_pool(name="ps", bufs=1))

        def tile(name, shape, dt=F32):
            return sb.tile(shape, dt, name=name, align_bytes=64)

        def shared(name, shape, dt, place):
            return reuse.tile(shape, dt, name=name, offset=place, align_bytes=64)

        offsets = sb.tile([P, S // 16], U16, name="offsets")
        h_bank = [ps.tile([P, SLOTS * P], F32, name="h_bank%d" % c) for c in range(4)]
        y_bank = [ps.tile([P, SLOTS * P], F32, name="y_bank%d" % c) for c in range(4)]

        e_scale_win = tile("e_scale_win", [P, T], U8)
        x_scale_win = tile("x_scale_win", [P, T], U8)
        e_word_win = tile("e_word_win", [P, T], I32)
        x_word_win = shared("x_word_win", [P, T], I32, 16384)
        w1_raw = [tile("w1_raw0", [P, SLOTS, HALF]), shared("w1_raw1", [P, SLOTS, HALF], F32, 24576)]
        w2_raw = tile("w2_raw", [P, SLOTS, N])
        unit_sb = tile("unit_sb", [P, SLOTS])
        ident = tile("ident", [P, P])
        warm = tile("warm", [P, 1])
        e_sc, x_sc_picked = (tile(nm, [P, S], U8) for nm in ("e_sc", "x_sc_picked"))

        nc.gpsimd.memset(x_scale_win[:].bitcast(I32), 0)
        nc.vector.memset(warm[:], 1.0)
        nc.vector.memset(e_scale_win[:].bitcast(I32), 0)
        nc.scalar.activation(warm[:], warm[:], ACT.Abs_reciprocal_sqrt)
        make_identity(nc, ident[:])

        def load_scales(win, src, plane):
            nc.sync.dma_start(win[plane:P:8, :].bitcast(I32), src[0].bitcast(I32))

        def place_scales(dst, picked, plane):
            for r in range(4):
                nc.scalar.dma_start(dst[plane + r : P : 32, :].bitcast(I32), picked[plane + 8 * r : P : 32, :].bitcast(I32))

        def load_words(win, src):
            nc.sync.dma_start(win[:], src[0].rearrange("p n t -> p (n t)").bitcast(I32))

        w1_rows = w1.rearrange("(p j) c -> p j c", j=SLOTS)

        def load_w1(part):
            nc.sync.dma_start(w1_raw[part][:], w1_rows[:, :, HALF * part : HALF * (part + 1)])

        nc.sync.dma_start(offsets[:], offs)
        load_w1(0)
        load_scales(x_scale_win, x_scales, X_PLANE)
        for r in range(4):
            nc.sync.dma_start(e_scale_win[E_PLANE + r : P : 32, :].bitcast(I32), e_scales[0][r:16:4, :].bitcast(I32))
        load_w1(1)
        load_words(e_word_win, e_words)
        nc.vector.tensor_copy(x_sc_picked[:], x_scale_win[:].indirect(offsets[:]))
        nc.vector.tensor_copy(e_sc[:], e_scale_win[:].indirect(offsets[:]))
        load_words(x_word_win, x_words)
        nc.sync.dma_start(w2_raw[:], w2.rearrange("(p j) m -> p j m", j=SLOTS))
        nc.sync.dma_start(unit_sb[:], unit.rearrange("(p t) o -> p (t o)", t=SLOTS))

        def by_slot(x):
            return x.rearrange("p (v t) -> p v t", t=SLOTS)

        def chunk_cols(c):
            return slice(CHUNK_COLS * (c % 2), CHUNK_COLS * (c % 2 + 1))

        def region(bank, r):
            return bank[:, P * r : P * (r + 1)]

        def members(bank):
            return bank[:].rearrange("p (t v d) -> p d v t", t=SLOTS, d=D)

        def over_groups(x):
            return x[:].unsqueeze(1).to_broadcast([P, 2 * GROUPS, SLOTS])

        def turned_sum(dst, parts):
            for n, part in enumerate(parts):
                nc.tensor.matmul(dst, lhsT=part, rhs=ident[:], start=(n == 0), stop=(n == len(parts) - 1), is_transpose=True)

        def rows_of(x):
            return [x[:, d, :] for d in range(x.shape[1])]

        neg_unit = tile("neg_unit", [P, SLOTS])
        unit8 = tile("unit8", [P, P])
        nc.gpsimd.tensor_scalar(by_slot(unit8[:]), over_groups(unit_sb), 1.0 / D, 0.0, ALU.mult, ALU.add)
        nc.gpsimd.tensor_scalar(neg_unit[:], unit_sb[:], -1.0, 0.0, ALU.mult, ALU.add)

        w1_bf = tile("w1_bf", [P, SLOTS, P, SLOTS], BF16)
        w1_codes = tile("w1_codes", [P, SLOTS, P], U32)
        w1_sc = tile("w1_sc", [P, SLOTS, P], U8)
        w2_codes = shared("w2_codes", [P, N], U32, 32768 + 512)
        w2_sc = tile("w2_sc", [P, N], U8)
        for part in range(2):
            nc.scalar.copy(w1_bf[:].rearrange("p t m j -> p m j t")[:, 64 * part : 64 * (part + 1)],
                           w1_raw[part][:].rearrange("p j (m t) -> p m j t", t=SLOTS))
        x_sc = shared("x_sc", [P, S], U8, 24576)
        nc.gpsimd.memset(x_sc[:].bitcast(I32), 0)
        place_scales(x_sc, x_sc_picked, X_PLANE)
        for t0 in (0, 2):
            nc.vector.quantize_mx(
                out=w1_codes[:, t0 : t0 + 2, :].rearrange("p t m -> p (t m)").bitcast(FP8X4),
                scales=w1_sc[:, t0 : t0 + 2, :].rearrange("p t m -> p (t m)"),
                in_=w1_bf[:, t0 : t0 + 2].rearrange("p t m j -> p (t m j)"),
            )

        e_codes, x_codes = {}, {}

        def gather_words(codes, picked, win, first):
            count = picked.shape[1] // P
            nc.vector.tensor_copy(picked[:], win[:].bitcast(U32).indirect(offsets[:, P // 16 * first : P // 16 * (first + count)]))
            codes.update({first + n: region(picked, n) for n in range(count)})

        def first_product(bank, codes, scales, plane, c):
            for t in range(SLOTS):
                nc.tensor.matmul_mx(
                    out=region(bank[c], t),
                    lhsT=w1_codes[:, t, :].bitcast(FP8X4), lhsT_scale=w1_sc[:, t, :],
                    rhs=codes[c].bitcast(FP8X4),
                    rhs_scale=scales[plane:P, P * c : P * (c + 1)],
                    start=True, stop=True,
                )

        e_quads, e_sc_quads = tile("e_quads", [P, HALF], U32), tile("e_sc_quads", [P, HALF], U8)
        nc.vector.tensor_copy(e_sc_quads[:].bitcast(I32).rearrange("p (q v) -> p q v", q=2), e_sc[:, HALF:S].bitcast(I32).rearrange("p (v q) -> p q v", q=2))
        nc.tensor.matmul_mx(out=y_bank[3][:], lhsT=w1_codes[:, 0, :].bitcast(FP8X4), lhsT_scale=w1_sc[:, 0, :],
                            rhs=w1_codes[:].rearrange("p t m -> p (t m)").bitcast(FP8X4),
                            rhs_scale=w1_sc[:].rearrange("p t m -> p (t m)"), start=True, stop=True)
        e_picked = [tile("e_codes%d" % first, [P, count * P], U32) for first, count in ((0, 1), (1, 1), (2, 2))]
        for first in range(3):
            gather_words(e_codes, e_picked[first], e_word_win, first)
        for c in range(4):
            first_product(h_bank, e_codes, e_sc, E_PLANE, c)

        nc.vector.tensor_copy(e_quads[:].bitcast(I32).rearrange("p (q v d) -> p q v d", q=2, d=QUAD), e_picked[2][:].bitcast(I32).rearrange("p (v q d) -> p q v d", q=2, d=QUAD))
        pivot = [tile("pivot%d" % a, [P, P]) for a in range(2)]
        dev = [shared("dev0", [P, D - 1, P], F32, 28672), tile("dev1", [P, D - 1, P])]
        sq = [tile("sq0", [P, D - 1, P]), tile("sq1", [P, D - 1, P])]

        def deviate(c):
            cols = chunk_cols(c)
            nc.vector.tensor_tensor(
                dev[c // 2][:, :, cols].rearrange("p d (v t) -> p d v t", t=SLOTS),
                members(h_bank[c])[:, 1:D],
                by_slot(pivot[c // 2][:, cols]).unsqueeze(1).to_broadcast([P, D - 1, GROUPS, SLOTS]),
                ALU.subtract,
            )

        def square(c):
            cols = chunk_cols(c)
            nc.scalar.activation(sq[c // 2][:, :, cols], dev[c // 2][:, :, cols], ACT.Square)

        def group_sum(dst, bank, c):
            nc.vector.tensor_reduce(by_slot(dst[:, chunk_cols(c)]), bank[c][:].rearrange("p (t v d) -> p v t d", t=SLOTS, d=D), AX.X, ALU.add)

        def take_pivot(c):
            nc.scalar.copy(by_slot(pivot[c // 2][:, chunk_cols(c)]), members(h_bank[c])[:, 0])

        for c in range(4):
            take_pivot(c)
        for c in range(4):
            deviate(c)
        pivot8_turned = tile("pivot8_turned", [P, P])
        turned_sum(region(y_bank[0], 0), [pivot[0][:]])
        square(0)
        square(1)
        gather_words(x_codes, shared("x_codes2", [P, HALF], U32, 40960), x_word_win, 2)
        gather_words(x_codes, shared("x_codes0", [P, HALF], U32, 32768), x_word_win, 0)
        nc.scalar.activation(pivot8_turned[:], region(y_bank[0], 0), ACT.Copy, scale=float(D))
        w2_bf = shared("w2_bf", [P, N, SLOTS], BF16, 16384)
        nc.gpsimd.tensor_copy(w2_bf[:].rearrange("p (c i) j -> p c j i", i=SLOTS), w2_raw[:].rearrange("p j (c i) -> p c j i", i=SLOTS))
        square(2)
        square(3)

        dev_sum, dev_sum_sq = tile("dev_sum", [P, P]), tile("dev_sum_sq", [P, P])
        for t in range(MX_SUM_SLOTS):
            for q in range(2):
                nc.tensor.matmul_mx(out=region(h_bank[0], t), lhsT=w1_codes[:, t, :].bitcast(FP8X4), lhsT_scale=w1_sc[:, t, :],
                                    rhs=region(e_quads, q).bitcast(FP8X4), rhs_scale=region(e_sc_quads, q), start=(q == 0), stop=(q == 1))
        turned_sum(region(y_bank[1], 0), rows_of(dev[0]))
        turned_sum(region(h_bank[1], 0), rows_of(sq[0]))
        nc.scalar.activation(dev_sum_sq[:], region(y_bank[1], 0), ACT.Square, scale=1.0 / (D * math.sqrt(VAR_NOISE)))
        nc.scalar.copy(dev_sum[:], region(y_bank[1], 0))

        for c in (2, 3, 0, 1):
            first_product(y_bank, x_codes, x_sc, X_PLANE, c)
        neg_sq_sum = shared("neg_sq_sum", [P, P], F32, 16384 + 4096)
        nc.scalar.activation(neg_sq_sum[:], region(h_bank[1], 0), ACT.Copy, scale=-1.0 / (D * VAR_NOISE))
        mean0, spread0 = region(h_bank[1], 2), region(h_bank[1], 1)
        turned_sum(mean0, [pivot8_turned[:], dev_sum[:]])
        turned_sum(spread0, [dev_sum_sq[:], neg_sq_sum[:]])

        h_sum, dev_sum1, neg_dev_sq = shared("h_sum", [P, P], F32, 28672), tile("dev_sum1", [P, P]), shared("neg_dev_sq", [P, P], F32, 32768)
        nc.vector.tensor_reduce(by_slot(h_sum[:])[:, :, 0:MX_SUM_SLOTS], h_bank[0][:].rearrange("p (t v d) -> p v t d", t=SLOTS, d=QUAD)[:, :, 0:MX_SUM_SLOTS], AX.X, ALU.add)
        for c in (2, 3):
            nc.vector.tensor_reduce(by_slot(h_sum[:, chunk_cols(c)])[:, :, MX_SUM_SLOTS:SLOTS],
                                    h_bank[c][:].rearrange("p (t v d) -> p v t d", t=SLOTS, d=D)[:, :, MX_SUM_SLOTS:SLOTS], AX.X, ALU.add)
        for c in (2, 3):
            cols = chunk_cols(c)
            nc.vector.scalar_tensor_tensor(out=dev_sum1[:, cols], in0=pivot[1][:, cols], scalar=-float(D), in1=h_sum[:, cols], op0=ALU.mult, op1=ALU.add)
        y_rows = tile("y_rows", [P, D, P])
        for c in (2, 3):
            nc.scalar.copy(y_rows[:, :, chunk_cols(c)].rearrange("p d (v t) -> p d v t", t=SLOTS), members(y_bank[c]))
        y_sum = [tile("y_sum0", [P, P]), tile("y_sum1", [P, P])]
        group_sum(y_sum[0], y_bank, 0)
        nc.vector.scalar_tensor_tensor(out=neg_dev_sq[:], in0=dev_sum1[:], scalar=-1.0 / D, in1=dev_sum1[:], op0=ALU.mult, op1=ALU.mult)
        group_sum(y_sum[1], y_bank, 1)

        spread_root0, spread_q0 = shared("spread_root0", [P, P], F32, 0), tile("spread_q0", [P, P])
        mean_sq = [tile("mean_sq0", [P, P]), tile("mean_sq1", [P, P])]
        mean_root, mean_q = [tile("mean_root0", [P, P]), shared("mean_root1", [P, P], F32, 40960)], [tile("mean_q%d" % a, [P, P]) for a in range(2)]
        mean_scale = 1.0 / (D * math.sqrt(MEAN_NOISE))
        nc.gpsimd.tensor_tensor(mean_sq[1][:], h_sum[:], h_sum[:], ALU.mult)
        nc.scalar.activation(mean_root[1][:], mean_sq[1][:], ACT.Abs_reciprocal_sqrt, bias=1.0, scale=mean_scale * mean_scale)
        nc.gpsimd.tensor_tensor(mean_q[1][:], mean_root[1][:], mean_root[1][:], ALU.mult)
        nc.scalar.activation(mean_sq[0][:], mean0, ACT.Square, scale=mean_scale)
        nc.scalar.activation(spread_root0[:], spread0, ACT.Abs_reciprocal_sqrt, bias=1.0, scale=-1.0)
        nc.scalar.activation(mean_root[0][:], mean_sq[0][:], ACT.Abs_reciprocal_sqrt, bias=1.0)
        nc.scalar.activation(spread_q0[:], spread_root0[:], ACT.Square)
        nc.scalar.activation(mean_q[0][:], mean_root[0][:], ACT.Square)

        spread1, y_sum1_turned = region(h_bank[0], 2), region(h_bank[2], 0)
        turned_sum(spread1, rows_of(sq[1]) + [neg_dev_sq[:]])
        unit8_turned, mean_q1_turned = region(h_bank[3], 2), region(h_bank[3], 3)
        turned_sum(unit8_turned, [unit8[:]])
        turned_sum(mean_q1_turned, [mean_q[1][:]])
        turned_sum(y_sum1_turned, rows_of(y_rows))
        spread_root1 = shared("spread_root1", [P, P], F32, 4096 - 256)
        spread_q1_turned = tile("spread_q1_turned", [P, P])
        nc.scalar.activation(spread_root1[:], spread1, ACT.Abs_reciprocal_sqrt, bias=1.0, scale=1.0 / (D * VAR_NOISE))
        nc.scalar.activation(spread_q1_turned[:], spread_root1[:], ACT.Square)
        spread_q1, bias1 = region(h_bank[1], 3), region(h_bank[1], 0)
        turned_sum(spread_q1, [spread_q1_turned[:]])

        gain = [shared("gain0", [P, P], F32, 10240), tile("gain1", [P, P])]
        bias = [shared("bias0", [P, P], F32, 10752), bias1]
        q_diff = [tile("q_diff0", [P, P]), tile("q_diff1", [P, P])]
        unit_mean0, unit_diff1, bias1_turned = tile("unit_mean0", [P, P]), tile("unit_diff1", [P, P]), tile("bias1_turned", [P, P])
        ay = [tile("ay0", [P, GROUPS, D, SLOTS]), shared("ay1", [P, GROUPS, D, SLOTS], F32, 4096), shared("ay2", [P, GROUPS, D, SLOTS], F32, 12288), tile("ay3", [P, GROUPS, D, SLOTS])]
        z_bf = [tile("z_bf0", [P, GROUPS, D, SLOTS], BF16)[:], shared("z_bf1", [P, GROUPS * D * SLOTS], BF16, 3072)[:].rearrange("p (v d t) -> p v d t", d=D, t=SLOTS), tile("z_bf2", [P, GROUPS, D, SLOTS], BF16)[:], tile("z_bf3", [P, GROUPS, D, SLOTS], BF16)[:]]

        def make_gain(a, q):
            nc.vector.scalar_tensor_tensor(out=by_slot(gain[a][:]), in0=by_slot(q), scalar=-1.0, in1=over_groups(neg_unit), op0=ALU.add, op1=ALU.mult)

        def per_member(g, c, groups):
            return by_slot(g[c // 2][:, chunk_cols(c)])[:, 0:groups].unsqueeze(2).to_broadcast([P, groups, D, SLOTS])

        def times_gain(c, groups):
            nc.vector.tensor_tensor(ay[c][:, 0:groups], y_bank[c][:].rearrange("p (t v d) -> p v d t", t=SLOTS, d=D)[:, 0:groups], per_member(gain, c, groups), ALU.mult)

        def plus_bias(engine, c, groups):
            engine.tensor_tensor(z_bf[c][:, 0:groups], ay[c][:, 0:groups], per_member(bias, c, groups), ALU.add)

        nc.vector.quantize_mx(out=w2_codes[:].bitcast(FP8X4), scales=w2_sc[:], in_=w2_bf[:].rearrange("p m j -> p (m j)"))
        make_gain(0, spread_q0[:])
        nc.gpsimd.tensor_tensor(unit_mean0[:, chunk_cols(0)], y_sum[0][:, chunk_cols(0)], unit8[:, chunk_cols(0)], ALU.mult)
        nc.gpsimd.tensor_tensor(unit_mean0[:, chunk_cols(1)], y_sum[1][:, chunk_cols(1)], unit8[:, chunk_cols(1)], ALU.mult)
        nc.gpsimd.tensor_tensor(q_diff[0][:], spread_q0[:], mean_q[0][:], ALU.subtract)
        times_gain(0, GROUPS)
        nc.gpsimd.tensor_tensor(bias[0][:], q_diff[0][:], unit_mean0[:], ALU.mult)
        nc.vector.tensor_tensor(q_diff[1][:], spread_q1_turned[:], mean_q1_turned, ALU.subtract)
        times_gain(1, OWN_GROUPS)
        plus_bias(nc.gpsimd, 0, GROUPS)
        plus_bias(nc.gpsimd, 1, OWN_GROUPS)
        for v in range(OWN_GROUPS, GROUPS):
            for t in range(SLOTS):
                col = CHUNK_COLS + SLOTS * v + t
                nc.scalar.activation(z_bf[1][:, v, :, t], y_bank[1][:, P * t + D * v : P * t + D * (v + 1)], ACT.Identity,
                                     bias=bias[0][:, col : col + 1], scale=gain[0][:, col : col + 1])
        nc.vector.tensor_tensor(unit_diff1[:], unit8_turned, q_diff[1][:], ALU.mult)
        make_gain(1, spread_q1)
        nc.vector.tensor_tensor(bias1_turned[:], y_sum1_turned, unit_diff1[:], ALU.mult)
        turned_sum(bias1, [bias1_turned[:]])
        times_gain(2, GROUPS)
        times_gain(3, GROUPS)
        plus_bias(nc.vector, 2, GROUPS)

        def second_product(name, codes, z, cols, acc, queue, res):
            width = cols.stop - cols.start
            scales = tile(name + "_sc", [P, width], U8)
            part = width // len(z)
            for n, piece in enumerate(z):
                nc.vector.quantize_mx(out=codes[:, part * n : part * (n + 1)].bitcast(FP8X4), scales=scales[:, part * n : part * (n + 1)],
                                      in_=piece.rearrange("p v d t -> p (v d t)"))
            nc.tensor.matmul_mx(out=acc, lhsT=w2_codes[:].bitcast(FP8X4), lhsT_scale=w2_sc[:],
                                rhs=codes[:].bitcast(FP8X4), rhs_scale=scales[:], start=True, stop=True)
            nc.scalar.copy(res[:], acc)
            queue.dma_start(out[:, cols], res[:])

        plus_bias(nc.vector, 3, GROUPS)
        second_product("third", tile("third_codes", [P, P], U32), [z_bf[2]],
                       slice(2 * P, 3 * P), region(h_bank[2], 3), nc.sync, shared("res2", [P, P], F32, 10240))
        second_product("first", shared("first_codes", [P, P], U32, 12288), [z_bf[0]],
                       slice(0, P), region(h_bank[3], 1), nc.sync, tile("res0", [P, P]))
        second_product("second", shared("second_codes", [P, P], U32, 12288 + 512), [z_bf[1]],
                       slice(P, 2 * P), region(h_bank[0], 3), nc.sync, tile("res1", [P, P]))
        second_product("fourth", tile("fourth_codes", [P, P], U32), [z_bf[3]],
                       slice(3 * P, 4 * P), region(y_bank[0], 0), nc.scalar, tile("res3", [P, P]))
